import numpy as np, ml_dtypes
CORES = [48,51,52,55]
N = 4
BF = ml_dtypes.bfloat16
V, L, A, T = 4096, 256, 2048, 4
H = L // 2; B = V - T * H
def draw0(rng):
    ax = np.clip(np.floor(rng.random((N, 8, 1, V)) * 300 - 22 + 140 * (rng.random((N, 8, 16, V)) - 0.5)), 0, 255).astype(np.int64)
    zp = np.clip(np.floor(rng.random((N, 8, 1, A)) * 170 + 40 + 160 * (rng.random((N, 8, 16, A)) - 0.5)), 0, 255).astype(np.int64)
    p = np.clip(np.floor(rng.random((N, 8, 1, L)) * 130 + 60 + 160 * (rng.random((N, 8, 16, L)) - 0.5)), 0, 255).astype(np.int64)
    near = (rng.random((N, 8, 1, H)) < 0.6) & (rng.random((N, 8, 16, H)) > 0.15)
    p[..., 1::2] = np.where(near, p[..., ::2], p[..., 1::2])
    rt = rng.integers(0, V, (N, 8, 16, A)); ex = rng.integers(0, V, (N, 8, 16, L))
    ex[..., 1::2] = np.where(rng.random((N, 8, 16, H)) < 0.2, ex[:, :, ::-1, ::2], ex[..., 1::2])
    return ax, rt, zp, ex, p, rng.integers(0, 4096, (N, 8, 16)), rng.integers(0, 4096, (N, 8, 16))
def pack(ax, rt, zp, ex, p, wt, km):
    b = lambda a: np.ascontiguousarray(a.reshape(N, 128, -1)).astype(np.float32).astype(BF)
    w = lambda a: np.ascontiguousarray(a.reshape(N, 128, -1)).astype(np.int32)
    return {"ax": b(ax), "rt": w(rt), "zp": b(zp), "ex": w(ex), "p0": b(p), "wt": w(wt), "km": w(km)}
def setup_inputs(rng):
    return pack(*draw0(rng))
def setup_inputs_spread(rng):
    def uneven(n): return np.minimum(np.floor(np.exp2(1 + 7.3 * rng.random((N, 8, 1, n))) * rng.random((N, 8, 16, n))), 255).astype(np.int64)
    ax, zp, p = uneven(V), uneven(A), uneven(L)
    p[..., 1::2] = np.where(rng.random((N, 8, 1, H)) < 0.4, p[..., ::2], p[..., 1::2])
    rt = np.minimum(np.floor(V * rng.random((N, 8, 16, A)) ** (0.5 + 3 * rng.random((N, 8, 1, A)))), V - 1).astype(np.int64)
    ex = np.minimum(np.floor(V * rng.random((N, 8, 16, L)) ** (0.5 + 3 * rng.random((N, 8, 1, L)))), V - 1).astype(np.int64)
    wt = np.minimum(np.floor(np.exp2(12.1 * rng.random((N, 8, 16)))) - 1, 4095).astype(np.int64)
    km = np.minimum(np.floor(np.exp2(12.1 * rng.random((N, 8, 16)))) - 1, 4095).astype(np.int64)
    return pack(ax, rt, zp, ex, p, wt, km)
def setup_inputs_ends(rng):
    den = np.array([0.0, 0.1, 0.25, 0.5, 0.75, 1.0])
    ax = 255 * (rng.random((N, 8, 16, V)) < rng.choice(den, (N, 8, 1, V))); zp = 255 * (rng.random((N, 8, 16, A)) < rng.choice(den, (N, 8, 1, A)))
    p = 255 * (rng.random((N, 8, 16, L)) < rng.choice(np.array([0.0, 0.25, 0.5, 0.75, 0.9, 1.0]), (N, 8, 1, L)))
    p[..., 1::2] = np.where(rng.random((N, 8, 1, H)) < 0.5, p[..., ::2], p[..., 1::2])
    for g, (a, b) in enumerate(((0.0, 0.4), (0.2, 1.0), (0.3, 0.7), (0.4, 0.0), (0.5, 0.3), (0.7, 0.2), (1.0, 0.3), (0.3, 0.5))):
        ax[:, g, :, 0] = 255 * (rng.random((N, 16)) < a); ax[:, g, :, V - 1] = 255 * (rng.random((N, 16)) < b)
    def names(n): return np.where(rng.random((N, 8, 16, n)) < 0.85, (V - 1) * rng.integers(0, 2, (N, 8, 16, n)), rng.integers(0, V, (N, 8, 16, n)))
    rt, ex = names(A), names(L)
    wt = 4095 * rng.integers(0, 2, (N, 8, 16)); km = 4095 * rng.integers(0, 2, (N, 8, 16))
    wt[:, 7] = 4095; wt[:, 5:7, 15] = 4095; wt[:, 0, 0] = 0; wt[:, 0, 1] = 4095
    for m, k in ((0, 0), (1, 4095), (3, 8), (9, 3856), (15, 3841)): km[:, 5:, m] = k
    one = np.zeros(16, np.int64); one[15] = 1
    for i in (0, 1, L - 2, L - 1): p[:, 5:, :, i] = one
    for i in (2, 3, L - 4, L - 3): p[:, 7, :, i] = 255; p[:, 6, :, i] = 0
    p[N - 1, 7, :, L - 2:] = 255
    for h in (3840, 3841, 4095, 4080, 3832): zp[:, 5:, :, (h * A) >> 12] = 255
    zp[:, 6, :, (4080 * A) >> 12] = 0; zp[:, 6, :, (4095 * A) >> 12] = 0; zp[:, 5, :, (4095 * A) >> 12] = 0
    for h in (8, 4088, 24, 264, 136): zp[:, 7, :, (h * A) >> 12] = 0
    zp[:, 6, :, 0] = 255
    return pack(ax, rt, zp, ex, p, wt, km)
def setup_inputs_corners(rng):
    ax, rt, zp, ex, p, wt, km = draw0(rng)
    cnt = rng.integers(0, 17, (N, 8, 1, V)); cnt[..., :17] = np.arange(17)
    hi = ((np.arange(16)[:, None] + rng.integers(0, 16, (N, 8, 1, V))) & 15) < cnt
    ax = np.where(hi, rng.integers(139, 256, ax.shape), rng.integers(0, 111, ax.shape))
    p = rng.integers(111, 140, p.shape); p[..., 1::2] = np.where(rng.random((N, 8, 1, H)) < 0.5, p[..., ::2], p[..., 1::2])
    sets = ((0, 1, 2, 3), (9, 10, 12, 16), (3, 4), (4, 5, 6, 7, 8), (8, 9), tuple(range(17)), (8,), ())
    full = int(rng.integers(0, N))
    for q in range(N):
        for g in range(8):
            s = 0 if q == full else (q + g) & 7
            cand = np.flatnonzero(np.isin(cnt[q, g, 0], np.array(sets[s], np.int64))) if s < 7 else np.array([0, B - 1, B, B + H - 1, B + H, V - 2, V - 1])
            if s == 6: cand = cand[:1]
            rt[q, g] = cand[rng.integers(0, len(cand), (16, A))]
    nm = (rng.integers(0, V, (N, 8, 1, H)) + (2 * rng.integers(0, V // 2, (N, 8, 1, H)) + 1) * np.arange(32)[:, None]) & (V - 1)
    ea, eb = nm[:, :, :16], nm[:, :, 16:]; rep = np.broadcast_to(nm[:, :, :1], ea.shape)
    kd = (np.arange(H)[None, None, None, :] + np.arange(8)[None, :, None, None] + np.arange(N)[:, None, None, None]) % 6
    lone = eb.copy(); lone[:, :, 0] = ea[:, :, 15]
    ex[..., ::2] = np.where(kd >= 4, rep, ea)
    ex[..., 1::2] = np.where(kd == 0, ea, np.where(kd == 1, ea[:, :, ::-1], np.where(kd == 3, lone, np.where(kd == 4, rep, eb))))
    ch = rng.integers(0, 3, (N, 8, 1, A)); ch[:, 1] = 0
    zp = np.take_along_axis(rng.integers(0, 256, (N, 8, 16, 3)), ch, 3)
    km[:, 2] = rng.integers(0, 4096, (N, 1)); km[:, 3, ::2] = 0; km[:, 3, 1::2] = 4095; wt[:, 4] = 0; wt[:, 6, 1:] = 0; wt[:, 6, 0] = 4095
    return pack(ax, rt, zp, ex, p, wt, km)
def setup_inputs_alike(rng):
    ax, rt, zp, ex, p, wt, km = draw0(rng)
    p[:, ::2] = p[:, ::2, :, :1]
    p[:, 1::2] = np.take_along_axis(p[:, 1::2, :, :4], rng.integers(0, 4, (N, 4, 1, L)), 3)
    rt = np.take_along_axis(rt[..., :8], rng.integers(0, 8, (N, 8, 1, A)), 3)
    rt[:, 3] = rng.choice(np.array([0, V - 1, B, B - 1]), (N, 16, A))
    ex[:, ::2] = rng.choice(np.array([0, 5, B - 1, B, B + H, V - 1]), (N, 4, 16, L))
    zp[:, 4:] = np.take_along_axis(zp[:, 4:, :, :16], rng.integers(0, 16, (N, 4, 1, A)), 3)
    wt[:, 5, :14] = rng.integers(3200, 4096, (N, 14)); wt[:, 5, 14] = 256; wt[:, 5, 15] = 1
    aim = np.array([0, 4095, 4075, 4077, 4087])[np.arange(H // 2) % 5]
    big = rng.integers(200, 256, (N, 14, H // 2))
    rest = (4096 + aim - np.sum(wt[:, 5, :14, None] * big, axis=1)) & 8191
    p[:, 5, :14, 2::4] = big; p[:, 5, 14, 2::4] = rest >> 8; p[:, 5, 15, 2::4] = rest & 255; p[:, 5, :, 3::4] = 0
    for k, v in ((5, V - 3), (6, V - 5), (7, V - 7)):
        rt[:, 5, k] = v; ax[:, 5, :, v] = 0; ax[:, 5, :4, v] = 255; ax[:, 5, 14:, v] = 255
    for v, u in ((V - 3, 4075), (V - 5, 4077), (V - 7, 4087), (V - 3, 4095), (V - 3, 4096)): ax[:, 5, :, (((v * u) >> 5) + v) & (V - 1)] = 255
    return pack(ax, rt, zp, ex, p, wt, km)
def check_inputs(d):
    bad = []
    for k, hi in (("ax", 255), ("rt", V - 1), ("zp", 255), ("ex", V - 1), ("p0", 255), ("wt", 4095), ("km", 4095)):
        v = np.asarray(d[k]).astype(np.float64)
        if not (np.min(v) >= 0 and np.max(v) <= hi): bad.append("range of " + k)
        elif np.any(v != np.floor(v)): bad.append("whole numbers of " + k)
    return bad
def pick(x, e):
    n = e.shape[3]
    return np.take_along_axis(x, e.reshape(N, 8, 1, 16 * n), 3).reshape(N, 8, 16, 16, n)
def reference(ax, rt, zp, ex, p0, wt, km):
    x = ax.astype(np.float32).astype(np.int64).reshape(N, 8, 16, V)
    r = np.zeros((N, 8, 16, A + T * L), np.int64); z = np.zeros((N, 8, 16, A + T * L), np.int64)
    r[..., :A] = rt.reshape(N, 8, 16, A); z[..., :A] = zp.astype(np.float32).astype(np.int64).reshape(N, 8, 16, A)
    e0 = ex.astype(np.int64).reshape(N, 8, 16, L); p = p0.astype(np.float32).astype(np.int64).reshape(N, 8, 16, L)
    w = wt.astype(np.int64).reshape(N, 8, 16, 1); k = km.astype(np.int64).reshape(N, 8, 16, 1); odd = np.zeros(N, np.int64)
    for t in range(T):
        n = A + L * t
        u = np.repeat(np.add.reduce(w * p, axis=2)[:, :, ::2] & 4095, 2, axis=2)[:, :, None, :]
        c = (((((u * u) >> 5) & 4095) + ((k * u) & 4095)) & 4095) * n >> 12
        score = np.sum(np.abs(pick(z, c) - p[:, :, :, None, :]), axis=2)
        a = np.minimum.reduce(score * 4096 + c, axis=2) & 4095
        e = np.take_along_axis(r, a[:, :, None, :], 3)
        v = np.sum(pick(x, e) >= p[:, :, :, None, :], axis=2)
        barred = v < 4 + odd[:, None, None, None]
        e2 = (((e * u) >> 5) + e + 77 * t) & (V - 1)
        v2 = np.sum(pick(x, e2) >= p[:, :, :, None, :], axis=2)
        f = np.where(barred, e0, np.where((v < 9) & (v2 >= v), e2, e))
        odd = np.sum(barred, axis=(1, 2, 3)) & 1
        fa, fb = f[..., ::2].copy(), f[..., 1::2].copy()
        same = fa[:, :, :, None, :] == fb[:, :, None, :, :]
        ca, cb = np.any(same, axis=3), np.any(same, axis=2)
        rec = np.maximum.reduce(np.where(ca[:, :, None], pick(x, fa), 0), axis=3)
        new = B + H * t + np.arange(H)
        f[..., ::2] = np.where(ca, new, fa); f[..., 1::2] = np.where(cb, new, fb)
        src = (np.arange(N) - 1 - t % 3) % N
        f, p = f[src], p[src]
        r[..., n:n + L] = f
        if t < T - 1: z[..., n:n + L] = p
        x[..., B + H * t:B + H * t + H] = rec[src]
        p = (p + 255 - np.take_along_axis(x, f[:, :, :1], 3)) >> 1
    return {"yr": r[..., A:].reshape(N, 128, T * L).astype(np.float32), "yp": p.reshape(N, 128, L).astype(np.float32)}

@@ -1,0 +1,561 @@
+from concourse.mybir import AluOpType, ActivationFunctionType
+
+ALU = AluOpType
+ACT = ActivationFunctionType
+ROUNDS, H, A0, NV, REC = 4, 128, 2048, 4096, 3584
+CHUNKS = ((0, 64), (64, 64))
+SCALAR_LANES = (128, 64)
+REP = "GGGSSSSSSVVVVVVV"
+REP0 = "SSSSSSSSVVVVVVVV"
+REC_S = (0.75, 0.5)
+Z_S = ((1, 0), (1, 1))
+EQ_S = (1, 0)
+C1STEP = 32
+
+F32, BF, I32, U16, F16 = "float32", "bfloat16", "int32", "uint16", "float16"
+LOGICAL = {}
+
+
+def declare(dtype, **bufs):
+    for n, w in bufs.items():
+        LOGICAL[n] = ("sbuf", [128, w], dtype)
+
+
+declare(BF, X=4112, Z=3072, pin=256, ones=2048, blk=128, gsp=144, gmin=144, gz=144, ghalf=144, g0b=144, idb=128, nidb=128, nid100=128,
+        prmb=512, bcb=2048, wh=128, wl=128, rmask=1024, p=256, prep=4096)
+declare(F32, R=3072, whf=1, wlf=1, kf=1, cnt=1, bar=1, seg=128, ef=256, dd=256, yv=256, junk=128)
+declare(I32, rti=2048, exi=256, wti=1, kmi=1, whi=1, wli=1, cnti=1, par=1, ui=128, u=128, uu=128, ku=128, su=128, hs=128, hh=128, pi=256)
+declare(F16, g0=144, nidh=128, idh=128, prm=512, bc=2048, ch=128, uh=128, k2048=64)
+declare(U16, cq=128)
+for _t in range(ROUNDS):
+    declare(BF, **{"pn%d" % _t: 256, "Q%d" % _t: 128, "QL%d" % _t: 128})
+    declare(F32, **{"F%d" % _t: 256, "nr%d" % _t: 256})
+    declare(U16, **{"LT%d" % _t: 16, "LL%d" % _t: 16})
+for _c, (_j, _p) in enumerate(CHUNKS):
+    _l = 2 * _p
+    for _d, _names in ((BF, (("de", 16 * _p), ("do", 16 * _p), ("zg", 16 * _p), ("ez", 16 * _p), ("c1", 16 * _l), ("c2", 16 * _l), ("xg", 16 * _l),
+                             ("mb", _l), ("r1", _l), ("g1c", _l), ("eq", 16 * _p), ("cm", _l), ("xr", 16 * _p), ("qs", 16 * _p))),
+                       (F32, (("tr", _l), ("sg", _l), ("e", _l), ("em", _l), ("t1", _l), ("base", _l), ("ma", _l), ("rt1", _p))),
+                       (I32, (("mk", _l), ("ai", _l // 16), ("nn", _l), ("e2", _l))),
+                       (F16, (("ah", _l // 16), ("f", _l), ("fh", _l))),
+                       (U16, (("au", _l // 16), ("eu", _l), ("e2u", _l), ("ro", _p)))):
+        declare(_d, **{"%s_%d" % (n, _c): w for n, w in _names})
+OWN = {"X", "Z", "R", "rti", "exi", "pin", "wti", "kmi"} | {"%s%d" % (n, t) for n in ("pn", "F", "Q", "QL", "LT", "LL") for t in range(ROUNDS)}
+SCRATCH, PLACE = {}, {}
+for _n, (_w, _s, _d) in LOGICAL.items():
+    if _n in OWN:
+        SCRATCH[_n], PLACE[_n] = (_w, _s, _d), (_n, 0)
+    else:
+        _k = "pool_" + _d
+        _o = SCRATCH.get(_k, (0, [128, 0]))[1][1]
+        PLACE[_n] = (_k, _o)
+        SCRATCH[_k] = ("sbuf", [128, _o + (_s[1] + 31) // 32 * 32], _d)
+for _b in range(8):
+    LOGICAL["B%d" % _b] = SCRATCH["B%d" % _b] = ("psum", [128, 512], F32)
+    PLACE["B%d" % _b] = ("B%d" % _b, 0)
+LOADS = ("p0", "wt", "km", "zp", "rt", "ax", "ex")
+KINDS = ("p", "F", "L", "Q")
+SEMAPHORES = (["v", "s", "t", "gp", "out"] + ["ld_" + n for n in LOADS]
+              + ["l%s%d" % (k, t) for k in KINDS for t in range(ROUNDS)] + ["a%s%d" % (k, t) for k in KINDS for t in range(ROUNDS)])
+WIDTH = {n: s[1][1] for n, s in LOGICAL.items()}
+PSUM = {n for n, s in LOGICAL.items() if s[0] == "psum"}
+TWO = {n for n, s in LOGICAL.items() if s[2] in (BF, F16, U16)}
+CYC, GATHER = 1.0e-3, 1.55
+
+
+def A(name, lo=0, hi=None, st=1):
+    return (name, lo, WIDTH[name] if hi is None else hi, st)
+
+
+def Ind(win, off):
+    return ("@", win, off)
+
+
+def size(a):
+    return 16 * size(a[2]) if a[0] == "@" else (a[2] - a[1] + a[3] - 1) // a[3]
+
+
+def ap(T, a):
+    if a[0] == "@":
+        return ap(T, a[1]).indirect(ap(T, a[2]))
+    name, o = PLACE[a[0]]
+    if a[3] == 1:
+        return T[name][:, o + a[1]:o + a[2]]
+    return T[name][:, o + a[1]:o + a[2]:a[3]]
+
+
+def flat(aps):
+    out = []
+    for a in aps:
+        if isinstance(a, tuple):
+            out += [a[1], a[2]] if a[0] == "@" else [a]
+    return out
+
+
+def build():
+    ops = []
+
+    def add(q, cost, outs, ins, fn, **kw):
+        op = dict(q=q, cost=cost, outs=flat(outs), ins=flat(ins), fn=fn, **kw)
+        ops.append(op)
+        return op
+
+    def vcost(aps, mode):
+        n = size(aps[0])
+        if any(a[0] == "@" for a in aps):
+            return 0.06 + n * GATHER * CYC
+        per = 1.0
+        if mode == "tt":
+            per = 1.0 if any(a[0] in PSUM for a in aps[1:]) else 2.0
+        elif all(a[0] in TWO for a in aps):
+            per = 0.5
+        return 0.06 + max(64, n * per) * CYC
+
+    def tt(out, a, b, op):
+        add("V", vcost((out, a, b), "tt"), [out], [a, b], lambda c: c["V"].tensor_tensor(ap(c["T"], out), ap(c["T"], a), ap(c["T"], b), op))
+
+    def ts(out, a, s1, op0, s2=None, op1=None):
+        def fn(c):
+            x1 = ap(c["T"], s1) if isinstance(s1, tuple) else s1
+            if op1 is None:
+                return c["V"].tensor_scalar(ap(c["T"], out), ap(c["T"], a), x1, None, op0)
+            return c["V"].tensor_scalar(ap(c["T"], out), ap(c["T"], a), x1, s2, op0, op1)
+        add("V", vcost((out, a), "ts"), [out], [a, s1], fn)
+
+    def cp(out, a):
+        add("V", vcost((out, a), "ts"), [out], [a], lambda c: c["V"].tensor_copy(ap(c["T"], out), ap(c["T"], a)))
+
+    def fill(out, val):
+        add("V", 0.06 + size(out) * CYC, [out], [], lambda c: c["V"].memset(ap(c["T"], out), val))
+
+    def scan(out, d0, d1, op0, op1):
+        add("V", vcost((out, d0, d1), "ts"), [out], [d0, d1],
+            lambda c: c["V"].tensor_tensor_scan(ap(c["T"], out), ap(c["T"], d0), ap(c["T"], d1), 0.0, op0, op1))
+
+    def vtr(out, a):
+        add("V", vcost((out, a), "ts"), [out], [a], lambda c: c["V"].transpose(ap(c["T"], out), ap(c["T"], a)))
+
+    def act(out, a, func=None, bias=0.0, scale=1.0, accum=None):
+        func = ACT.Identity if func is None else func
+        n = size(out)
+
+        def fn(c):
+            x = ap(c["T"], accum) if accum is not None else None
+            b = ap(c["T"], bias) if isinstance(bias, tuple) else bias
+            return c["S"].activation(ap(c["T"], out), ap(c["T"], a), func, bias=b, scale=scale, accum_out=x)
+        add("S", 0.08 + n * CYC * (GATHER if a[0] == "@" else 1.0), [out] + ([accum] if accum is not None else []), [a, bias], fn)
+
+    def mm(items):
+        def fn(c):
+            m = None
+            for o, l, r, s, e in items:
+                m = c["P"].matmul(ap(c["T"], o), ap(c["T"], l), ap(c["T"], r), s, e)
+            return m
+        outs, ins = [], []
+        for o, l, r, s, e in items:
+            for x, d in ((o, outs), (l, ins), (r, ins)):
+                if x not in d:
+                    d.append(x)
+        add("P", sum(max(64, size(i[2])) for i in items) * 0.5e-3 + 0.02, outs, ins, fn)
+
+    def aff(out, a, pattern, cmp, base, cm):
+        add("G", 0.2 + 2 * size(out) * CYC, [out], [a], lambda c: c["g"].affine_select(ap(c["T"], out), ap(c["T"], a), pattern, cmp, 0.0, base, cm), sem="gp")
+
+    def iota(out, pattern, base):
+        add("G", 0.15 + 2 * size(out) * CYC, [out], [], lambda c: c["g"].iota(ap(c["T"], out), pattern, base, 0, allow_small_or_imprecise_dtypes=True), sem="gp")
+
+    def load(out, name):
+        add("Y", 0.15, [out], [], lambda c: c["g"].sync.dma_start(ap(c["T"], out), c["T"][name][:]), sem="ld_" + name, inc=16, lat=2.0 + size(out) / 2000.0)
+
+    def store(name, lo, hi, a):
+        add("Y", 0.15, [], [a], lambda c: c["g"].sync.dma_start(c["T"][name][:, lo:hi], ap(c["T"], a)), sem="out", inc=16, lat=2.0)
+
+    def send(kind, t, dst, src):
+        def fn(c):
+            to = c["T"].cores[(c["rank"] + 1 + t % 3) % len(c["T"].cores)]
+            topo = c["topo"]
+            rid, pid, _ = topo.addr(to)
+            c["g"].remote_dma(ap(c["T"], dst), ap(c["T"], src), c["T"].sem["a%s%d" % (kind, t)], c["T"].sem["l%s%d" % (kind, t)],
+                              pid, rid, topo.mask(c["core"], to))
+        s = add("G", 0.2, [], [src], fn, sem="l%s%d" % (kind, t), inc=16, own=True, lat=2.0)
+        add("R", 0.0, [dst], [], None, sem="a%s%d" % (kind, t), inc=16, after=s, lat=2.2)
+
+    def route(tab, x):
+        return A(tab, 15 - x, 143 - x)
+
+    load(A("pin"), "p0"); load(A("wti"), "wt"); load(A("kmi"), "km")
+    load(A("Z", 0, A0), "zp"); load(A("rti"), "rt"); load(A("X", 0, NV), "ax"); load(A("exi"), "ex")
+    fill(A("ones", 0, 128), 1.0)
+    aff(A("blk"), A("ones", 0, 128), [[-16, 8], [0, 16]], ALU.is_ge, 0, 1)
+    aff(A("blk"), A("blk"), [[16, 8], [0, 16]], ALU.is_ge, 15, -1)
+    for c, (j0, P) in enumerate(CHUNKS):
+        for par in range(2):
+            cp(A("p", 2 * j0 + par * P, 2 * j0 + par * P + P), A("pin", 2 * j0 + par, 2 * j0 + 2 * P, 2))
+    ts(A("whi"), A("wti"), 6, ALU.logical_shift_right)
+    ts(A("wli"), A("wti"), 63, ALU.bitwise_and)
+    ts(A("whf"), A("whi"), 64.0, ALU.mult)
+    cp(A("wlf"), A("wli"))
+    ts(A("wh"), A("blk"), A("whf"), ALU.mult)
+    ts(A("wl"), A("blk"), A("wlf"), ALU.mult)
+    ts(A("kf"), A("kmi"), 4096.0, ALU.subtract)
+    send("p", 0, A("Z", A0, A0 + 256), A("pin"))
+    fill(A("gsp"), 0.0)
+    aff(A("gsp", 15, 143, 16), A("ones", 0, 8), [[-16, 8]], ALU.is_ge, 0, 1)
+    aff(A("gsp", 15, 143, 16), A("gsp", 15, 143, 16), [[16, 8]], ALU.is_ge, 15, -1)
+    act(A("gmin"), A("gsp"), scale=-8192.0)
+    act(A("gz"), A("gsp"), scale=4096.0)
+    act(A("ghalf"), A("gsp"), scale=0.5)
+    fill(A("seg"), 0.0)
+    fill(A("seg", 0, 128, 16), 1e9)
+    for qh in range(2):
+        for gp in range(2):
+            k = 128 * (2 * qh + gp)
+            aff(A("prmb", k, k + 128), A("ones", 0, 128), [[-32, 4], [-1000, 2], [-1, 16]], ALU.is_equal, 1000 * gp - 16 * qh, 1)
+    cp(A("prm"), A("prmb"))
+    aff(A("idb"), A("ones", 0, 128), [[-1, 128]], ALU.is_equal, 0, 1)
+    act(A("nidb"), A("idb"), scale=-1.0)
+    act(A("nid100"), A("idb"), scale=-100.0)
+    ts(A("nidh"), A("idb"), -1.0, ALU.mult)
+    cp(A("idh"), A("idb"))
+    ts(A("k2048"), A("ones", 0, 64), 2048.0, ALU.mult)
+    fill(A("bar"), 3.5)
+    fill(A("ones", 128, 2048), 1.0)
+    aff(A("bcb"), A("ones"), [[-1, 16], [-16, 8], [0, 16]], ALU.is_equal, 0, 1)
+    fill(A("X", NV, NV + 16), 0.0)
+    fill(A("rmask"), 1.0)
+    fill(A("rmask", 0, 1024, 16), 0.0)
+    fill(A("g0b"), 0.0)
+    aff(A("g0b", 15, 143, 16), A("ones", 0, 8), [[-16, 8]], ALU.is_equal, 0, 1)
+    for k in range(0, 2048, 512):
+        cp(A("bc", k, k + 512), A("bcb", k, k + 512))
+    cp(A("g0"), A("g0b"))
+    for t in range(ROUNDS):
+        for c, (j0, P) in enumerate(CHUNKS):
+            iota(A("nr%d" % t, 2 * j0, 2 * j0 + 2 * P), [[0, 2], [1, P]], REC - 2048 + H * t + j0)
+    for k in range(0, A0, 512):
+        cp(A("R", k, k + 512), A("rti", k, k + 512))
+    for c, (j0, P) in enumerate(CHUNKS):
+        for par in range(2):
+            cp(A("ef", 2 * j0 + par * P, 2 * j0 + par * P + P), A("exi", 2 * j0 + par, 2 * j0 + 2 * P, 2))
+
+    for t in range(ROUNDS):
+        n = A0 + 256 * t
+        NC = len(CHUNKS)
+        if t > 0:
+            for c, (j0, P) in enumerate(CHUNKS):
+                for par in range(2):
+                    aff(A("pn%d" % t, 2 * j0 + par, 2 * j0 + 2 * P, 2), A("p", 2 * j0 + par * P, 2 * j0 + par * P + P), [[0, P]], ALU.is_ge, 0, 0)
+            send("p", t, A("Z", n, n + 256), A("pn%d" % t))
+        for c, (j0, P) in enumerate(CHUNKS):
+            mm([(A("B0", j0, j0 + P), A("wh"), A("p", 2 * j0, 2 * j0 + P), True, False),
+                (A("B0", j0, j0 + P), A("wl"), A("p", 2 * j0, 2 * j0 + P), False, True)])
+        cp(A("ui"), A("B0", 0, 128))
+        ts(A("u"), A("ui"), 4095, ALU.bitwise_and)
+        tt(A("uu"), A("u"), A("u"), ALU.mult)
+        ts(A("ku"), A("u"), A("kf"), ALU.mult)
+        ts(A("su"), A("uu"), 5, ALU.logical_shift_right)
+        tt(A("hs"), A("su"), A("ku"), ALU.add)
+        ts(A("hh"), A("hs"), 4095, ALU.bitwise_and)
+        ts(A("cq"), A("hh"), (8 + t) / 16.0, ALU.mult, -15.0 / 32, ALU.add)
+        for k in range(16):
+            rep = (REP if t else REP0)[k]
+            if rep == "S":
+                act(A("prep", k, 4096, 16), A("p"))
+            elif rep == "G":
+                aff(A("prep", k, 4096, 16), A("p"), [[0, 256]], ALU.is_ge, 0, 0)
+            else:
+                cp(A("prep", k, 4096, 16), A("p"))
+        ts(A("ch"), A("cq"), 2048.0, ALU.subtract)
+        ts(A("uh"), A("u"), 2048.0, ALU.subtract)
+        for c, (j0, P) in enumerate(CHUNKS):
+            for par, d in ((0, "de_%d" % c), (1, "do_%d" % c)):
+                b = 16 * (2 * j0 + par * P)
+                if (c, par) not in Z_S:
+                    tt(A(d), Ind(A("Z", 0, n), A("cq", j0, j0 + P)), A("prep", b, b + 16 * P), ALU.min)
+            act(A("zg_%d" % c), Ind(A("Z", 0, n), A("cq", j0, j0 + P)))
+        for c, par in Z_S:
+            j0, P = CHUNKS[c]
+            b = 16 * (2 * j0 + par * P)
+            for i, k in enumerate(range(0, 16 * P, 512)):
+                sb = ("B7", "B%d" % (1 + c % 2))[i % 2]
+                mm([(A(sb), A("idb"), A("zg_%d" % c, k, k + 512), True, False), (A(sb), A("nidb"), A("prep", b + k, b + k + 512), False, True)])
+                act(A("%s_%d" % (("de", "do")[par], c), k, k + 512), A(sb), ACT.Abs)
+        for c, (j0, P) in enumerate(CHUNKS):
+            L, bk, tb, cs = 2 * P, "B%d" % (1 + c % 2), "B%d" % (3 + c % 2), "_%d" % c
+            for par, d in ((0, "de"), (1, "do")):
+                o = A(bk, par * P, par * P + P)
+                mm([(o, A("idh"), A("k2048", 0, P), True, False), (o, A("idh"), A("ch", j0, j0 + P), False, False)]
+                   + [(o, route("gz", m), A("zg" + cs, m, 16 * P, 16), False, False) for m in range(16) if (c, par) not in Z_S])
+                mm([(o, route("gz" if (c, par) in Z_S else "gmin", m), A(d + cs, m, 16 * P, 16), False, m == 15) for m in range(16)])
+            vtr(A("tr" + cs), A(bk, 0, L))
+            scan(A("mk" + cs), A("seg", 0, L), A("tr" + cs), ALU.add, ALU.min)
+            ts(A("ai" + cs), A("mk" + cs, 15, L, 16), 4095, ALU.bitwise_and)
+            ts(A("ah" + cs), A("ai" + cs), 2048.0, ALU.subtract)
+            q0 = 128 + 2 * j0 // 16
+            items = []
+            for qh in range(2):
+                for gp in range(2):
+                    k = 128 * (2 * qh + gp)
+                    items.append((A("B0", q0 + qh, q0 + L // 16, 2), A("prm", k, k + 128), A("ah" + cs, gp, L // 16, 2), gp == 0, gp == 1))
+            mm(items)
+            ts(A("au" + cs), A("B0", q0, q0 + L // 16), 2048.0, ALU.add)
+            cp(A("eu" + cs), Ind(A("R", 0, n), A("au" + cs)))
+            act(A("e" + cs), Ind(A("R", 0, n), A("au" + cs)))
+            mm([(A(tb, par * P, par * P + P), A("idh"), A("uh", j0, j0 + P), True, True) for par in range(2)])
+            act(A(tb, 128, 128 + L), A("e" + cs), bias=2464.0 * t - 131072.0, scale=2080.0)
+            act(A(tb, 256, 256 + L), A("e" + cs))
+            tt(A("t1" + cs), A("e" + cs), A(tb, 0, L), ALU.mult)
+            tt(A("nn" + cs), A("t1" + cs), A(tb, 128, 128 + L), ALU.add)
+            ts(A("e2" + cs), A("nn" + cs), 5, ALU.arith_shift_right, 4095, ALU.bitwise_and)
+            cp(A("e2u" + cs), A("e2" + cs))
+        for c, (j0, P) in enumerate(CHUNKS):
+            L, bk, tb, cs = 2 * P, "B%d" % (1 + c % 2), "B%d" % (3 + c % 2), "_%d" % c
+            b = 32 * j0
+            for l0 in range(0, L, C1STEP):
+                tt(A("c1" + cs, 16 * l0, 16 * (l0 + C1STEP)), Ind(A("X", 0, NV), A("eu" + cs, l0, l0 + C1STEP)),
+                   A("prep", b + 16 * l0, b + 16 * (l0 + C1STEP)), ALU.is_ge)
+            act(A("em" + cs), A("e" + cs), bias=-2048.0)
+            tt(A(tb, 384, 384 + L), A("ef", 2 * j0, 2 * j0 + L), A(tb, 256, 256 + L), ALU.subtract)
+            tt(A(tb, 0, L), A("e2" + cs), A(tb, 256, 256 + L), ALU.subtract)
+            ns = SCALAR_LANES[c]
+            for i, l0 in enumerate(range(0, ns, 32)):
+                sb = ("B7", "B6" if c == 0 else "B0")[i % 2]
+                x = A("xg" + cs, 16 * l0, 16 * (l0 + 32))
+                act(x, Ind(A("X", 0, NV), A("e2u" + cs, l0, l0 + 32)))
+                mm([(A(sb), A("idb"), x, True, False),
+                    (A(sb), A("nidb"), A("prep", b + 16 * l0, b + 16 * (l0 + 32)), False, True)])
+                act(A("c2" + cs, 16 * l0, 16 * (l0 + 32)), A(sb), ACT.Sign, bias=0.5)
+            for l0 in range(ns, L, 64):
+                hi = min(l0 + 64, L)
+                tt(A("c2" + cs, 16 * l0, 16 * hi), Ind(A("X", 0, NV), A("e2u" + cs, l0, hi)), A("prep", b + 16 * l0, b + 16 * hi), ALU.is_ge)
+        for c, (j0, P) in enumerate(CHUNKS):
+            L, bk, tb, cs = 2 * P, "B%d" % (1 + c % 2), "B%d" % (3 + c % 2), "_%d" % c
+            ns = SCALAR_LANES[c]
+            for h in range(2):
+                mm([(A(bk, 128 + h * P, 128 + h * P + P), route("gsp", k), A("c1" + cs, 16 * P * h + k, 16 * P * h + 16 * P, 16), k == 0, k == 15) for k in range(16)])
+            act(A("sg" + cs), A(bk, 128, 128 + L), ACT.Sign, bias=A("bar"), scale=-1.0)
+            act(A("mb" + cs), A("sg" + cs), ACT.Relu)
+            act(A("r1" + cs), A(bk, 128, 128 + L), ACT.Relu, bias=-800.0, scale=100.0)
+            if ns > 0:
+                act(A("g1c" + cs, 0, ns), A(bk, 128, 128 + ns), bias=-8.0)
+            if ns < L:
+                act(A("g1c" + cs, ns, L), A(bk, 128 + ns, 128 + L))
+            tt(A(tb, 128, 128 + L), A("mb" + cs), A(tb, 384, 384 + L), ALU.mult)
+            tt(A("base" + cs), A(tb, 128, 128 + L), A("em" + cs), ALU.add)
+            for lo, hi, tab in [(l0, min(l0 + 64, L), "gsp") for l0 in range(ns, L, 64)] + [(0, ns, "ghalf")] * (ns > 0):
+                o = A(bk, 256 + lo, 256 + hi)
+                mm([(o, route(tab, k), A("c2" + cs, 16 * lo + k, 16 * hi, 16), k == 0, False) for k in range(16)])
+                mm([(o, A("nid100"), A("mb" + cs, lo, hi), False, False), (o, A("nidb"), A("r1" + cs, lo, hi), False, False),
+                    (o, A("nidb"), A("g1c" + cs, lo, hi), False, True)])
+            ts(A("ma" + cs), A(bk, 256, 256 + L), 0.0, ALU.is_ge)
+            tt(A(tb, 256, 256 + L), A("ma" + cs), A(tb, 0, L), ALU.mult)
+            tt(A("f" + cs), A(tb, 256, 256 + L), A("base" + cs), ALU.add)
+            tt(A(tb, 0, L), A("nr%d" % t, 2 * j0, 2 * j0 + L), A("f" + cs), ALU.subtract)
+            for h in range(2):
+                eb = "B%d" % (5 + h)
+                items = []
+                for k in range(8):
+                    o = A(eb, k * P, k * P + P)
+                    items.append((o, A("nidh"), A("f" + cs, 0, P), True, False))
+                    items.append((o, A("bc", 128 * (8 * h + k), 128 * (8 * h + k) + 128), A("f" + cs, P, L), False, True))
+                mm(items)
+                x = A("eq" + cs, 8 * P * h, 8 * P * h + 8 * P)
+                if EQ_S[c]:
+                    y = A("ez" + cs, 8 * P * h, 8 * P * h + 8 * P)
+                    act(y, A(eb, 0, 8 * P), ACT.Abs)
+                    act(x, y, ACT.Relu, bias=1.0, scale=-1.0)
+                else:
+                    ts(x, A(eb, 0, 8 * P), 0.0, ALU.is_equal)
+            for h in range(2):
+                for par in range(2):
+                    mm([(A(("B7" if par else bk), 384, 384 + P), route("gsp", k) if par else A("idb"), A("eq" + cs, k * P, k * P + P), k == 0, k == 15)
+                        for k in range(8 * h, 8 * h + 8)])
+            act(A(tb, 384, 384 + P), A(bk, 384, 384 + P), bias=2048.0, scale=-8192.0)
+            act(A("cm" + cs, P, L), A("B7", 384, 384 + P), ACT.Sign)
+            act(A("cm" + cs, 0, P), A(bk, 384, 384 + P), ACT.Sign)
+            tt(A("rt1" + cs), A(tb, 384, 384 + P), A("f" + cs, 0, P), ALU.max)
+            ts(A("ro" + cs), A("rt1" + cs), 2048.0, ALU.add)
+            ps = int(P * REC_S[c]) // 16 * 16
+            if ps:
+                act(A("xr" + cs, 0, 16 * ps), Ind(A("X"), A("ro" + cs, 0, ps)))
+            if ps < P:
+                cp(A("xr" + cs, 16 * ps, 16 * P), Ind(A("X"), A("ro" + cs, ps, P)))
+            tt(A(tb, 128, 128 + L), A("cm" + cs), A(tb, 0, L), ALU.mult)
+            tt(A("fh" + cs), A(tb, 128, 128 + L), A("f" + cs), ALU.add)
+            for par in range(2):
+                mm([(A("B0", 256 + 2 * j0 + par, 256 + 2 * j0 + L, 2), A("nidh"), A("fh" + cs, par * P, par * P + P), True, True)])
+            act(A("F%d" % t, 2 * j0, 2 * j0 + L), A("B0", 256 + 2 * j0, 256 + 2 * j0 + L), bias=2048.0, scale=-1.0)
+            q0 = 160 + 2 * j0 // 16
+            mm([(A("B0", q0, q0 + L // 16), route("g0", x), A("fh" + cs, x, L, 16), x == 0, x == 15) for x in range(16)])
+            ts(A("LT%d" % t, 2 * j0 // 16, 2 * j0 // 16 + L // 16), A("B0", q0, q0 + L // 16), 2048.0, ALU.add)
+            scan(A("qs" + cs), A("rmask", 0, 16 * P), A("xr" + cs), ALU.mult, ALU.max)
+            cp(A("Q%d" % t, j0, j0 + P), A("qs" + cs, 15, 16 * P, 16))
+        send("F", t, A("R", n, n + 256), A("F%d" % t))
+        send("L", t, A("LL%d" % t), A("LT%d" % t))
+        send("Q", t, A("QL%d" % t), A("Q%d" % t))
+        if t < ROUNDS - 1:
+            mm([(A("B7", 0, 2 * P), A("ones", 0, 128), A("mb_%d" % c), c == 0, c == NC - 1) for c, (j0, P) in enumerate(CHUNKS)])
+            P0 = CHUNKS[0][1]
+            act(A("junk", 0, 2 * P0), A("B7", 0, 2 * P0), accum=A("cnt"))
+            cp(A("cnti"), A("cnt"))
+            ts(A("par"), A("cnti"), 1, ALU.bitwise_and)
+            ts(A("bar"), A("par"), 3.5, ALU.add)
+        store("yr", 256 * t, 256 * t + 256, A("R", n, n + 256))
+        cp(A("X", REC + H * t, REC + H * t + H), A("QL%d" % t))
+        for par in range(2):
+            for c, (j0, P) in enumerate(CHUNKS):
+                lo, hi = 2 * j0 + par * P, 2 * j0 + par * P + P
+                tt(A("dd", lo, hi), Ind(A("X", 0, NV), A("LL%d" % t, lo // 16, hi // 16)), A("Z", n + 2 * j0 + par, n + 2 * j0 + 2 * P, 2), ALU.subtract)
+                ts(A("pi", lo, hi), A("dd", lo, hi), -0.5, ALU.mult, 127.25, ALU.add)
+                if t < ROUNDS - 1:
+                    cp(A("p", lo, hi), A("pi", lo, hi))
+                else:
+                    cp(A("yv", 2 * j0 + par, 2 * j0 + 2 * P, 2), A("pi", lo, hi))
+    store("yp", 0, 256, A("yv"))
+    return ops
+
+
+def overlap(a, b):
+    if a[1] >= b[2] or b[1] >= a[2]:
+        return False
+    return not (a[3] == b[3] and a[3] > 1 and (a[1] - b[1]) % a[3])
+
+
+def dependencies(ops):
+    hist = {}
+    for i, op in enumerate(ops):
+        op["i"] = i
+        deps = {}
+        acc = [(a, False) for a in op["ins"]] + [(a, True) for a in op["outs"]]
+        for a, wr in acc:
+            for j, b, bw in hist.setdefault(a[0], []):
+                same = ops[j]["q"] == op["q"]
+                if (wr or bw) and overlap(a, b):
+                    deps[j] = deps.get(j, False) or not same or op["q"] != "P"
+                elif same and a[0] in PSUM and op["q"] == "P":
+                    deps[j] = deps.get(j, False)
+        for a, wr in acc:
+            h = hist[a[0]]
+            if a[0] in PSUM:
+                h[:] = [e for e in h if e[0] >= i - 400]
+            elif wr and a[3] == 1:
+                h[:] = [e for e in h if not (e[0] != i and e[1][1] >= a[1] and e[1][2] <= a[2])]
+            h.append((i, a, wr))
+        op["deps"] = deps
+        op["banks"] = {a[0] for a, _ in acc if a[0] in PSUM}
+
+
+LOOK, BIG = 0.2, 0.45
+
+
+def schedule(ops, wake=0.25):
+    n = len(ops)
+    succ = [[] for _ in range(n)]
+    npred = [0] * n
+    for i, op in enumerate(ops):
+        op["preds"] = set(op["deps"]) | ({op["after"]["i"]} if "after" in op else set())
+        npred[i] = len(op["preds"])
+        for j in op["preds"]:
+            succ[j].append(i)
+    prio = [0.0] * n
+    for i in range(n - 1, -1, -1):
+        b = max([prio[k] + (0.0 if ops[k]["q"] == ops[i]["q"] else wake) for k in succ[i]] + [0.0])
+        prio[i] = b + ops[i]["cost"] + ops[i].get("lat", 0.0)
+    free, count, done, last = {}, {}, [0.0] * n, {}
+    ready = {i for i in range(n) if npred[i] == 0}
+    while ready:
+        best = {}
+        for i in sorted(ready):
+            q = ops[i]["q"]
+            s = free.get(q, 0.0) if q != "R" else 0.0
+            for j in ops[i]["preds"]:
+                s = max(s, done[j] + (wake if ops[j]["q"] != q else 0.02))
+            for b in ops[i]["banks"]:
+                for q2, j in last.get(b, {}).items():
+                    if q2 != q:
+                        s = max(s, done[j] + wake)
+            best.setdefault(q, []).append((s, i))
+        pick = None
+        for q, lst in sorted(best.items()):
+            m = min(s for s, _ in lst)
+            s, i = max(((s, i) for s, i in lst if s <= m), key=lambda e: (prio[e[1]], -e[1]))
+            if ops[i]["cost"] > BIG:
+                s, i = max(((s, i) for s, i in lst if s <= m + LOOK), key=lambda e: (prio[e[1]], -e[1]))
+            if pick is None or (s, -prio[i]) < pick[:2]:
+                pick = (s, -prio[i], i, q)
+        s, _, i, q = pick
+        ready.remove(i)
+        for b in ops[i]["banks"]:
+            users = last.setdefault(b, {})
+            for q2, j in users.items():
+                if q2 != q:
+                    ops[i]["deps"][j] = True
+            users[q] = i
+        free[q] = s + ops[i]["cost"]
+        done[i] = s + ops[i]["cost"] + ops[i].get("lat", 0.0)
+        count[q] = count.get(q, 0) + 1
+        ops[i]["pos"] = (s, count[q])
+        for k in succ[i]:
+            npred[k] -= 1
+            if npred[k] == 0:
+                ready.add(k)
+
+
+PLAN = {}
+
+
+def plan():
+    if not PLAN:
+        ops = build()
+        dependencies(ops)
+        schedule(ops)
+        PLAN["ops"], PLAN["seq"] = ops, sorted(range(len(ops)), key=lambda i: ops[i]["pos"])
+    return PLAN["ops"], PLAN["seq"]
+
+
+def rank_program(g, core, T, topo):
+    rank = T.rank_of(core)
+    if rank is None:
+        return
+    ops, seq = plan()
+    ctx = dict(g=g, V=g.vector, S=g.scalar, P=g.tensor, T=T, topo=topo, core=core, rank=rank)
+    queue = {"V": g.vector, "S": g.scalar, "P": g.tensor, "G": g, "Y": g.sync}
+    default = {"V": "v", "S": "s", "P": "t"}
+    total, val, known, clock = {}, {}, {q: {} for q in queue}, {}
+    for i in seq:
+        op = ops[i]
+        q = op["q"]
+        name = op.get("sem") or default[q]
+        inc = op.get("inc", 1)
+        if q == "R":
+            total[name] = total.get(name, 0) + inc
+            val[i], clock[i] = (name, total[name]), {name: total[name]}
+            continue
+        kn = known[q]
+        hard = [j for j, h in op["deps"].items() if h]
+        need = {}
+        for j in hard:
+            s, v = val[j]
+            if kn.get(s, 0) < v:
+                need[s] = max(need.get(s, 0), v)
+        for j in sorted(hard, key=lambda j: -ops[j]["pos"][0]):
+            s0, v0 = val[j]
+            if need.get(s0) == v0:
+                for s, v in clock[j].items():
+                    if s != s0 and need.get(s, v + 1) <= v:
+                        del need[s]
+        for s in sorted(need):
+            queue[q].wait_ge(T.sem[s], need[s])
+        for j in hard:
+            for s, v in clock[j].items():
+                kn[s] = max(kn.get(s, 0), v)
+        ins = op["fn"](ctx)
+        total[name] = total.get(name, 0) + inc
+        val[i] = (name, total[name])
+        clock[i] = dict(kn)
+        clock[i][name] = total[name]
+        if not op.get("own"):
+            ins.then_inc(T.sem[name], inc)
+    for s in sorted(total):
+        if known["G"].get(s, 0) < total[s]:
+            g.wait_ge(T.sem[s], total[s])

@@ -1,17 +1,18 @@
+import math
 from concourse.mybir import AluOpType, ActivationFunctionType
 
 ALU = AluOpType
 ACT = ActivationFunctionType
-ROUNDS, H, A0, NV, REC = 4, 128, 2048, 4096, 3584
-CHUNKS = ((0, 64), (64, 64))
-SCALAR_LANES = (128, 64)
-REP = "GGGSSSSSSVVVVVVV"
-REP0 = "SSSSSSSSVVVVVVVV"
-REC_S = (0.75, 0.5)
-Z_S = ((1, 0), (1, 1))
-EQ_S = (1, 0)
-C1STEP = 32
-
+ROUNDS, RANKS, H, A0, NV, REC = 4, 4, 128, 2048, 4096, 3584
+L, P = 128, 64
+CFG = dict(z=(1, 3), nv1=(64, 64), nv2=(128, 64), step=32, sstep=32, rec_s=(64, 32), rstep=32, eq=("SS", "VV"), e_v=(0, 0), delta=1,
+           ro1=(0, 0), ddw=(0, 1), lin_g=0, csplit=(0, 0), uu2=0,
+           lead=2.0, wake=0.2, same=0.08, bw=250e3, rbw=150e3, passes=6, al=0.5, boost={"ek0": 30.0, "w0": 30.0, "Z0": 30.0, "R0": 3.0}, rounds=15000, width=0.1)
+B = 32768.0
+AT = [0]
+for _t in range(ROUNDS):
+    AT.append((AT[-1] + 1 + _t % 3) % RANKS)
+SLOT = [AT.index(x) for x in AT]
 F32, BF, I32, U16, F16 = "float32", "bfloat16", "int32", "uint16", "float16"
 LOGICAL = {}
 
@@ -21,26 +22,23 @@ def declare(dtype, **bufs):
         LOGICAL[n] = ("sbuf", [128, w], dtype)
 
 
-declare(BF, X=4112, Z=3072, pin=256, ones=2048, blk=128, gsp=144, gmin=144, gz=144, ghalf=144, g0b=144, idb=128, nidb=128, nid100=128,
-        prmb=512, bcb=2048, wh=128, wl=128, rmask=1024, p=256, prep=4096)
-declare(F32, R=3072, whf=1, wlf=1, kf=1, cnt=1, bar=1, seg=128, ef=256, dd=256, yv=256, junk=128)
-declare(I32, rti=2048, exi=256, wti=1, kmi=1, whi=1, wli=1, cnti=1, par=1, ui=128, u=128, uu=128, ku=128, su=128, hs=128, hh=128, pi=256)
-declare(F16, g0=144, nidh=128, idh=128, prm=512, bc=2048, ch=128, uh=128, k2048=64)
-declare(U16, cq=128)
+declare(BF, pin=256, ones=512, blk=128, gsp=144, gz=144, gz2=144, gzn=144, ghalf=144, gb=144, gbh=144, g0=144, idb=128, nidb=128, ih=128, nih=128,
+        ib=128, nib=128, i8=128, ni8=128, prm=512, bc=2048, rmask=1024, k8=128, nrb=128, k2048=128, QL=H, Z4=256)
+declare(F32, seg=128, half=128, cnt=2, whf=1, wlf=1, yv=256, yl=256, R4=256)
+declare(I32, rti=2048, exi=256, wti=1, kmi=1, whi=1, wli=1, cnti=1, par=1)
+OWN = {"rti", "exi", "pin", "wti", "kmi", "yv", "yl", "QL", "R4"}
 for _t in range(ROUNDS):
-    declare(BF, **{"pn%d" % _t: 256, "Q%d" % _t: 128, "QL%d" % _t: 128})
-    declare(F32, **{"F%d" % _t: 256, "nr%d" % _t: 256})
-    declare(U16, **{"LT%d" % _t: 16, "LL%d" % _t: 16})
-for _c, (_j, _p) in enumerate(CHUNKS):
-    _l = 2 * _p
-    for _d, _names in ((BF, (("de", 16 * _p), ("do", 16 * _p), ("zg", 16 * _p), ("ez", 16 * _p), ("c1", 16 * _l), ("c2", 16 * _l), ("xg", 16 * _l),
-                             ("mb", _l), ("r1", _l), ("g1c", _l), ("eq", 16 * _p), ("cm", _l), ("xr", 16 * _p), ("qs", 16 * _p))),
-                       (F32, (("tr", _l), ("sg", _l), ("e", _l), ("em", _l), ("t1", _l), ("base", _l), ("ma", _l), ("rt1", _p))),
-                       (I32, (("mk", _l), ("ai", _l // 16), ("nn", _l), ("e2", _l))),
-                       (F16, (("ah", _l // 16), ("f", _l), ("fh", _l))),
-                       (U16, (("au", _l // 16), ("eu", _l), ("e2u", _l), ("ro", _p)))):
-        declare(_d, **{"%s_%d" % (n, _c): w for n, w in _names})
-OWN = {"X", "Z", "R", "rti", "exi", "pin", "wti", "kmi"} | {"%s%d" % (n, t) for n in ("pn", "F", "Q", "QL", "LT", "LL") for t in range(ROUNDS)}
+    declare(BF, **{"X%d" % _t: NV + 16, "Z%d" % _t: A0 + 256 * _t, "w%d" % _t: 256})
+    declare(F32, **{"R%d" % _t: A0 + 256 * _t, "ek%d" % _t: 264, "bar%d" % _t: 1, "bo%d" % _t: 1, "FL%d" % _t: 256})
+    OWN |= {n + str(_t) for n in ("X", "Z", "w", "R", "ek", "bar", "bo", "FL")}
+for _s in "ab":
+    for _d, _names in ((BF, dict(pz=16 * L, prep=16 * L, zg=16 * P, re=16 * P, ad=16 * L, c1=16 * L, c2=16 * L, x1=16 * L, x2=16 * L,
+                                 dl=P, gq=L, sb=L, eq=16 * P, cm=L, xr=16 * P, qs=16 * P)),
+                       (F32, dict(tr=L, lin=L, d1=4 * L, rt1=P, bs=L, pq=L)),
+                       (I32, dict(ui=P, u=P, uu=P, su=P, hs=P, hh=P, mk=L, ai=8, nn=L, e2=L, sc=4 * L, fi=L)),
+                       (F16, dict(pm=L, ch=P, ah=8, f=L, F=L)),
+                       (U16, dict(cq=P, au=8, eu=L, e2u=L, ro=P, lu=8))):
+        declare(_d, **{n + _s: w for n, w in _names.items()})
 SCRATCH, PLACE = {}, {}
 for _n, (_w, _s, _d) in LOGICAL.items():
     if _n in OWN:
@@ -54,13 +52,13 @@ for _b in range(8):
     LOGICAL["B%d" % _b] = SCRATCH["B%d" % _b] = ("psum", [128, 512], F32)
     PLACE["B%d" % _b] = ("B%d" % _b, 0)
 LOADS = ("p0", "wt", "km", "zp", "rt", "ax", "ex")
-KINDS = ("p", "F", "L", "Q")
-SEMAPHORES = (["v", "s", "t", "gp", "out"] + ["ld_" + n for n in LOADS]
-              + ["l%s%d" % (k, t) for k in KINDS for t in range(ROUNDS)] + ["a%s%d" % (k, t) for k in KINDS for t in range(ROUNDS)])
+SEMAPHORES = (["v", "s", "t", "gp", "out", "sent", "aq", "aya", "ayb", "afa", "afb"] + ["ld_" + n for n in LOADS]
+              + ["%s%d" % (k, t) for k in ("tz", "tr", "tx", "tw", "ab", "af") for t in range(ROUNDS)]
+              + ["u%d%d" % (t, k) for t in range(ROUNDS) for k in range(t + 2, ROUNDS)])
 WIDTH = {n: s[1][1] for n, s in LOGICAL.items()}
 PSUM = {n for n, s in LOGICAL.items() if s[0] == "psum"}
 TWO = {n for n, s in LOGICAL.items() if s[2] in (BF, F16, U16)}
-CYC, GATHER = 1.0e-3, 1.55
+CYC, PECYC, GATHER = 0.83e-3, 0.42e-3, 1.56
 
 
 def A(name, lo=0, hi=None, st=1):
@@ -73,6 +71,10 @@ def Ind(win, off):
 
 def size(a):
     return 16 * size(a[2]) if a[0] == "@" else (a[2] - a[1] + a[3] - 1) // a[3]
+
+
+def nbytes(a):
+    return 128 * size(a) * (2 if a[0] in TWO else 4)
 
 
 def ap(T, a):
@@ -94,25 +96,26 @@ def flat(aps):
 
 def build():
     ops = []
+    tag = [""]
 
-    def add(q, cost, outs, ins, fn, **kw):
-        op = dict(q=q, cost=cost, outs=flat(outs), ins=flat(ins), fn=fn, **kw)
+    def add(q, work, outs, ins, fn, **kw):
+        op = dict(q=q, work=work, outs=flat(outs), ins=flat(ins), fn=fn, tag=tag[0], **kw)
         ops.append(op)
         return op
 
-    def vcost(aps, mode):
-        n = size(aps[0])
+    def vwork(aps, mode):
+        n = max(size(a) for a in aps)
         if any(a[0] == "@" for a in aps):
-            return 0.06 + n * GATHER * CYC
+            return ("gather", n)
         per = 1.0
         if mode == "tt":
             per = 1.0 if any(a[0] in PSUM for a in aps[1:]) else 2.0
         elif all(a[0] in TWO for a in aps):
             per = 0.5
-        return 0.06 + max(64, n * per) * CYC
+        return ("plain", max(64, n * per))
 
     def tt(out, a, b, op):
-        add("V", vcost((out, a, b), "tt"), [out], [a, b], lambda c: c["V"].tensor_tensor(ap(c["T"], out), ap(c["T"], a), ap(c["T"], b), op))
+        add("V", vwork((out, a, b), "tt"), [out], [a, b], lambda c: c["V"].tensor_tensor(ap(c["T"], out), ap(c["T"], a), ap(c["T"], b), op))
 
     def ts(out, a, s1, op0, s2=None, op1=None):
         def fn(c):
@@ -120,32 +123,31 @@ def build():
             if op1 is None:
                 return c["V"].tensor_scalar(ap(c["T"], out), ap(c["T"], a), x1, None, op0)
             return c["V"].tensor_scalar(ap(c["T"], out), ap(c["T"], a), x1, s2, op0, op1)
-        add("V", vcost((out, a), "ts"), [out], [a, s1], fn)
+        add("V", vwork((out, a), "ts"), [out], [a, s1], fn)
 
     def cp(out, a):
-        add("V", vcost((out, a), "ts"), [out], [a], lambda c: c["V"].tensor_copy(ap(c["T"], out), ap(c["T"], a)))
+        add("V", vwork((out, a), "ts"), [out], [a], lambda c: c["V"].tensor_copy(ap(c["T"], out), ap(c["T"], a)))
 
     def fill(out, val):
-        add("V", 0.06 + size(out) * CYC, [out], [], lambda c: c["V"].memset(ap(c["T"], out), val))
+        add("V", vwork((out,), "ts"), [out], [], lambda c: c["V"].memset(ap(c["T"], out), val))
 
     def scan(out, d0, d1, op0, op1):
-        add("V", vcost((out, d0, d1), "ts"), [out], [d0, d1],
+        add("V", vwork((out, d0, d1), "ts"), [out], [d0, d1],
             lambda c: c["V"].tensor_tensor_scan(ap(c["T"], out), ap(c["T"], d0), ap(c["T"], d1), 0.0, op0, op1))
 
     def vtr(out, a):
-        add("V", vcost((out, a), "ts"), [out], [a], lambda c: c["V"].transpose(ap(c["T"], out), ap(c["T"], a)))
+        add("V", vwork((out, a), "ts"), [out], [a], lambda c: c["V"].transpose(ap(c["T"], out), ap(c["T"], a)))
 
     def act(out, a, func=None, bias=0.0, scale=1.0, accum=None):
         func = ACT.Identity if func is None else func
-        n = size(out)
 
         def fn(c):
             x = ap(c["T"], accum) if accum is not None else None
             b = ap(c["T"], bias) if isinstance(bias, tuple) else bias
             return c["S"].activation(ap(c["T"], out), ap(c["T"], a), func, bias=b, scale=scale, accum_out=x)
-        add("S", 0.08 + n * CYC * (GATHER if a[0] == "@" else 1.0), [out] + ([accum] if accum is not None else []), [a, bias], fn)
+        add("S", ("gather" if a[0] == "@" else "plain", size(out)), [out] + ([accum] if accum is not None else []), [a, bias], fn)
 
-    def mm(items):
+    def mm(items, weight=1):
         def fn(c):
             m = None
             for o, l, r, s, e in items:
@@ -156,356 +158,532 @@ def build():
             for x, d in ((o, outs), (l, ins), (r, ins)):
                 if x not in d:
                     d.append(x)
-        add("P", sum(max(64, size(i[2])) for i in items) * 0.5e-3 + 0.02, outs, ins, fn)
+        add("P", ("pe", weight * sum(max(64, size(i[2])) for i in items)), outs, ins, fn)
 
     def aff(out, a, pattern, cmp, base, cm):
-        add("G", 0.2 + 2 * size(out) * CYC, [out], [a], lambda c: c["g"].affine_select(ap(c["T"], out), ap(c["T"], a), pattern, cmp, 0.0, base, cm), sem="gp")
+        add("G", ("aff", size(out)), [out], [a], lambda c: c["g"].affine_select(ap(c["T"], out), ap(c["T"], a), pattern, cmp, 0.0, base, cm), sem="gp")
 
     def iota(out, pattern, base):
-        add("G", 0.15 + 2 * size(out) * CYC, [out], [], lambda c: c["g"].iota(ap(c["T"], out), pattern, base, 0, allow_small_or_imprecise_dtypes=True), sem="gp")
+        add("G", ("aff", size(out)), [out], [], lambda c: c["g"].iota(ap(c["T"], out), pattern, base, 0, allow_small_or_imprecise_dtypes=True), sem="gp")
 
-    def load(out, name):
-        add("Y", 0.15, [out], [], lambda c: c["g"].sync.dma_start(ap(c["T"], out), c["T"][name][:]), sem="ld_" + name, inc=16, lat=2.0 + size(out) / 2000.0)
+    def load(q, out, name):
+        add(q, ("dma", 1), [out], [], lambda c: c[q].dma_start(ap(c["T"], out), c["T"][name][:]), sem="ld_" + name, inc=16, nbytes=nbytes(out), bulk="load")
 
-    def store(name, lo, hi, a):
-        add("Y", 0.15, [], [a], lambda c: c["g"].sync.dma_start(c["T"][name][:, lo:hi], ap(c["T"], a)), sem="out", inc=16, lat=2.0)
+    def store(name, lo, a):
+        add("Y", ("dma", 1), [], [a], lambda c: c["Y"].dma_start(c["T"][name][:, lo:lo + size(a)], ap(c["T"], a)), sem="out", inc=16, nbytes=nbytes(a))
 
-    def send(kind, t, dst, src):
+    def send(name, by, pairs, behind=(), bulk="table"):
         def fn(c):
-            to = c["T"].cores[(c["rank"] + 1 + t % 3) % len(c["T"].cores)]
+            to = c["T"].cores[(c["rank"] + by) % RANKS]
             topo = c["topo"]
             rid, pid, _ = topo.addr(to)
-            c["g"].remote_dma(ap(c["T"], dst), ap(c["T"], src), c["T"].sem["a%s%d" % (kind, t)], c["T"].sem["l%s%d" % (kind, t)],
-                              pid, rid, topo.mask(c["core"], to))
-        s = add("G", 0.2, [], [src], fn, sem="l%s%d" % (kind, t), inc=16, own=True, lat=2.0)
-        add("R", 0.0, [dst], [], None, sem="a%s%d" % (kind, t), inc=16, after=s, lat=2.2)
+            for dst, src in pairs:
+                c["g"].remote_dma(ap(c["T"], dst), ap(c["T"], src), c["T"].sem[name], c["T"].sem["sent"], pid, rid, topo.mask(c["core"], to))
+        k = len(pairs)
+        o = add("G", ("send", k), [], [x for _, x in pairs] + list(behind), fn, sem="sent", inc=16 * k, own=True, bulk=bulk and "call")
+        add("R", ("land", 0), [x for x, _ in pairs], [], None, sem=name, inc=16 * k, after=o, bulk=bulk, nbytes=sum(nbytes(x) for x, _ in pairs))
 
     def route(tab, x):
         return A(tab, 15 - x, 143 - x)
 
-    load(A("pin"), "p0"); load(A("wti"), "wt"); load(A("kmi"), "km")
-    load(A("Z", 0, A0), "zp"); load(A("rti"), "rt"); load(A("X", 0, NV), "ax"); load(A("exi"), "ex")
-    fill(A("ones", 0, 128), 1.0)
+    def steps(lo, hi, step):
+        return [(x, min(hi, x + step)) for x in range(lo, hi, step)]
+
+    step, sstep = CFG["step"], CFG["sstep"]
+    load("Y", A("pin"), "p0"); load("S", A("wti"), "wt"); load("S", A("kmi"), "km")
+    load("Y", A("Z0"), "zp"); load("Y", A("rti"), "rt"); load("Y", A("X0", 0, NV), "ax"); load("Y", A("exi"), "ex")
+    fill(A("ones"), 1.0)
     aff(A("blk"), A("ones", 0, 128), [[-16, 8], [0, 16]], ALU.is_ge, 0, 1)
     aff(A("blk"), A("blk"), [[16, 8], [0, 16]], ALU.is_ge, 15, -1)
-    for c, (j0, P) in enumerate(CHUNKS):
-        for par in range(2):
-            cp(A("p", 2 * j0 + par * P, 2 * j0 + par * P + P), A("pin", 2 * j0 + par, 2 * j0 + 2 * P, 2))
-    ts(A("whi"), A("wti"), 6, ALU.logical_shift_right)
-    ts(A("wli"), A("wti"), 63, ALU.bitwise_and)
-    ts(A("whf"), A("whi"), 64.0, ALU.mult)
-    cp(A("wlf"), A("wli"))
-    ts(A("wh"), A("blk"), A("whf"), ALU.mult)
-    ts(A("wl"), A("blk"), A("wlf"), ALU.mult)
-    ts(A("kf"), A("kmi"), 4096.0, ALU.subtract)
-    send("p", 0, A("Z", A0, A0 + 256), A("pin"))
+    aff(A("idb"), A("ones", 0, 128), [[-1, 128]], ALU.is_equal, 0, 1)
     fill(A("gsp"), 0.0)
     aff(A("gsp", 15, 143, 16), A("ones", 0, 8), [[-16, 8]], ALU.is_ge, 0, 1)
     aff(A("gsp", 15, 143, 16), A("gsp", 15, 143, 16), [[16, 8]], ALU.is_ge, 15, -1)
-    act(A("gmin"), A("gsp"), scale=-8192.0)
-    act(A("gz"), A("gsp"), scale=4096.0)
-    act(A("ghalf"), A("gsp"), scale=0.5)
+    for name, src, scale in (("nidb", "idb", -1.0), ("ih", "idb", 0.5), ("nih", "idb", -0.5), ("gz", "gsp", 4096.0), ("ghalf", "gsp", 0.5),
+                             ("gb", "gsp", B), ("gbh", "gsp", B / 2), ("ib", "idb", B), ("nib", "idb", -B), ("i8", "idb", 8192.0), ("ni8", "idb", -8192.0)):
+        act(A(name), A(src), scale=scale)
+    if 2 in CFG["z"]:
+        act(A("gz2"), A("gsp"), scale=8192.0)
+        act(A("gzn"), A("gsp"), scale=-4096.0)
+    fill(A("k2048"), 2048.0)
     fill(A("seg"), 0.0)
     fill(A("seg", 0, 128, 16), 1e9)
     for qh in range(2):
         for gp in range(2):
             k = 128 * (2 * qh + gp)
-            aff(A("prmb", k, k + 128), A("ones", 0, 128), [[-32, 4], [-1000, 2], [-1, 16]], ALU.is_equal, 1000 * gp - 16 * qh, 1)
-    cp(A("prm"), A("prmb"))
-    aff(A("idb"), A("ones", 0, 128), [[-1, 128]], ALU.is_equal, 0, 1)
-    act(A("nidb"), A("idb"), scale=-1.0)
-    act(A("nid100"), A("idb"), scale=-100.0)
-    ts(A("nidh"), A("idb"), -1.0, ALU.mult)
-    cp(A("idh"), A("idb"))
-    ts(A("k2048"), A("ones", 0, 64), 2048.0, ALU.mult)
-    fill(A("bar"), 3.5)
-    fill(A("ones", 128, 2048), 1.0)
-    aff(A("bcb"), A("ones"), [[-1, 16], [-16, 8], [0, 16]], ALU.is_equal, 0, 1)
-    fill(A("X", NV, NV + 16), 0.0)
+            aff(A("prm", k, k + 128), A("ones", 0, 128), [[-32, 4], [-1000, 2], [-1, 16]], ALU.is_equal, 1000 * gp - 16 * qh, 1)
+    fill(A("k8"), 8.0)
+    fill(A("bar0"), -3.5)
+    fill(A("half"), 0.5)
+    for k in range(0, 16, 4):
+        aff(A("bc", 128 * k, 128 * k + 512), A("ones"), [[-1, 4], [-16, 8], [0, 16]], ALU.is_equal, -k, 1)
     fill(A("rmask"), 1.0)
     fill(A("rmask", 0, 1024, 16), 0.0)
-    fill(A("g0b"), 0.0)
-    aff(A("g0b", 15, 143, 16), A("ones", 0, 8), [[-16, 8]], ALU.is_equal, 0, 1)
-    for k in range(0, 2048, 512):
-        cp(A("bc", k, k + 512), A("bcb", k, k + 512))
-    cp(A("g0"), A("g0b"))
-    for t in range(ROUNDS):
-        for c, (j0, P) in enumerate(CHUNKS):
-            iota(A("nr%d" % t, 2 * j0, 2 * j0 + 2 * P), [[0, 2], [1, P]], REC - 2048 + H * t + j0)
-    for k in range(0, A0, 512):
-        cp(A("R", k, k + 512), A("rti", k, k + 512))
-    for c, (j0, P) in enumerate(CHUNKS):
+    fill(A("g0"), 0.0)
+    aff(A("g0", 15, 143, 16), A("ones", 0, 8), [[-16, 8]], ALU.is_equal, 0, 1)
+    iota(A("nrb"), [[0, 2], [1, P]], 0)
+    ts(A("whi"), A("wti"), 6, ALU.logical_shift_right)
+    ts(A("wli"), A("wti"), 63, ALU.bitwise_and)
+    ts(A("whf"), A("whi"), -32.0, ALU.mult)
+    ts(A("wlf"), A("wli"), -0.5, ALU.mult)
+    ts(A("w0", 0, 128), A("blk"), A("whf"), ALU.mult)
+    ts(A("w0", 128, 256), A("blk"), A("wlf"), ALU.mult)
+    fill(A("ek0", 256, 264), 0.0)
+    ts(A("ek0", 256, 257), A("kmi"), 4096.0 - (0 if CFG["uu2"] else 64), ALU.subtract)
+    fill(A("X0", NV, NV + 16), 0.0)
+    wide = [max(CFG["nv1"][i], CFG["nv2"][i], P * (CFG["z"][i] > 1)) for i in range(2)]
+    for i, s in enumerate("ab"):
+        fill(A("pz" + s, 0, 16 * wide[i]), 0.0)
+        fill(A("B%d" % (4 * i + 1), 0, 512, 4), -B)
+        fill(A("d1" + s, 1, 4 * L, 4), -B)
         for par in range(2):
-            cp(A("ef", 2 * j0 + par * P, 2 * j0 + par * P + P), A("exi", 2 * j0 + par, 2 * j0 + 2 * P, 2))
+            ts(A("pm" + s, P * par, P * par + P), A("pin", L * i + par, L * i + L, 2), -2.0, ALU.mult, -2048.0, ALU.add)
+            ts(A("ek0", L * i + P * par, L * i + P * par + P), A("exi", L * i + par, L * i + L, 2), 4096.0, ALU.subtract)
+    for k in range(0, A0, 512):
+        cp(A("R0", k, k + 512), A("rti", k, k + 512))
+
+    def tables(k):
+        send("tx%d" % k, -AT[k], [(A("X%d" % k, 0, REC), A("X0", 0, REC)), (A("X%d" % k, REC + H * k), A("X0", REC + H * k))])
+        send("tw%d" % k, -AT[k], [(A("w%d" % k), A("w0")), (A("ek%d" % k), A("ek0"))])
+        send("tz%d" % k, -AT[k], [(A("Z%d" % k, 0, A0), A("Z0"))])
+        send("tr%d" % k, -AT[k], [(A("R%d" % k, 0, A0), A("R0"))])
+    tables(1)
 
     for t in range(ROUNDS):
         n = A0 + 256 * t
-        NC = len(CHUNKS)
-        if t > 0:
-            for c, (j0, P) in enumerate(CHUNKS):
-                for par in range(2):
-                    aff(A("pn%d" % t, 2 * j0 + par, 2 * j0 + 2 * P, 2), A("p", 2 * j0 + par * P, 2 * j0 + par * P + P), [[0, P]], ALU.is_ge, 0, 0)
-            send("p", t, A("Z", n, n + 256), A("pn%d" % t))
-        for c, (j0, P) in enumerate(CHUNKS):
-            mm([(A("B0", j0, j0 + P), A("wh"), A("p", 2 * j0, 2 * j0 + P), True, False),
-                (A("B0", j0, j0 + P), A("wl"), A("p", 2 * j0, 2 * j0 + P), False, True)])
-        cp(A("ui"), A("B0", 0, 128))
-        ts(A("u"), A("ui"), 4095, ALU.bitwise_and)
-        tt(A("uu"), A("u"), A("u"), ALU.mult)
-        ts(A("ku"), A("u"), A("kf"), ALU.mult)
-        ts(A("su"), A("uu"), 5, ALU.logical_shift_right)
-        tt(A("hs"), A("su"), A("ku"), ALU.add)
-        ts(A("hh"), A("hs"), 4095, ALU.bitwise_and)
-        ts(A("cq"), A("hh"), (8 + t) / 16.0, ALU.mult, -15.0 / 32, ALU.add)
-        for k in range(16):
-            rep = (REP if t else REP0)[k]
-            if rep == "S":
-                act(A("prep", k, 4096, 16), A("p"))
-            elif rep == "G":
-                aff(A("prep", k, 4096, 16), A("p"), [[0, 256]], ALU.is_ge, 0, 0)
+        X, Z, R, Xn = "X%d" % t, "Z%d" % t, "R%d" % t, "X%d" % SLOT[t + 1]
+        Zn, Rn = (A("%s%d" % (x, t + 1), n, n + 256) if t < ROUNDS - 1 else A(x + "4") for x in "ZR")
+        Qn = A(Xn, REC + H * t, REC + H * t + H)
+        for i, s in enumerate("ab"):
+            tag[0] = "%s%d" % (s, t)
+            a, b, c, d = ("B%d" % (4 * i + k) for k in range(4))
+            nv1, nv2, zv = CFG["nv1"][i], CFG["nv2"][i], CFG["z"][i]
+
+            def N(name, lo=0, hi=None, k=1, s=s):
+                return A(name + s, lo, hi, k)
+            o = A(a, 0, P)
+            wh, wl = A("w%d" % t, 0, 128), A("w%d" % t, 128, 256)
+            mm([(o, wh, N("pm", 0, P), True, False), (o, wh, A("k2048", 0, P), False, False),
+                (o, wl, A("k2048", 0, P), False, False), (o, wl, N("pm", 0, P), False, True)])
+            U, KU = A(b, 1, 4 * P, 4), A(b, 3, 4 * P, 4)
+            cp(N("ui"), o)
+            ts(N("u"), N("ui"), 4095, ALU.bitwise_and)
+            ts(U, N("u"), 2048.0, ALU.subtract)
+            ts(KU, N("u"), A("ek%d" % t, 256, 257), ALU.mult)
+            tt(N("uu"), N("u"), N("u") if CFG["uu2"] else U, ALU.mult)
+            ts(N("su"), N("uu"), 5, ALU.arith_shift_right)
+            tt(N("hs"), N("su"), KU, ALU.add)
+            ts(N("hh"), N("hs"), 4095, ALU.bitwise_and)
+            ts(N("cq"), N("hh"), (8 + t) / 16.0, ALU.mult, -15.0 / 32, ALU.add)
+            ts(N("ch"), N("cq"), 2048.0, ALU.subtract)
+            mm([(A(c, 0, L), A("nih"), N("pm"), True, True)])
+            for l0, l1 in steps(0, wide[i], P):
+                act(N("pz", 16 * l0, 16 * l1, 16), A(c, l0, l1), bias=-1024.0)
+                scan(N("prep", 16 * l0, 16 * l1), A("rmask", 0, 16 * (l1 - l0)), N("pz", 16 * l0, 16 * l1), ALU.mult, ALU.add)
+            act(N("pq"), A(c, 0, L), bias=255 + 2047.5 - 1024)
+            if t < ROUNDS - 1:
+                mm([(A(d, par, L, 2), A("nih"), N("pm", P * par, P * par + P), True, True) for par in range(2)])
+                act(A(Zn[0], n + L * i, n + L * i + L), A(d, 0, L), bias=-1024.0)
+            act(N("d1", 3, 4 * L, 4), A("ek%d" % t, L * i, L * i + L))
+            key = A(a, 192, 320)
+            ke, ko = A(a, 192, 256), A(a, 256, 320)
+            opening = [(key, A("idb"), A("k2048"), True, False), (ke, A("idb"), N("ch"), False, False), (ko, A("idb"), N("ch"), False, False)]
+            if zv > 1:
+                for l0, l1 in steps(0, P, step):
+                    tt(N("zg", 16 * l0, 16 * l1), Ind(A(Z), N("cq", l0, l1)), N("prep", 16 * l0, 16 * l1), ALU.subtract)
+                    if zv == 3:
+                        act(N("re", 16 * l0, 16 * l1), N("zg", 16 * l0, 16 * l1), ACT.Abs)
+                if zv == 2:
+                    ts(N("re"), N("zg"), 0.0, ALU.max)
+                if CFG["delta"]:
+                    tt(N("dl"), N("pm", P, L), N("pm", 0, P), ALU.subtract)
+                for k in range(2):
+                    bk, items = (c, d)[k], []
+                    for m in range(8 * k, 8 * k + 8):
+                        o = A(bk, P * (m % 8), P * (m % 8) + P)
+                        items += ([(o, A("ih"), N("dl"), True, False)] if CFG["delta"] else
+                                  [(o, A("nih"), N("pm", 0, P), True, False), (o, A("ih"), N("pm", P, L), False, False)])
+                        items += [(o, A("idb"), N("zg", m, 16 * P, 16), False, True)]
+                    mm(items)
+                    act(N("ad", 512 * k, 512 * k + 512), A(bk), ACT.Abs)
+                mm(opening)
+                if zv == 2:
+                    mm([(ke, route("gzn", m), N("zg", m, 16 * P, 16), False, False) for m in range(16)])
+                mm([(ke, route("gz2" if zv == 2 else "gz", m), N("re", m, 16 * P, 16), False, False) for m in range(16)])
+                for k in range(2):
+                    mm([(ko, route("gz", m), N("ad", P * m, P * m + P), False, m == 15) for m in range(8 * k, 8 * k + 8)])
             else:
-                cp(A("prep", k, 4096, 16), A("p"))
-        ts(A("ch"), A("cq"), 2048.0, ALU.subtract)
-        ts(A("uh"), A("u"), 2048.0, ALU.subtract)
-        for c, (j0, P) in enumerate(CHUNKS):
-            for par, d in ((0, "de_%d" % c), (1, "do_%d" % c)):
-                b = 16 * (2 * j0 + par * P)
-                if (c, par) not in Z_S:
-                    tt(A(d), Ind(A("Z", 0, n), A("cq", j0, j0 + P)), A("prep", b, b + 16 * P), ALU.min)
-            act(A("zg_%d" % c), Ind(A("Z", 0, n), A("cq", j0, j0 + P)))
-        for c, par in Z_S:
-            j0, P = CHUNKS[c]
-            b = 16 * (2 * j0 + par * P)
-            for i, k in enumerate(range(0, 16 * P, 512)):
-                sb = ("B7", "B%d" % (1 + c % 2))[i % 2]
-                mm([(A(sb), A("idb"), A("zg_%d" % c, k, k + 512), True, False), (A(sb), A("nidb"), A("prep", b + k, b + k + 512), False, True)])
-                act(A("%s_%d" % (("de", "do")[par], c), k, k + 512), A(sb), ACT.Abs)
-        for c, (j0, P) in enumerate(CHUNKS):
-            L, bk, tb, cs = 2 * P, "B%d" % (1 + c % 2), "B%d" % (3 + c % 2), "_%d" % c
-            for par, d in ((0, "de"), (1, "do")):
-                o = A(bk, par * P, par * P + P)
-                mm([(o, A("idh"), A("k2048", 0, P), True, False), (o, A("idh"), A("ch", j0, j0 + P), False, False)]
-                   + [(o, route("gz", m), A("zg" + cs, m, 16 * P, 16), False, False) for m in range(16) if (c, par) not in Z_S])
-                mm([(o, route("gz" if (c, par) in Z_S else "gmin", m), A(d + cs, m, 16 * P, 16), False, m == 15) for m in range(16)])
-            vtr(A("tr" + cs), A(bk, 0, L))
-            scan(A("mk" + cs), A("seg", 0, L), A("tr" + cs), ALU.add, ALU.min)
-            ts(A("ai" + cs), A("mk" + cs, 15, L, 16), 4095, ALU.bitwise_and)
-            ts(A("ah" + cs), A("ai" + cs), 2048.0, ALU.subtract)
-            q0 = 128 + 2 * j0 // 16
-            items = []
-            for qh in range(2):
-                for gp in range(2):
-                    k = 128 * (2 * qh + gp)
-                    items.append((A("B0", q0 + qh, q0 + L // 16, 2), A("prm", k, k + 128), A("ah" + cs, gp, L // 16, 2), gp == 0, gp == 1))
-            mm(items)
-            ts(A("au" + cs), A("B0", q0, q0 + L // 16), 2048.0, ALU.add)
-            cp(A("eu" + cs), Ind(A("R", 0, n), A("au" + cs)))
-            act(A("e" + cs), Ind(A("R", 0, n), A("au" + cs)))
-            mm([(A(tb, par * P, par * P + P), A("idh"), A("uh", j0, j0 + P), True, True) for par in range(2)])
-            act(A(tb, 128, 128 + L), A("e" + cs), bias=2464.0 * t - 131072.0, scale=2080.0)
-            act(A(tb, 256, 256 + L), A("e" + cs))
-            tt(A("t1" + cs), A("e" + cs), A(tb, 0, L), ALU.mult)
-            tt(A("nn" + cs), A("t1" + cs), A(tb, 128, 128 + L), ALU.add)
-            ts(A("e2" + cs), A("nn" + cs), 5, ALU.arith_shift_right, 4095, ALU.bitwise_and)
-            cp(A("e2u" + cs), A("e2" + cs))
-        for c, (j0, P) in enumerate(CHUNKS):
-            L, bk, tb, cs = 2 * P, "B%d" % (1 + c % 2), "B%d" % (3 + c % 2), "_%d" % c
-            b = 32 * j0
-            for l0 in range(0, L, C1STEP):
-                tt(A("c1" + cs, 16 * l0, 16 * (l0 + C1STEP)), Ind(A("X", 0, NV), A("eu" + cs, l0, l0 + C1STEP)),
-                   A("prep", b + 16 * l0, b + 16 * (l0 + C1STEP)), ALU.is_ge)
-            act(A("em" + cs), A("e" + cs), bias=-2048.0)
-            tt(A(tb, 384, 384 + L), A("ef", 2 * j0, 2 * j0 + L), A(tb, 256, 256 + L), ALU.subtract)
-            tt(A(tb, 0, L), A("e2" + cs), A(tb, 256, 256 + L), ALU.subtract)
-            ns = SCALAR_LANES[c]
-            for i, l0 in enumerate(range(0, ns, 32)):
-                sb = ("B7", "B6" if c == 0 else "B0")[i % 2]
-                x = A("xg" + cs, 16 * l0, 16 * (l0 + 32))
-                act(x, Ind(A("X", 0, NV), A("e2u" + cs, l0, l0 + 32)))
-                mm([(A(sb), A("idb"), x, True, False),
-                    (A(sb), A("nidb"), A("prep", b + 16 * l0, b + 16 * (l0 + 32)), False, True)])
-                act(A("c2" + cs, 16 * l0, 16 * (l0 + 32)), A(sb), ACT.Sign, bias=0.5)
-            for l0 in range(ns, L, 64):
-                hi = min(l0 + 64, L)
-                tt(A("c2" + cs, 16 * l0, 16 * hi), Ind(A("X", 0, NV), A("e2u" + cs, l0, hi)), A("prep", b + 16 * l0, b + 16 * hi), ALU.is_ge)
-        for c, (j0, P) in enumerate(CHUNKS):
-            L, bk, tb, cs = 2 * P, "B%d" % (1 + c % 2), "B%d" % (3 + c % 2), "_%d" % c
-            ns = SCALAR_LANES[c]
-            for h in range(2):
-                mm([(A(bk, 128 + h * P, 128 + h * P + P), route("gsp", k), A("c1" + cs, 16 * P * h + k, 16 * P * h + 16 * P, 16), k == 0, k == 15) for k in range(16)])
-            act(A("sg" + cs), A(bk, 128, 128 + L), ACT.Sign, bias=A("bar"), scale=-1.0)
-            act(A("mb" + cs), A("sg" + cs), ACT.Relu)
-            act(A("r1" + cs), A(bk, 128, 128 + L), ACT.Relu, bias=-800.0, scale=100.0)
-            if ns > 0:
-                act(A("g1c" + cs, 0, ns), A(bk, 128, 128 + ns), bias=-8.0)
-            if ns < L:
-                act(A("g1c" + cs, ns, L), A(bk, 128 + ns, 128 + L))
-            tt(A(tb, 128, 128 + L), A("mb" + cs), A(tb, 384, 384 + L), ALU.mult)
-            tt(A("base" + cs), A(tb, 128, 128 + L), A("em" + cs), ALU.add)
-            for lo, hi, tab in [(l0, min(l0 + 64, L), "gsp") for l0 in range(ns, L, 64)] + [(0, ns, "ghalf")] * (ns > 0):
-                o = A(bk, 256 + lo, 256 + hi)
-                mm([(o, route(tab, k), A("c2" + cs, 16 * lo + k, 16 * hi, 16), k == 0, False) for k in range(16)])
-                mm([(o, A("nid100"), A("mb" + cs, lo, hi), False, False), (o, A("nidb"), A("r1" + cs, lo, hi), False, False),
-                    (o, A("nidb"), A("g1c" + cs, lo, hi), False, True)])
-            ts(A("ma" + cs), A(bk, 256, 256 + L), 0.0, ALU.is_ge)
-            tt(A(tb, 256, 256 + L), A("ma" + cs), A(tb, 0, L), ALU.mult)
-            tt(A("f" + cs), A(tb, 256, 256 + L), A("base" + cs), ALU.add)
-            tt(A(tb, 0, L), A("nr%d" % t, 2 * j0, 2 * j0 + L), A("f" + cs), ALU.subtract)
-            for h in range(2):
-                eb = "B%d" % (5 + h)
-                items = []
-                for k in range(8):
-                    o = A(eb, k * P, k * P + P)
-                    items.append((o, A("nidh"), A("f" + cs, 0, P), True, False))
-                    items.append((o, A("bc", 128 * (8 * h + k), 128 * (8 * h + k) + 128), A("f" + cs, P, L), False, True))
-                mm(items)
-                x = A("eq" + cs, 8 * P * h, 8 * P * h + 8 * P)
-                if EQ_S[c]:
-                    y = A("ez" + cs, 8 * P * h, 8 * P * h + 8 * P)
-                    act(y, A(eb, 0, 8 * P), ACT.Abs)
-                    act(x, y, ACT.Relu, bias=1.0, scale=-1.0)
-                else:
-                    ts(x, A(eb, 0, 8 * P), 0.0, ALU.is_equal)
-            for h in range(2):
-                for par in range(2):
-                    mm([(A(("B7" if par else bk), 384, 384 + P), route("gsp", k) if par else A("idb"), A("eq" + cs, k * P, k * P + P), k == 0, k == 15)
-                        for k in range(8 * h, 8 * h + 8)])
-            act(A(tb, 384, 384 + P), A(bk, 384, 384 + P), bias=2048.0, scale=-8192.0)
-            act(A("cm" + cs, P, L), A("B7", 384, 384 + P), ACT.Sign)
-            act(A("cm" + cs, 0, P), A(bk, 384, 384 + P), ACT.Sign)
-            tt(A("rt1" + cs), A(tb, 384, 384 + P), A("f" + cs, 0, P), ALU.max)
-            ts(A("ro" + cs), A("rt1" + cs), 2048.0, ALU.add)
-            ps = int(P * REC_S[c]) // 16 * 16
-            if ps:
-                act(A("xr" + cs, 0, 16 * ps), Ind(A("X"), A("ro" + cs, 0, ps)))
-            if ps < P:
-                cp(A("xr" + cs, 16 * ps, 16 * P), Ind(A("X"), A("ro" + cs, ps, P)))
-            tt(A(tb, 128, 128 + L), A("cm" + cs), A(tb, 0, L), ALU.mult)
-            tt(A("fh" + cs), A(tb, 128, 128 + L), A("f" + cs), ALU.add)
+                for l0, l1 in steps(0, P, sstep):
+                    act(N("zg", 16 * l0, 16 * l1), Ind(A(Z), N("cq", l0, l1)))
+                for k in range(4):
+                    bk, items = (c, d)[k % 2], []
+                    for m in range(4 * k, 4 * k + 4):
+                        o0 = L * (m % 4)
+                        items += [(A(bk, o0, o0 + L), A("ih"), N("pm"), True, False),
+                                  (A(bk, o0, o0 + P), A("idb"), N("zg", m, 16 * P, 16), False, False),
+                                  (A(bk, o0 + P, o0 + L), A("idb"), N("zg", m, 16 * P, 16), False, True)]
+                    mm(items)
+                    act(N("ad", 512 * k, 512 * k + 512), A(bk), ACT.Abs, bias=1024.0)
+                mm(opening)
+                for k in range(4):
+                    mm([(key, route("gz", m), N("ad", L * m, L * m + L), False, m == 15) for m in range(4 * k, 4 * k + 4)])
+            vtr(N("tr"), key)
+            scan(N("mk"), A("seg"), N("tr"), ALU.add, ALU.min)
+            ts(N("ai"), N("mk", 15, L, 16), 4095, ALU.bitwise_and)
+            ts(N("ah"), N("ai"), 2048.0, ALU.subtract)
+            mm([(A(a, 320 + qh, 328, 2), A("prm", 128 * (2 * qh + gp), 128 * (2 * qh + gp) + 128), N("ah", gp, 8, 2), gp == 0, gp == 1)
+                for qh in range(2) for gp in range(2)])
+            ts(N("au"), A(a, 320, 328), 2048.0, ALU.add)
+            e = N("d1", 2, 4 * L, 4)
+            (cp if CFG["e_v"][i] == 1 else act)(e, Ind(A(R), N("au")))
+            cp(N("eu"), e if CFG["e_v"][i] else Ind(A(R), N("au")))
+            act(N("lin"), Ind(A(R), N("au")) if CFG["lin_g"] else e, bias=2464.0 * t - 131072.0, scale=2080.0)
             for par in range(2):
-                mm([(A("B0", 256 + 2 * j0 + par, 256 + 2 * j0 + L, 2), A("nidh"), A("fh" + cs, par * P, par * P + P), True, True)])
-            act(A("F%d" % t, 2 * j0, 2 * j0 + L), A("B0", 256 + 2 * j0, 256 + 2 * j0 + L), bias=2048.0, scale=-1.0)
-            q0 = 160 + 2 * j0 // 16
-            mm([(A("B0", q0, q0 + L // 16), route("g0", x), A("fh" + cs, x, L, 16), x == 0, x == 15) for x in range(16)])
-            ts(A("LT%d" % t, 2 * j0 // 16, 2 * j0 // 16 + L // 16), A("B0", q0, q0 + L // 16), 2048.0, ALU.add)
-            scan(A("qs" + cs), A("rmask", 0, 16 * P), A("xr" + cs), ALU.mult, ALU.max)
-            cp(A("Q%d" % t, j0, j0 + P), A("qs" + cs, 15, 16 * P, 16))
-        send("F", t, A("R", n, n + 256), A("F%d" % t))
-        send("L", t, A("LL%d" % t), A("LT%d" % t))
-        send("Q", t, A("QL%d" % t), A("Q%d" % t))
-        if t < ROUNDS - 1:
-            mm([(A("B7", 0, 2 * P), A("ones", 0, 128), A("mb_%d" % c), c == 0, c == NC - 1) for c, (j0, P) in enumerate(CHUNKS)])
-            P0 = CHUNKS[0][1]
-            act(A("junk", 0, 2 * P0), A("B7", 0, 2 * P0), accum=A("cnt"))
-            cp(A("cnti"), A("cnt"))
-            ts(A("par"), A("cnti"), 1, ALU.bitwise_and)
-            ts(A("bar"), A("par"), 3.5, ALU.add)
-        store("yr", 256 * t, 256 * t + 256, A("R", n, n + 256))
-        cp(A("X", REC + H * t, REC + H * t + H), A("QL%d" % t))
-        for par in range(2):
-            for c, (j0, P) in enumerate(CHUNKS):
-                lo, hi = 2 * j0 + par * P, 2 * j0 + par * P + P
-                tt(A("dd", lo, hi), Ind(A("X", 0, NV), A("LL%d" % t, lo // 16, hi // 16)), A("Z", n + 2 * j0 + par, n + 2 * j0 + 2 * P, 2), ALU.subtract)
-                ts(A("pi", lo, hi), A("dd", lo, hi), -0.5, ALU.mult, 127.25, ALU.add)
-                if t < ROUNDS - 1:
-                    cp(A("p", lo, hi), A("pi", lo, hi))
+                tt(A(b, 2 + 4 * P * par, 4 * P * (par + 1), 4), N("d1", 2 + 4 * P * par, 4 * P * (par + 1), 4), U, ALU.mult)
+            tt(N("nn"), N("lin"), A(b, 2, 512, 4), ALU.add)
+            ts(N("e2"), N("nn"), 5, ALU.arith_shift_right, 4095, ALU.bitwise_and)
+            cp(N("e2u"), N("e2"))
+            ts(N("d1", 0, 4 * L, 4), N("e2"), 4096.0, ALU.add)
+
+            def votes(off, cmp, raw, nv):
+                ns = L - nv
+                if ns:
+                    for l0, l1 in steps(0, ns, sstep):
+                        act(N(raw, 16 * l0, 16 * l1), Ind(A(X, 0, NV), N(off, nv + l0, nv + l1)))
+                    for j, (k0, k1) in enumerate(steps(0, 16, 512 // ns)):
+                        bk, items = (c, d)[j % 2], []
+                        for k in range(k0, k1):
+                            o = A(bk, ns * (k - k0), ns * (k - k0 + 1))
+                            items += [(o, A("ih"), N("pm", nv, L), True, False), (o, A("idb"), N(raw, k, 16 * ns, 16), False, True)]
+                        mm(items)
+                        act(N(cmp, 16 * nv + ns * k0, 16 * nv + ns * k1), A(bk, 0, ns * (k1 - k0)), ACT.Sign, bias=1024.5)
+                for l0, l1 in steps(0, nv, step):
+                    tt(N(cmp, 16 * l0, 16 * l1), Ind(A(X, 0, NV), N(off, l0, l1)), N("prep", 16 * l0, 16 * l1), ALU.is_ge)
+
+            def sums(out, cmp, nv, whole, half, first):
+                ns = L - nv
+                for lo, hi in steps(0, nv, P):
+                    o = out(lo, hi)
+                    f = first(o, lo, hi, False)
+                    mm(f + [(o, route(whole, k), N(cmp, 16 * lo + k, 16 * hi, 16), k == 0 and not f, k == 15) for k in range(16)])
+                if ns:
+                    o = out(nv, L)
+                    for j, (k0, k1) in enumerate(steps(0, 16, 512 // ns)):
+                        mm(first(o, nv, L, True) * (j == 0)
+                           + [(o, route(half, k), N(cmp, 16 * nv + ns * k, 16 * nv + ns * k + ns), False, k == 15) for k in range(k0, k1)])
+            votes("eu", "c1", "x1", nv1)
+            votes("e2u", "c2", "x2", nv2)
+            sums(lambda lo, hi: A(a, 328 + lo, 328 + hi), "c1", nv1, "gsp", "ghalf",
+                 lambda o, lo, hi, sc: [(o, A("idb"), A("k8", lo, hi), True, False)] if sc else [])
+            g1 = A(a, 328, 456)
+            act(N("gq"), g1, bias=-8.5)
+            act(N("sb"), g1, ACT.Sign, bias=A("bar%d" % t), accum=A("cnt", i, i + 1))
+            if i and t < ROUNDS - 1:
+                o = A(a, 464, 465)
+                mm([(o, A("half"), A("cnt", 0, 1), True, False), (o, A("half"), A("cnt", 1, 2), False, True)], 4)
+                cp(A("cnti"), o)
+                ts(A("par"), A("cnti"), 1, ALU.bitwise_and)
+                ts(A("bo%d" % t), A("par"), -1.0, ALU.mult, -3.5, ALU.add)
+                send("ab%d" % t, AT[t] - AT[t + 1], [(A("bar%d" % (t + 1)), A("bo%d" % t))])
+            mm([(A(b, 2, 512, 4), A("nib"), N("gq"), True, True)])
+            mm([(A(b, 3, 512, 4), A("ib"), N("sb"), True, True)])
+            sums(lambda lo, hi: A(b, 4 * lo + 1, 4 * hi, 4), "c2", nv2, "gb", "gbh",
+                 lambda o, lo, hi, sc: [(o, A("nib"), N("gq", lo, hi), True, False)] + ([] if sc else [(o, A("nib"), A("k8", lo, hi), False, False)]))
+            for l0, l1 in steps(0, L, P if CFG["csplit"][i] else L):
+                scan(N("sc", 4 * l0, 4 * l1), A(b, 4 * l0, 4 * l1), N("d1", 4 * l0, 4 * l1), ALU.min, ALU.max)
+                ts(N("fi", l0, l1), N("sc", 4 * l0 + 3, 4 * l1, 4), 4095, ALU.bitwise_and)
+                ts(N("f", l0, l1), N("fi", l0, l1), 2048.0, ALU.subtract)
+            fe, fo = N("f", 0, P), N("f", P, L)
+            w = 16 // len(CFG["eq"][i])
+            for h, who in enumerate(CFG["eq"][i]):
+                bk, items = (c, d)[h % 2], []
+                for k in range(w):
+                    o = A(bk, k * P, k * P + P)
+                    items += [(o, A("nidb"), fe, True, False), (o, A("bc", 128 * (w * h + k), 128 * (w * h + k) + 128), fo, False, True)]
+                mm(items)
+                x = N("eq", w * P * h, w * P * h + w * P)
+                if who == "V":
+                    ts(x, A(bk, 0, w * P), 0.0, ALU.is_equal)
                 else:
-                    cp(A("yv", 2 * j0 + par, 2 * j0 + 2 * P, 2), A("pi", lo, hi))
-    store("yp", 0, 256, A("yv"))
+                    act(N("x1", w * P * h, w * P * h + w * P), A(bk, 0, w * P), ACT.Abs)
+                    act(x, N("x1", w * P * h, w * P * h + w * P), ACT.Relu, bias=1.0, scale=-1.0)
+            ye, co = A(a, 0, P), A(b, 1, 4 * P, 4)
+            for k0, k1 in steps(0, 16, w):
+                mm([(ye, A("idb"), A("k2048", 0, P), True, False)] * (k0 == 0)
+                   + [(ye, A("ni8"), N("eq", k * P, k * P + P), False, k == 15) for k in range(k0, k1)])
+            for k0, k1 in steps(0, 16, 8):
+                mm([(co, route("gsp", k), N("eq", k * P, k * P + P), k == 0, k == 15) for k in range(k0, k1)])
+            act(N("cm", 0, P), ye, ACT.Sign, bias=2048.0, scale=-1.0)
+            if CFG["ro1"][i]:
+                o = A(c, 0, P)
+                mm([(o, A("idb"), fe, True, False), (o, A("ni8"), N("cm", 0, P), False, True)])
+                ts(N("ro"), o, 2048.0 + 8192.0, ALU.add, 4096.0, ALU.min)
+            else:
+                tt(N("rt1"), fe, ye, ALU.max)
+                ts(N("ro"), N("rt1"), 2048.0, ALU.add)
+            act(N("cm", P, L), co, ACT.Sign)
+            ps = CFG["rec_s"][i]
+            for l0, l1 in steps(0, ps, CFG["rstep"]):
+                act(N("xr", 16 * l0, 16 * l1), Ind(A(X), N("ro", l0, l1)))
+            for l0, l1 in steps(ps, P, CFG["rstep"]):
+                cp(N("xr", 16 * l0, 16 * l1), Ind(A(X), N("ro", l0, l1)))
+            for l0, l1 in steps(0, ps, CFG["rstep"]) + steps(ps, P, CFG["rstep"]):
+                scan(N("qs", 16 * l0, 16 * l1), A("rmask", 0, 16 * (l1 - l0)), N("xr", 16 * l0, 16 * l1), ALU.mult, ALU.max)
+            cp(A(Xn, Qn[1] + P * i, Qn[1] + P * i + P), N("qs", 15, 16 * P, 16))
+            ops[-1]["mark"] = True
+            mm([(A(d, 0, L), A("idb"), A("nrb"), True, False), (A(d, 0, L), A("i8"), N("cm"), False, True)])
+            act(N("bs"), A(d, 0, L), bias=REC - 2048.0 - 8192.0 + H * t + P * i)
+            mm([(key, A("idb"), N("f"), True, False), (key, A("ni8"), N("cm"), False, True)])
+            tt(N("F"), N("bs"), key, ALU.max)
+            mm([(A(a, 456, 464), route("g0", x), N("F", x, L, 16), x == 0, x == 15) for x in range(16)])
+            ts(N("lu"), A(a, 456, 464), 2048.0, ALU.add)
+            mm([(A(d, par, L, 2), A("idb"), N("F", P * par, P * par + P), True, True) for par in range(2)])
+            mine = A(Rn[0], Rn[1] + L * i, Rn[1] + L * i + L)
+            act(mine, A(d, 0, L), bias=2048.0)
+            if t == ROUNDS - 1:
+                send("af" + s, AT[t + 1], [(A("FL%d" % t, L * i, L * i + L), mine)])
+                store("yr", 256 * t + L * i, A("FL%d" % t, L * i, L * i + L))
+        tag[0] = "u%d" % t
+        if t < ROUNDS - 1:
+            send("af%d" % t, AT[t + 1], [(A("FL%d" % t), Rn)])
+            store("yr", 256 * t, A("FL%d" % t))
+        for k in range(t + 2, ROUNDS):
+            send("u%d%d" % (t, k), AT[t + 1] - AT[k], [(A("%s%d" % (x[0][0], k), x[1], x[2]), x) for x in (Zn, Rn, Qn)])
+        if t + 2 < ROUNDS:
+            tables(t + 2)
+        if SLOT[ROUNDS] == t:
+            send("aq", AT[t + 1] - AT[ROUNDS], [(A("QL"), Qn)])
+            cp(A(X, Qn[1], Qn[2]), A("QL"))
+        for l0, l1, i in sorted((l0, l1, i) for i in range(2) for l0, l1 in steps(0, L, L if CFG["ddw"][i] or t == ROUNDS - 1 else P)):
+            s = "ab"[i]
+            tag[0] = "%s%d" % (s, t)
+            tt(A("pm" + s, l0, l1), Ind(A(Xn, 0, NV), A("lu" + s, l0 // 16, l1 // 16)), A("pq" + s, l0, l1), ALU.subtract)
+    for i, s in enumerate("ab"):
+        tag[0] = s + "4"
+        for par in range(2):
+            ts(A("yv", L * i + par, L * i + L, 2), A("pm" + s, P * par, P * par + P), -0.5, ALU.mult, -1024.0, ALU.add)
+        send("ay" + s, AT[ROUNDS], [(A("yl", L * i, L * i + L), A("yv", L * i, L * i + L))])
+        store("yp", L * i, A("yl", L * i, L * i + L))
     return ops
+
+
+def cost(op):
+    kind, n = op["work"]
+    if kind == "gather":
+        return 0.06 + n * GATHER * CYC, 0.0
+    if kind == "plain":
+        return 0.06 + n * CYC, 0.0
+    if kind == "pe":
+        return 0.02 + n * PECYC, 0.0
+    if kind == "aff":
+        return 0.17 + 2 * n * CYC, 0.0
+    if kind == "dma":
+        return 0.1 * n, 1.5
+    return (0.3 * n, 0.0) if kind == "send" else (0.0, 1.6)
 
 
 def overlap(a, b):
     if a[1] >= b[2] or b[1] >= a[2]:
         return False
-    return not (a[3] == b[3] and a[3] > 1 and (a[1] - b[1]) % a[3])
+    return (a[1] - b[1]) % math.gcd(a[3], b[3]) == 0
+
+
+def covers(a, b):
+    return a[1] <= b[1] and b[2] <= a[2] and b[3] % a[3] == 0 and (b[1] - a[1]) % a[3] == 0
 
 
 def dependencies(ops):
-    hist = {}
+    hist, last = {}, {}
     for i, op in enumerate(ops):
         op["i"] = i
         deps = {}
         acc = [(a, False) for a in op["ins"]] + [(a, True) for a in op["outs"]]
         for a, wr in acc:
             for j, b, bw in hist.setdefault(a[0], []):
-                same = ops[j]["q"] == op["q"]
                 if (wr or bw) and overlap(a, b):
-                    deps[j] = deps.get(j, False) or not same or op["q"] != "P"
-                elif same and a[0] in PSUM and op["q"] == "P":
-                    deps[j] = deps.get(j, False)
+                    deps[j] = deps.get(j, False) or ops[j]["q"] != "P" or op["q"] != "P"
+            if a[0] in PSUM and op["q"] == "P":
+                if last.get(a[0], i) != i:
+                    deps[last[a[0]]] = deps.get(last[a[0]], False)
+                last[a[0]] = i
         for a, wr in acc:
             h = hist[a[0]]
-            if a[0] in PSUM:
-                h[:] = [e for e in h if e[0] >= i - 400]
-            elif wr and a[3] == 1:
-                h[:] = [e for e in h if not (e[0] != i and e[1][1] >= a[1] and e[1][2] <= a[2])]
+            if wr:
+                h[:] = [e for e in h if e[0] == i or not covers(a, e[1])]
             h.append((i, a, wr))
         op["deps"] = deps
         op["banks"] = {a[0] for a, _ in acc if a[0] in PSUM}
 
 
-LOOK, BIG = 0.2, 0.45
-
-
-def schedule(ops, wake=0.25):
+def improve(ops, pred, seq, wake, rounds, width):
     n = len(ops)
+    q = [op["q"] for op in ops]
+    cost = [op["cost"] for op in ops]
+    lat = [op["lat"] for op in ops]
+    banks = [tuple(op["banks"]) for op in ops]
+    pr = [tuple(p.items()) for p in pred]
     succ = [[] for _ in range(n)]
-    npred = [0] * n
-    for i, op in enumerate(ops):
-        op["preds"] = set(op["deps"]) | ({op["after"]["i"]} if "after" in op else set())
-        npred[i] = len(op["preds"])
-        for j in op["preds"]:
+    for i in range(n):
+        for j in pred[i]:
             succ[j].append(i)
-    prio = [0.0] * n
+
+    def run(seq):
+        end, by = [0.0] * n, [None] * n
+        last, users = {}, {}
+        top, at = 0.0, 0
+        for i in seq:
+            s, w = 0.0, None
+            for j, d in pr[i]:
+                x = end[j] + d
+                if x > s:
+                    s, w = x, (j, 0)
+            qi = q[i]
+            if qi != "R":
+                j = last.get(qi)
+                if j is not None and end[j] > s:
+                    s, w = end[j], (j, 1)
+                last[qi] = i
+            for b in banks[i]:
+                u = users.setdefault(b, {})
+                for q2, j in u.items():
+                    if q2 != qi and end[j] + wake > s:
+                        s, w = end[j] + wake, (j, 1)
+                u[qi] = i
+            end[i] = s = s + cost[i]
+            by[i] = w
+            if s + lat[i] > top:
+                top, at = s + lat[i], i
+        return top, end, by, at
+
+    def moved(seq, pos, j, i, early):
+        part = seq[pos[j]:pos[i] + 1]
+        take = {i if early else j}
+        for k in (reversed(part) if early else part):
+            if k in take:
+                take.update(x for x in (pred[k] if early else succ[k]) if pos[j] <= pos[x] <= pos[i])
+        if (j if early else i) in take:
+            return None
+        a, b = [k for k in part if k in take], [k for k in part if k not in take]
+        return seq[:pos[j]] + (a + b if early else b + a) + seq[pos[i] + 1:]
+
+    def arcs(now, seq):
+        top, end, by, i = now
+        seq = sorted(seq, key=lambda k: end[k] - cost[k])
+        pos = [0] * n
+        for p, k in enumerate(seq):
+            pos[k] = p
+        pairs, block = [], []
+        while by[i] is not None:
+            j, res = by[i]
+            block = block[-2:] + [i] if res else []
+            pairs += [(j, k) for k in block]
+            i = j
+        return seq, pos, pairs
+
+    now = run(seq)
+    best = (now[0], seq)
+    seq, pos, pairs = arcs(now, seq)
+    x = 12345
+    for it in range(rounds):
+        x = (x * 1103515245 + 12345) % 2147483648
+        j, i = pairs[(x >> 8) % len(pairs)]
+        s2 = moved(seq, pos, j, i, (x >> 7) & 1)
+        if s2 is None:
+            continue
+        r = run(s2)
+        x = (x * 1103515245 + 12345) % 2147483648
+        if r[0] <= now[0] - width * (1 - it / rounds) * math.log((x + 1) / 2147483649.0):
+            now = r
+            seq, pos, pairs = arcs(now, s2)
+            if now[0] < best[0]:
+                best = (now[0], seq)
+    top, end, by, i = run(best[1])
+    return top, [end[k] - cost[k] for k in range(n)]
+
+
+def schedule(ops):
+    wake, same, al = CFG["wake"], CFG["same"], CFG["al"]
+    n = len(ops)
+    pred, succ = [{} for _ in range(n)], [{} for _ in range(n)]
+    wire, lastload = 0.0, {}
+    for i, op in enumerate(ops):
+        op["cost"], op["lat"] = cost(op)
+        if op.get("bulk"):
+            if op["bulk"] == "load":
+                wire += op["nbytes"] / CFG["bw"]
+                op["lat"] += wire
+            j = lastload.get(op["q"])
+            if j is not None:
+                pred[i][j] = ops[j]["nbytes"] / CFG["rbw"] if op["q"] == "R" else 0.0
+            if op["q"] == "R":
+                op["lat"] += op["nbytes"] / CFG["rbw"]
+            lastload[op["q"]] = i
+        for j in op["deps"]:
+            pred[i][j] = ops[j]["lat"] + (wake if ops[j]["q"] != op["q"] else same if op["q"] != "P" else 0.0)
+        if "after" in op:
+            pred[i][op["after"]["i"]] = 0.0
+        for j, w in pred[i].items():
+            succ[j][i] = w
+
+    def place(before, after, key, back):
+        start, taken = [0.0] * n, {}
+        left = [len(before[i]) for i in range(n)]
+        ready = [i for i in range(n) if not left[i]]
+        while ready:
+            i = min(ready, key=lambda k: (key[k], k))
+            ready.remove(i)
+            op = ops[i]
+            s = max([start[j] + ops[j]["cost"] + w for j, w in before[i].items()] + [op["lat"] if back else 0.0])
+            busy = [(x, y) for x, y in taken.get(op["q"], []) if y > s]
+            for b in op["banks"]:
+                busy += [(x - wake, y + wake) for x, y, q in taken.get(b, []) if q != op["q"] and y + wake > s]
+            for x, y in sorted(busy):
+                if x >= s + op["cost"]:
+                    break
+                s = max(s, y)
+            start[i] = s
+            if op["q"] != "R":
+                taken.setdefault(op["q"], []).append((s, s + op["cost"]))
+            for b in op["banks"]:
+                taken.setdefault(b, []).append((s, s + op["cost"], op["q"]))
+            for k in after[i]:
+                left[k] -= 1
+                if not left[k]:
+                    ready.append(k)
+        return start
+
+    key = [0.0] * n
     for i in range(n - 1, -1, -1):
-        b = max([prio[k] + (0.0 if ops[k]["q"] == ops[i]["q"] else wake) for k in succ[i]] + [0.0])
-        prio[i] = b + ops[i]["cost"] + ops[i].get("lat", 0.0)
-    free, count, done, last = {}, {}, [0.0] * n, {}
-    ready = {i for i in range(n) if npred[i] == 0}
-    while ready:
-        best = {}
-        for i in sorted(ready):
-            q = ops[i]["q"]
-            s = free.get(q, 0.0) if q != "R" else 0.0
-            for j in ops[i]["preds"]:
-                s = max(s, done[j] + (wake if ops[j]["q"] != q else 0.02))
-            for b in ops[i]["banks"]:
-                for q2, j in last.get(b, {}).items():
-                    if q2 != q:
-                        s = max(s, done[j] + wake)
-            best.setdefault(q, []).append((s, i))
-        pick = None
-        for q, lst in sorted(best.items()):
-            m = min(s for s, _ in lst)
-            s, i = max(((s, i) for s, i in lst if s <= m), key=lambda e: (prio[e[1]], -e[1]))
-            if ops[i]["cost"] > BIG:
-                s, i = max(((s, i) for s, i in lst if s <= m + LOOK), key=lambda e: (prio[e[1]], -e[1]))
-            if pick is None or (s, -prio[i]) < pick[:2]:
-                pick = (s, -prio[i], i, q)
-        s, _, i, q = pick
-        ready.remove(i)
+        key[i] = min([key[k] - w for k, w in succ[i].items()] + [-ops[i]["lat"]]) - ops[i]["cost"]
+    PLAN["way"] = -min(key)
+    bias = [(1 - al) * op["cost"] - CFG["boost"].get((op["outs"] or op["ins"])[0][0], 0.0) for op in ops]
+    key = [key[i] + bias[i] - (CFG["lead"] if ops[i]["tag"][:1] == "a" else 0.0) for i in range(n)]
+    best = None
+    for _ in range(CFG["passes"]):
+        start = place(pred, succ, key, False)
+        end = max(start[i] + ops[i]["cost"] + ops[i]["lat"] for i in range(n))
+        if best is None or end < best[0]:
+            best = (end, start)
+        back = place(succ, pred, [-start[i] - al * ops[i]["cost"] for i in range(n)], True)
+        key = [-back[i] - ops[i]["cost"] + bias[i] for i in range(n)]
+    best = improve(ops, pred, sorted(range(n), key=lambda i: (best[1][i], i)), wake, CFG["rounds"], CFG["width"])
+    last = {}
+    for i in sorted(range(n), key=lambda i: (best[1][i], i)):
+        ops[i]["pos"] = (best[1][i], i)
         for b in ops[i]["banks"]:
             users = last.setdefault(b, {})
             for q2, j in users.items():
-                if q2 != q:
+                if q2 != ops[i]["q"]:
                     ops[i]["deps"][j] = True
-            users[q] = i
-        free[q] = s + ops[i]["cost"]
-        done[i] = s + ops[i]["cost"] + ops[i].get("lat", 0.0)
-        count[q] = count.get(q, 0) + 1
-        ops[i]["pos"] = (s, count[q])
-        for k in succ[i]:
-            npred[k] -= 1
-            if npred[k] == 0:
-                ready.add(k)
+            users[ops[i]["q"]] = i
+    PLAN["end"] = best[0]
 
 
 PLAN = {}
 
 
 def plan():
-    if not PLAN:
+    if "ops" not in PLAN:
         ops = build()
         dependencies(ops)
         schedule(ops)
@@ -518,7 +696,7 @@ def rank_program(g, core, T, topo):
     if rank is None:
         return
     ops, seq = plan()
-    ctx = dict(g=g, V=g.vector, S=g.scalar, P=g.tensor, T=T, topo=topo, core=core, rank=rank)
+    ctx = dict(g=g, V=g.vector, S=g.scalar, P=g.tensor, Y=g.sync, T=T, topo=topo, core=core, rank=rank)
     queue = {"V": g.vector, "S": g.scalar, "P": g.tensor, "G": g, "Y": g.sync}
     default = {"V": "v", "S": "s", "P": "t"}
     total, val, known, clock = {}, {}, {q: {} for q in queue}, {}

@@ -5,9 +5,10 @@ ALU = AluOpType
 ACT = ActivationFunctionType
 ROUNDS, RANKS, H, A0, NV, REC = 4, 4, 128, 2048, 4096, 3584
 L, P = 128, 64
-CFG = dict(z=(1, 3), nv1=(64, 64), nv2=(128, 64), step=32, sstep=32, rec_s=(64, 32), rstep=32, eq=("SS", "VV"), e_v=(0, 0), delta=1,
-           ro1=(0, 0), ddw=(0, 1), lin_g=0, csplit=(0, 0), uu2=0,
-           lead=2.0, wake=0.2, same=0.08, bw=250e3, rbw=150e3, passes=6, al=0.5, boost={"ek0": 30.0, "w0": 30.0, "Z0": 30.0, "R0": 3.0}, rounds=15000, width=0.1)
+CFG = dict(gprep=(), gd1=1, gconv=2, z=(0, 3), nv1=(64, 64), nv2=(128, 64), step=32, sstep=32, rec_s=(64, 32), rstep=32, eq=("VS", "VV"), e_v=(0, 0), delta=1,
+           ro1=(0, 0), ddw=(0, 1), lin_g=0, csplit=(0, 0), uu2=1, fsplit=(0, 0), hm=0, zb=2, eb=(2, 2),
+           first=dict(c1a="VS", c2a="VS", c1b="VS", c2b="SV"),
+           lead=2.0, wake=0.2, same=0.08, bw=250e3, rbw=150e3, passes=6, al=0.5, boost={"ek0": 30.0, "w0": 30.0, "Z0": 30.0, "R0": 3.0}, rounds=8000, steady=25000, width=0.1, seed=1)
 B = 32768.0
 AT = [0]
 for _t in range(ROUNDS):
@@ -25,7 +26,9 @@ def declare(dtype, **bufs):
 declare(BF, pin=256, ones=512, blk=128, gsp=144, gz=144, gz2=144, gzn=144, ghalf=144, gb=144, gbh=144, g0=144, idb=128, nidb=128, ih=128, nih=128,
         ib=128, nib=128, i8=128, ni8=128, prm=512, bc=2048, rmask=1024, k8=128, nrb=128, k2048=128, QL=H, Z4=256)
 declare(F32, seg=128, half=128, cnt=2, whf=1, wlf=1, yv=256, yl=256, R4=256)
-declare(I32, rti=2048, exi=256, wti=1, kmi=1, whi=1, wli=1, cnti=1, par=1)
+declare(I32, rti=2048, exi=256, wti=1, kmi=1, whi=1, wli=1, cnti=1, par=1, ui=H, u=H, uu=H, su=H, hs=H, hh=H)
+declare(F16, ch=H)
+declare(U16, cq=H)
 OWN = {"rti", "exi", "pin", "wti", "kmi", "yv", "yl", "QL", "R4"}
 for _t in range(ROUNDS):
     declare(BF, **{"X%d" % _t: NV + 16, "Z%d" % _t: A0 + 256 * _t, "w%d" % _t: 256})
@@ -35,9 +38,9 @@ for _s in "ab":
     for _d, _names in ((BF, dict(pz=16 * L, prep=16 * L, zg=16 * P, re=16 * P, ad=16 * L, c1=16 * L, c2=16 * L, x1=16 * L, x2=16 * L,
                                  dl=P, gq=L, sb=L, eq=16 * P, cm=L, xr=16 * P, qs=16 * P)),
                        (F32, dict(tr=L, lin=L, d1=4 * L, rt1=P, bs=L, pq=L)),
-                       (I32, dict(ui=P, u=P, uu=P, su=P, hs=P, hh=P, mk=L, ai=8, nn=L, e2=L, sc=4 * L, fi=L)),
-                       (F16, dict(pm=L, ch=P, ah=8, f=L, F=L)),
-                       (U16, dict(cq=P, au=8, eu=L, e2u=L, ro=P, lu=8))):
+                       (I32, dict(mk=L, ai=8, nn=L, e2=L, sc=4 * L, fi=L)),
+                       (F16, dict(pm=L, ah=8, f=L, F=L)),
+                       (U16, dict(au=8, eu=L, e2u=L, ro=P, lu=8))):
         declare(_d, **{n + _s: w for n, w in _names.items()})
 SCRATCH, PLACE = {}, {}
 for _n, (_w, _s, _d) in LOGICAL.items():
@@ -163,6 +166,9 @@ def build():
     def aff(out, a, pattern, cmp, base, cm):
         add("G", ("aff", size(out)), [out], [a], lambda c: c["g"].affine_select(ap(c["T"], out), ap(c["T"], a), pattern, cmp, 0.0, base, cm), sem="gp")
 
+    def gcp(out, a):
+        aff(out, a, [[0, size(out)]], ALU.is_ge, 0, 0)
+
     def iota(out, pattern, base):
         add("G", ("aff", size(out)), [out], [], lambda c: c["g"].iota(ap(c["T"], out), pattern, base, 0, allow_small_or_imprecise_dtypes=True), sem="gp")
 
@@ -231,7 +237,7 @@ def build():
     fill(A("ek0", 256, 264), 0.0)
     ts(A("ek0", 256, 257), A("kmi"), 4096.0 - (0 if CFG["uu2"] else 64), ALU.subtract)
     fill(A("X0", NV, NV + 16), 0.0)
-    wide = [max(CFG["nv1"][i], CFG["nv2"][i], P * (CFG["z"][i] > 1)) for i in range(2)]
+    wide = [max(CFG["nv1"][i], CFG["nv2"][i], (L, 0, P, P)[CFG["z"][i]]) for i in range(2)]
     for i, s in enumerate("ab"):
         fill(A("pz" + s, 0, 16 * wide[i]), 0.0)
         fill(A("B%d" % (4 * i + 1), 0, 512, 4), -B)
@@ -240,13 +246,16 @@ def build():
             ts(A("pm" + s, P * par, P * par + P), A("pin", L * i + par, L * i + L, 2), -2.0, ALU.mult, -2048.0, ALU.add)
             ts(A("ek0", L * i + P * par, L * i + P * par + P), A("exi", L * i + par, L * i + L, 2), 4096.0, ALU.subtract)
     for k in range(0, A0, 512):
-        cp(A("R0", k, k + 512), A("rti", k, k + 512))
+        (gcp if k < 512 * CFG["gconv"] else cp)(A("R0", k, k + 512), A("rti", k, k + 512))
+
+    def columns(k):
+        send("tx%d" % k, -AT[k], [(A("X%d" % k, 0, REC), A("X0", 0, REC)), (A("X%d" % k, REC + H * k), A("X0", REC + H * k))])
 
     def tables(k):
-        send("tx%d" % k, -AT[k], [(A("X%d" % k, 0, REC), A("X0", 0, REC)), (A("X%d" % k, REC + H * k), A("X0", REC + H * k))])
         send("tw%d" % k, -AT[k], [(A("w%d" % k), A("w0")), (A("ek%d" % k), A("ek0"))])
         send("tz%d" % k, -AT[k], [(A("Z%d" % k, 0, A0), A("Z0"))])
         send("tr%d" % k, -AT[k], [(A("R%d" % k, 0, A0), A("R0"))])
+    columns(1)
     tables(1)
 
     for t in range(ROUNDS):
@@ -257,40 +266,52 @@ def build():
         for i, s in enumerate("ab"):
             tag[0] = "%s%d" % (s, t)
             a, b, c, d = ("B%d" % (4 * i + k) for k in range(4))
+            four = (c, d, "B%d" % (6 - 4 * i), "B%d" % (7 - 4 * i))
             nv1, nv2, zv = CFG["nv1"][i], CFG["nv2"][i], CFG["z"][i]
 
             def N(name, lo=0, hi=None, k=1, s=s):
                 return A(name + s, lo, hi, k)
-            o = A(a, 0, P)
             wh, wl = A("w%d" % t, 0, 128), A("w%d" % t, 128, 256)
-            mm([(o, wh, N("pm", 0, P), True, False), (o, wh, A("k2048", 0, P), False, False),
-                (o, wl, A("k2048", 0, P), False, False), (o, wl, N("pm", 0, P), False, True)])
-            U, KU = A(b, 1, 4 * P, 4), A(b, 3, 4 * P, 4)
-            cp(N("ui"), o)
-            ts(N("u"), N("ui"), 4095, ALU.bitwise_and)
-            ts(U, N("u"), 2048.0, ALU.subtract)
-            ts(KU, N("u"), A("ek%d" % t, 256, 257), ALU.mult)
-            tt(N("uu"), N("u"), N("u") if CFG["uu2"] else U, ALU.mult)
-            ts(N("su"), N("uu"), 5, ALU.arith_shift_right)
-            tt(N("hs"), N("su"), KU, ALU.add)
-            ts(N("hh"), N("hs"), 4095, ALU.bitwise_and)
-            ts(N("cq"), N("hh"), (8 + t) / 16.0, ALU.mult, -15.0 / 32, ALU.add)
-            ts(N("ch"), N("cq"), 2048.0, ALU.subtract)
+            j0, j1 = (0, H) if CFG["hm"] else (P * i, P * i + P)
+            hb = "B1" if CFG["hm"] else b
+            U, KU = A(hb, 4 * j0 + 1, 4 * j1, 4), A(hb, 4 * j0 + 3, 4 * j1, 4)
+            if not (CFG["hm"] and i):
+                for j in range(j0, j1, P):
+                    o, pe = A(a, j - j0, j - j0 + P), A("pm" + "ab"[j // P], 0, P)
+                    mm([(o, wh, pe, True, False), (o, wh, A("k2048", 0, P), False, False),
+                        (o, wl, A("k2048", 0, P), False, False), (o, wl, pe, False, True)])
+                ui, u, uu, su, hs, hh = (A(x, j0, j1) for x in ("ui", "u", "uu", "su", "hs", "hh"))
+                cp(ui, A(a, 0, j1 - j0))
+                ts(u, ui, 4095, ALU.bitwise_and)
+                ts(U, u, 2048.0, ALU.subtract)
+                ts(KU, u, A("ek%d" % t, 256, 257), ALU.mult)
+                tt(uu, u, u if CFG["uu2"] else U, ALU.mult)
+                ts(su, uu, 5, ALU.arith_shift_right)
+                tt(hs, su, KU, ALU.add)
+                ts(hh, hs, 4095, ALU.bitwise_and)
+                ts(A("cq", j0, j1), hh, (8 + t) / 16.0, ALU.mult, -15.0 / 32, ALU.add)
+                ts(A("ch", j0, j1), A("cq", j0, j1), 2048.0, ALU.subtract)
+            U, ch = A(hb, 4 * P * i + 1, 4 * P * i + 4 * P, 4), A("ch", P * i, P * i + P)
             mm([(A(c, 0, L), A("nih"), N("pm"), True, True)])
             for l0, l1 in steps(0, wide[i], P):
                 act(N("pz", 16 * l0, 16 * l1, 16), A(c, l0, l1), bias=-1024.0)
-                scan(N("prep", 16 * l0, 16 * l1), A("rmask", 0, 16 * (l1 - l0)), N("pz", 16 * l0, 16 * l1), ALU.mult, ALU.add)
+                if t and (i, l0 // P) in CFG["gprep"]:
+                    for k in range(16):
+                        gcp(N("prep", 16 * l0 + k, 16 * l1, 16), N("pz", 16 * l0, 16 * l1, 16))
+                else:
+                    scan(N("prep", 16 * l0, 16 * l1), A("rmask", 0, 16 * (l1 - l0)), N("pz", 16 * l0, 16 * l1), ALU.mult, ALU.add)
             act(N("pq"), A(c, 0, L), bias=255 + 2047.5 - 1024)
             if t < ROUNDS - 1:
                 mm([(A(d, par, L, 2), A("nih"), N("pm", P * par, P * par + P), True, True) for par in range(2)])
                 act(A(Zn[0], n + L * i, n + L * i + L), A(d, 0, L), bias=-1024.0)
-            act(N("d1", 3, 4 * L, 4), A("ek%d" % t, L * i, L * i + L))
+            (gcp if CFG["gd1"] else act)(N("d1", 3, 4 * L, 4), A("ek%d" % t, L * i, L * i + L))
+            ops[-1]["ins"].append(ch)
             key = A(a, 192, 320)
             ke, ko = A(a, 192, 256), A(a, 256, 320)
-            opening = [(key, A("idb"), A("k2048"), True, False), (ke, A("idb"), N("ch"), False, False), (ko, A("idb"), N("ch"), False, False)]
+            opening = [(key, A("idb"), A("k2048"), True, False), (ke, A("idb"), ch, False, False), (ko, A("idb"), ch, False, False)]
             if zv > 1:
                 for l0, l1 in steps(0, P, step):
-                    tt(N("zg", 16 * l0, 16 * l1), Ind(A(Z), N("cq", l0, l1)), N("prep", 16 * l0, 16 * l1), ALU.subtract)
+                    tt(N("zg", 16 * l0, 16 * l1), Ind(A(Z), A("cq", P * i + l0, P * i + l1)), N("prep", 16 * l0, 16 * l1), ALU.subtract)
                     if zv == 3:
                         act(N("re", 16 * l0, 16 * l1), N("zg", 16 * l0, 16 * l1), ACT.Abs)
                 if zv == 2:
@@ -312,11 +333,21 @@ def build():
                 mm([(ke, route("gz2" if zv == 2 else "gz", m), N("re", m, 16 * P, 16), False, False) for m in range(16)])
                 for k in range(2):
                     mm([(ko, route("gz", m), N("ad", P * m, P * m + P), False, m == 15) for m in range(8 * k, 8 * k + 8)])
+            elif zv == 0:
+                for l0, l1 in steps(0, P, 32):
+                    act(N("zg", 16 * l0, 16 * l1), Ind(A(Z), A("cq", P * i + l0, P * i + l1)))
+                for k in range(4):
+                    bk, x0 = four[k % CFG["zb"]], 512 * (k // 2) + 1024 * (k % 2)
+                    mm([(A(bk), A("nidb"), N("prep", x0, x0 + 512), True, False), (A(bk), A("idb"), N("zg", x0 % 1024, x0 % 1024 + 512), False, True)])
+                    act(N("ad", x0, x0 + 512), A(bk), ACT.Abs)
+                mm(opening)
+                for par in range(2):
+                    mm([((ke, ko)[par], route("gz", m), N("ad", 1024 * par + m, 1024 * par + 1024, 16), False, par == 1 and m == 15) for m in range(16)])
             else:
                 for l0, l1 in steps(0, P, sstep):
-                    act(N("zg", 16 * l0, 16 * l1), Ind(A(Z), N("cq", l0, l1)))
+                    act(N("zg", 16 * l0, 16 * l1), Ind(A(Z), A("cq", P * i + l0, P * i + l1)))
                 for k in range(4):
-                    bk, items = (c, d)[k % 2], []
+                    bk, items = four[k % CFG["zb"]], []
                     for m in range(4 * k, 4 * k + 4):
                         o0 = L * (m % 4)
                         items += [(A(bk, o0, o0 + L), A("ih"), N("pm"), True, False),
@@ -362,15 +393,16 @@ def build():
 
             def sums(out, cmp, nv, whole, half, first):
                 ns = L - nv
-                for lo, hi in steps(0, nv, P):
-                    o = out(lo, hi)
-                    f = first(o, lo, hi, False)
-                    mm(f + [(o, route(whole, k), N(cmp, 16 * lo + k, 16 * hi, 16), k == 0 and not f, k == 15) for k in range(16)])
-                if ns:
-                    o = out(nv, L)
-                    for j, (k0, k1) in enumerate(steps(0, 16, 512 // ns)):
-                        mm(first(o, nv, L, True) * (j == 0)
-                           + [(o, route(half, k), N(cmp, 16 * nv + ns * k, 16 * nv + ns * k + ns), False, k == 15) for k in range(k0, k1)])
+                for who in CFG["first"][cmp + s]:
+                    for lo, hi in steps(0, nv, P) * (who == "V"):
+                        o = out(lo, hi)
+                        f = first(o, lo, hi, False)
+                        mm(f + [(o, route(whole, k), N(cmp, 16 * lo + k, 16 * hi, 16), k == 0 and not f, k == 15) for k in range(16)])
+                    if ns and who == "S":
+                        o = out(nv, L)
+                        for j, (k0, k1) in enumerate(steps(0, 16, 512 // ns)):
+                            mm(first(o, nv, L, True) * (j == 0)
+                               + [(o, route(half, k), N(cmp, 16 * nv + ns * k, 16 * nv + ns * k + ns), False, k == 15) for k in range(k0, k1)])
             votes("eu", "c1", "x1", nv1)
             votes("e2u", "c2", "x2", nv2)
             sums(lambda lo, hi: A(a, 328 + lo, 328 + hi), "c1", nv1, "gsp", "ghalf",
@@ -385,6 +417,8 @@ def build():
                 ts(A("par"), A("cnti"), 1, ALU.bitwise_and)
                 ts(A("bo%d" % t), A("par"), -1.0, ALU.mult, -3.5, ALU.add)
                 send("ab%d" % t, AT[t] - AT[t + 1], [(A("bar%d" % (t + 1)), A("bo%d" % t))])
+                if t + 2 < ROUNDS:
+                    columns(t + 2)
             mm([(A(b, 2, 512, 4), A("nib"), N("gq"), True, True)])
             mm([(A(b, 3, 512, 4), A("ib"), N("sb"), True, True)])
             sums(lambda lo, hi: A(b, 4 * lo + 1, 4 * hi, 4), "c2", nv2, "gb", "gbh",
@@ -396,7 +430,7 @@ def build():
             fe, fo = N("f", 0, P), N("f", P, L)
             w = 16 // len(CFG["eq"][i])
             for h, who in enumerate(CFG["eq"][i]):
-                bk, items = (c, d)[h % 2], []
+                bk, items = four[h % CFG["eb"][i]], []
                 for k in range(w):
                     o = A(bk, k * P, k * P + P)
                     items += [(o, A("nidb"), fe, True, False), (o, A("bc", 128 * (w * h + k), 128 * (w * h + k) + 128), fo, False, True)]
@@ -431,12 +465,14 @@ def build():
                 scan(N("qs", 16 * l0, 16 * l1), A("rmask", 0, 16 * (l1 - l0)), N("xr", 16 * l0, 16 * l1), ALU.mult, ALU.max)
             cp(A(Xn, Qn[1] + P * i, Qn[1] + P * i + P), N("qs", 15, 16 * P, 16))
             ops[-1]["mark"] = True
-            mm([(A(d, 0, L), A("idb"), A("nrb"), True, False), (A(d, 0, L), A("i8"), N("cm"), False, True)])
-            act(N("bs"), A(d, 0, L), bias=REC - 2048.0 - 8192.0 + H * t + P * i)
-            mm([(key, A("idb"), N("f"), True, False), (key, A("ni8"), N("cm"), False, True)])
-            tt(N("F"), N("bs"), key, ALU.max)
-            mm([(A(a, 456, 464), route("g0", x), N("F", x, L, 16), x == 0, x == 15) for x in range(16)])
-            ts(N("lu"), A(a, 456, 464), 2048.0, ALU.add)
+            for l0, l1 in steps(0, L, P if CFG["fsplit"][i] and t < ROUNDS - 1 else L):
+                o, o2, o3 = A(d, l0, l1), A(a, 192 + l0, 192 + l1), A(a, 456 + l0 // 16, 456 + l1 // 16)
+                mm([(o, A("idb"), A("nrb", l0, l1), True, False), (o, A("i8"), N("cm", l0, l1), False, True)])
+                act(N("bs", l0, l1), o, bias=REC - 2048.0 - 8192.0 + H * t + P * i)
+                mm([(o2, A("idb"), N("f", l0, l1), True, False), (o2, A("ni8"), N("cm", l0, l1), False, True)])
+                tt(N("F", l0, l1), N("bs", l0, l1), o2, ALU.max)
+                mm([(o3, route("g0", x), N("F", l0 + x, l1, 16), x == 0, x == 15) for x in range(16)])
+                ts(N("lu", l0 // 16, l1 // 16), o3, 2048.0, ALU.add)
             mm([(A(d, par, L, 2), A("idb"), N("F", P * par, P * par + P), True, True) for par in range(2)])
             mine = A(Rn[0], Rn[1] + L * i, Rn[1] + L * i + L)
             act(mine, A(d, 0, L), bias=2048.0)
@@ -444,16 +480,19 @@ def build():
                 send("af" + s, AT[t + 1], [(A("FL%d" % t, L * i, L * i + L), mine)])
                 store("yr", 256 * t + L * i, A("FL%d" % t, L * i, L * i + L))
         tag[0] = "u%d" % t
-        if t < ROUNDS - 1:
-            send("af%d" % t, AT[t + 1], [(A("FL%d" % t), Rn)])
-            store("yr", 256 * t, A("FL%d" % t))
         for k in range(t + 2, ROUNDS):
             send("u%d%d" % (t, k), AT[t + 1] - AT[k], [(A("%s%d" % (x[0][0], k), x[1], x[2]), x) for x in (Zn, Rn, Qn)])
         if t + 2 < ROUNDS:
             tables(t + 2)
         if SLOT[ROUNDS] == t:
             send("aq", AT[t + 1] - AT[ROUNDS], [(A("QL"), Qn)])
-            cp(A(X, Qn[1], Qn[2]), A("QL"))
+        if t == ROUNDS - 1:
+            k = REC + H * SLOT[ROUNDS]
+            gcp(A(Xn, k, k + H), A("QL"))
+            ops[-1]["ins"].append(A("fa"))
+        if t < ROUNDS - 1:
+            send("af%d" % t, AT[t + 1], [(A("FL%d" % t), Rn)])
+            store("yr", 256 * t, A("FL%d" % t))
         for l0, l1, i in sorted((l0, l1, i) for i in range(2) for l0, l1 in steps(0, L, L if CFG["ddw"][i] or t == ROUNDS - 1 else P)):
             s = "ab"[i]
             tag[0] = "%s%d" % (s, t)
@@ -462,8 +501,8 @@ def build():
         tag[0] = s + "4"
         for par in range(2):
             ts(A("yv", L * i + par, L * i + L, 2), A("pm" + s, P * par, P * par + P), -0.5, ALU.mult, -1024.0, ALU.add)
-        send("ay" + s, AT[ROUNDS], [(A("yl", L * i, L * i + L), A("yv", L * i, L * i + L))])
-        store("yp", L * i, A("yl", L * i, L * i + L))
+    send("aya", AT[ROUNDS], [(A("yl"), A("yv"))])
+    store("yp", 0, A("yl"))
     return ops
 
 
@@ -515,25 +554,31 @@ def dependencies(ops):
         op["banks"] = {a[0] for a, _ in acc if a[0] in PSUM}
 
 
-def improve(ops, pred, seq, wake, rounds, width):
+def improve(ops, pred, seq, rounds, nxt):
     n = len(ops)
+    wake, width = CFG["wake"], CFG["width"] * (2 if nxt else 1)
     q = [op["q"] for op in ops]
     cost = [op["cost"] for op in ops]
-    lat = [op["lat"] for op in ops]
+    lat = [op["lat"] if not nxt else 0.0 if op.get("mark") else -1e9 for op in ops]
     banks = [tuple(op["banks"]) for op in ops]
-    pr = [tuple(p.items()) for p in pred]
+    back = {k: i for i, k in nxt.items()}
+    inside = set(seq) | set(back)
+    pr = [tuple((j, d) for j, d in p.items() if j in inside) for p in pred]
+    pred = [[j for j, d in p] for p in pr]
     succ = [[] for _ in range(n)]
-    for i in range(n):
+    for i in inside:
         for j in pred[i]:
             succ[j].append(i)
 
     def run(seq):
-        end, by = [0.0] * n, [None] * n
+        end, by = [None] * n, [None] * n
         last, users = {}, {}
         top, at = 0.0, 0
-        for i in seq:
+        for i in seq + [nxt[k] for k in seq if nxt]:
             s, w = 0.0, None
             for j, d in pr[i]:
+                if end[j] is None:
+                    return None
                 x = end[j] + d
                 if x > s:
                     s, w = x, (j, 0)
@@ -568,29 +613,31 @@ def improve(ops, pred, seq, wake, rounds, width):
 
     def arcs(now, seq):
         top, end, by, i = now
-        seq = sorted(seq, key=lambda k: end[k] - cost[k])
-        pos = [0] * n
+        timed = sorted(seq, key=lambda k: end[nxt.get(k, k)] - cost[k])
+        if not nxt or run(timed):
+            seq = timed
+        pos = [-1] * n
         for p, k in enumerate(seq):
             pos[k] = p
         pairs, block = [], []
         while by[i] is not None:
             j, res = by[i]
-            block = block[-2:] + [i] if res else []
-            pairs += [(j, k) for k in block]
+            block = block[-3:] + [i] if res else []
+            pairs += [(back.get(j, j), back.get(k, k)) for k in block if (j in back) == (k in back) and pos[back.get(j, j)] < pos[back.get(k, k)]]
             i = j
         return seq, pos, pairs
 
     now = run(seq)
     best = (now[0], seq)
     seq, pos, pairs = arcs(now, seq)
-    x = 12345
+    x = CFG["seed"]
     for it in range(rounds):
         x = (x * 1103515245 + 12345) % 2147483648
         j, i = pairs[(x >> 8) % len(pairs)]
         s2 = moved(seq, pos, j, i, (x >> 7) & 1)
-        if s2 is None:
+        r = s2 and run(s2)
+        if not r:
             continue
-        r = run(s2)
         x = (x * 1103515245 + 12345) % 2147483648
         if r[0] <= now[0] - width * (1 - it / rounds) * math.log((x + 1) / 2147483649.0):
             now = r
@@ -598,7 +645,37 @@ def improve(ops, pred, seq, wake, rounds, width):
             if now[0] < best[0]:
                 best = (now[0], seq)
     top, end, by, i = run(best[1])
-    return top, [end[k] - cost[k] for k in range(n)]
+    return top, [None if end[k] is None else end[k] - cost[k] for k in range(n)]
+
+
+def steady(ops, pred, succ, start):
+    n, seen, where = len(ops), {}, {}
+    for i, op in enumerate(ops):
+        a = (op["outs"] or op["ins"])[0]
+        t = int(op["tag"][-1]) if op["tag"] else -1
+        name = a[0] if a[0] in PSUM else a[0].rstrip("0123456789")
+        kind = (op["tag"][:1], op["q"], name, a[1] - {"X": H, "Z": 256, "R": 256}.get(name, 0) * t, len(op["outs"]))
+        seen[kind, t] = seen.get((kind, t), 0) + 1
+        op["kind"], op["round"] = kind + (seen[kind, t],), t
+        where[op["kind"], t] = i
+    edge = max(start[i] for i, op in enumerate(ops) if op.get("mark") and op["round"] == 0)
+    first = {}
+    for i in sorted(range(n), key=lambda i: (start[i], i)):
+        if start[i] > edge and ops[i]["round"] >= 0:
+            first.setdefault(ops[i]["kind"], i)
+    nxt = {i: where[k, ops[i]["round"] + 1] for k, i in first.items() if (k, ops[i]["round"] + 1) in where}
+    top, at = improve(ops, pred, list(nxt), CFG["steady"], nxt)
+    span = top - max(at[i] + ops[i]["cost"] for i in nxt if ops[i].get("mark"))
+    PLAN["span"] = span
+    key = [0.0] * n
+    for i in range(n - 1, -1, -1):
+        j = first.get(ops[i]["kind"])
+        if j in nxt:
+            key[i] = at[nxt[j]] + span * (ops[i]["round"] - ops[j]["round"])
+        else:
+            key[i] = min([key[k] - w for k, w in succ[i].items()] + [span * (ROUNDS + 1)]) - ops[i]["cost"]
+        key[i] -= CFG["boost"].get((ops[i]["outs"] or ops[i]["ins"])[0][0], 0.0) * (ops[i]["round"] < 0)
+    return key
 
 
 def schedule(ops):
@@ -666,7 +743,10 @@ def schedule(ops):
             best = (end, start)
         back = place(succ, pred, [-start[i] - al * ops[i]["cost"] for i in range(n)], True)
         key = [-back[i] - ops[i]["cost"] + bias[i] for i in range(n)]
-    best = improve(ops, pred, sorted(range(n), key=lambda i: (best[1][i], i)), wake, CFG["rounds"], CFG["width"])
+    start = best[1]
+    if CFG["steady"]:
+        start = place(pred, succ, steady(ops, pred, succ, start), False)
+    best = improve(ops, pred, sorted(range(n), key=lambda i: (start[i], i)), CFG["rounds"], {})
     last = {}
     for i in sorted(range(n), key=lambda i: (best[1][i], i)):
         ops[i]["pos"] = (best[1][i], i)

@@ -5,10 +5,11 @@ ALU = AluOpType
 ACT = ActivationFunctionType
 ROUNDS, RANKS, H, A0, NV, REC = 4, 4, 128, 2048, 4096, 3584
 L, P = 128, 64
-CFG = dict(gprep=(), gd1=1, gconv=2, z=(0, 3), nv1=(64, 64), nv2=(128, 64), step=32, sstep=32, rec_s=(64, 32), rstep=32, eq=("VS", "VV"), e_v=(0, 0), delta=1,
-           ro1=(0, 0), ddw=(0, 1), lin_g=0, csplit=(0, 0), uu2=1, fsplit=(0, 0), hm=0, zb=2, eb=(2, 2),
-           first=dict(c1a="VS", c2a="VS", c1b="VS", c2b="SV"),
-           lead=2.0, wake=0.2, same=0.08, bw=250e3, rbw=150e3, passes=6, al=0.5, boost={"ek0": 30.0, "w0": 30.0, "Z0": 30.0, "R0": 3.0}, rounds=8000, steady=25000, width=0.1, seed=1)
+CFG = dict(p1=1, g0=0, w=3, ge2u=(0, 0), gq=1, gprep=((1, 1),), gd1=1, gconv=2, gch=(0, 0), sbar=1, glu=1, lv=(0, 1),
+           z=(0, 3), nv1=(64, 128), nv2=(64, 64), step=32, sstep=32, rec_s=(64, 32), rstep=32, eq=("VV", "VVVV"), e_v=(0, 3), delta=1,
+           ro1=(1, 0), ddw=(0, 1), lin_g=0, csplit=(0, 0), uu2=1, fsplit=(0, 0), tri=(1, 1), eb=(2, 3),
+           first=dict(c1a="VS", c2a="SV", c1b="SV", c2b="SV"),
+           lead=2.0, wake=0.25, same=0.1, send=1.2, f=1.2, bw=250e3, rbw=150e3, passes=6, al=0.5, boost={"ek0": 30.0, "w0": 30.0, "Z0": 30.0, "R0": 30.0, "X0": 30.0}, rounds=25000, steady=25000, starts=2, width=0.1, seed=13)
 B = 32768.0
 AT = [0]
 for _t in range(ROUNDS):
@@ -24,8 +25,9 @@ def declare(dtype, **bufs):
 
 
 declare(BF, pin=256, ones=512, blk=128, gsp=144, gz=144, gz2=144, gzn=144, ghalf=144, gb=144, gbh=144, g0=144, idb=128, nidb=128, ih=128, nih=128,
-        ib=128, nib=128, i8=128, ni8=128, prm=512, bc=2048, rmask=1024, k8=128, nrb=128, k2048=128, QL=H, Z4=256)
-declare(F32, seg=128, half=128, cnt=2, whf=1, wlf=1, yv=256, yl=256, R4=256)
+        ib=128, nib=128, i8=128, ni8=128, prm=512, bc=2048, rmask=1024, k8=256, y0a=3 * L, y0b=3 * L, nrb=128, k2048=128, QL=H, Z4=256)
+declare(BF, zero=128)
+declare(F32, idf=128, cf=H, lf=8, cj=2, c0=1, c1=1, c2=1, c3=1, seg=128, half=128, cnt=2, whf=1, wlf=1, yv=256, yl=256, R4=256)
 declare(I32, rti=2048, exi=256, wti=1, kmi=1, whi=1, wli=1, cnti=1, par=1, ui=H, u=H, uu=H, su=H, hs=H, hh=H)
 declare(F16, ch=H)
 declare(U16, cq=H)
@@ -36,10 +38,10 @@ for _t in range(ROUNDS):
     OWN |= {n + str(_t) for n in ("X", "Z", "w", "R", "ek", "bar", "bo", "FL")}
 for _s in "ab":
     for _d, _names in ((BF, dict(pz=16 * L, prep=16 * L, zg=16 * P, re=16 * P, ad=16 * L, c1=16 * L, c2=16 * L, x1=16 * L, x2=16 * L,
-                                 dl=P, gq=L, sb=L, eq=16 * P, cm=L, xr=16 * P, qs=16 * P)),
-                       (F32, dict(tr=L, lin=L, d1=4 * L, rt1=P, bs=L, pq=L)),
+                                 dl=P, r9=L, gq=L, sb=L, eq=16 * P, cm=L, xr=16 * P, qs=16 * P)),
+                       (F32, dict(e=L, tr=L, lin=L, d1=4 * L, rt1=P, bs=L, pq=L)),
                        (I32, dict(mk=L, ai=8, nn=L, e2=L, sc=4 * L, fi=L)),
-                       (F16, dict(pm=L, ah=8, f=L, F=L)),
+                       (F16, dict(uh=P, pm=L, ah=8, f=L, F=L, Ft=L)),
                        (U16, dict(au=8, eu=L, e2u=L, ro=P, lu=8))):
         declare(_d, **{n + _s: w for n, w in _names.items()})
 SCRATCH, PLACE = {}, {}
@@ -61,7 +63,7 @@ SEMAPHORES = (["v", "s", "t", "gp", "out", "sent", "aq", "aya", "ayb", "afa", "a
 WIDTH = {n: s[1][1] for n, s in LOGICAL.items()}
 PSUM = {n for n, s in LOGICAL.items() if s[0] == "psum"}
 TWO = {n for n, s in LOGICAL.items() if s[2] in (BF, F16, U16)}
-CYC, PECYC, GATHER = 0.83e-3, 0.42e-3, 1.56
+CYC, PECYC, GATHER = 0.83e-3, 0.42e-3, 1.75
 
 
 def A(name, lo=0, hi=None, st=1):
@@ -150,18 +152,19 @@ def build():
             return c["S"].activation(ap(c["T"], out), ap(c["T"], a), func, bias=b, scale=scale, accum_out=x)
         add("S", ("gather" if a[0] == "@" else "plain", size(out)), [out] + ([accum] if accum is not None else []), [a, bias], fn)
 
-    def mm(items, weight=1):
+    def mm(items, group=None):
         def fn(c):
             m = None
-            for o, l, r, s, e in items:
-                m = c["P"].matmul(ap(c["T"], o), ap(c["T"], l), ap(c["T"], r), s, e)
+            for k, (o, l, r, s, e) in enumerate(items):
+                m = c["P"].matmul(ap(c["T"], o), ap(c["T"], l), ap(c["T"], r), s, e or (k == len(items) - 1 and "stop" in op))
             return m
         outs, ins = [], []
         for o, l, r, s, e in items:
             for x, d in ((o, outs), (l, ins), (r, ins)):
                 if x not in d:
                     d.append(x)
-        add("P", ("pe", weight * sum(max(64, size(i[2])) for i in items)), outs, ins, fn)
+        op = add("P", ("pe", sum(max(64, size(i[2])) * (1 if i[2][0] in TWO else 4) for i in items)), outs, ins, fn,
+                 group=group and (group, tag[0]), opens=items[0][3])
 
     def aff(out, a, pattern, cmp, base, cm):
         add("G", ("aff", size(out)), [out], [a], lambda c: c["g"].affine_select(ap(c["T"], out), ap(c["T"], a), pattern, cmp, 0.0, base, cm), sem="gp")
@@ -195,7 +198,7 @@ def build():
     def steps(lo, hi, step):
         return [(x, min(hi, x + step)) for x in range(lo, hi, step)]
 
-    step, sstep = CFG["step"], CFG["sstep"]
+    step, sstep, W = CFG["step"], CFG["sstep"], CFG["w"]
     load("Y", A("pin"), "p0"); load("S", A("wti"), "wt"); load("S", A("kmi"), "km")
     load("Y", A("Z0"), "zp"); load("Y", A("rti"), "rt"); load("Y", A("X0", 0, NV), "ax"); load("Y", A("exi"), "ex")
     fill(A("ones"), 1.0)
@@ -211,21 +214,26 @@ def build():
     if 2 in CFG["z"]:
         act(A("gz2"), A("gsp"), scale=8192.0)
         act(A("gzn"), A("gsp"), scale=-4096.0)
+    if any(CFG["gch"]):
+        act(A("idf"), A("idb"))
+        act(A("zero"), A("idb"), scale=0.0)
     fill(A("k2048"), 2048.0)
-    fill(A("seg"), 0.0)
-    fill(A("seg", 0, 128, 16), 1e9)
+    act(A("seg"), A("ones", 0, 128), scale=0.0)
+    act(A("seg", 0, 128, 16), A("ones", 0, 8), scale=1e9)
     for qh in range(2):
         for gp in range(2):
             k = 128 * (2 * qh + gp)
             aff(A("prm", k, k + 128), A("ones", 0, 128), [[-32, 4], [-1000, 2], [-1, 16]], ALU.is_equal, 1000 * gp - 16 * qh, 1)
-    fill(A("k8"), 8.0)
-    fill(A("bar0"), -3.5)
-    fill(A("half"), 0.5)
+    act(A("k8", 0, L), A("ones", 0, L), scale=0.0)
+    act(A("k8", L), A("ones", 0, L), scale=8.0)
+    act(A("bar0"), A("ones", 0, 1), scale=-3.5)
+    act(A("half"), A("ones", 0, 128), scale=0.5)
     for k in range(0, 16, 4):
         aff(A("bc", 128 * k, 128 * k + 512), A("ones"), [[-1, 4], [-16, 8], [0, 16]], ALU.is_equal, -k, 1)
-    fill(A("rmask"), 1.0)
-    fill(A("rmask", 0, 1024, 16), 0.0)
-    fill(A("g0"), 0.0)
+    for k in range(0, 1024, 512):
+        act(A("rmask", k, k + 512), A("ones"))
+    act(A("rmask", 0, 1024, 16), A("ones", 0, 64), scale=0.0)
+    act(A("g0"), A("ones", 0, 144), scale=0.0)
     aff(A("g0", 15, 143, 16), A("ones", 0, 8), [[-16, 8]], ALU.is_equal, 0, 1)
     iota(A("nrb"), [[0, 2], [1, P]], 0)
     ts(A("whi"), A("wti"), 6, ALU.logical_shift_right)
@@ -239,12 +247,16 @@ def build():
     fill(A("X0", NV, NV + 16), 0.0)
     wide = [max(CFG["nv1"][i], CFG["nv2"][i], (L, 0, P, P)[CFG["z"][i]]) for i in range(2)]
     for i, s in enumerate("ab"):
-        fill(A("pz" + s, 0, 16 * wide[i]), 0.0)
-        fill(A("B%d" % (4 * i + 1), 0, 512, 4), -B)
-        fill(A("d1" + s, 1, 4 * L, 4), -B)
+        for l0, l1 in steps(0, wide[i], P):
+            if not (CFG["g0"] and (i, l0 // P) in CFG["gprep"]):
+                fill(A("pz" + s, 16 * l0, 16 * l1), 0.0)
+        act(A("y0" + s), A("ones", 0, W * L), scale=0.0)
+        act(A("y0" + s, 0, W * L, W), A("ones", 0, L))
+        act(A("y0" + s, 1, W * CFG["nv2"][i], W), A("ones", 0, CFG["nv2"][i]), scale=8.0)
         for par in range(2):
             ts(A("pm" + s, P * par, P * par + P), A("pin", L * i + par, L * i + L, 2), -2.0, ALU.mult, -2048.0, ALU.add)
-            ts(A("ek0", L * i + P * par, L * i + P * par + P), A("exi", L * i + par, L * i + L, 2), 4096.0, ALU.subtract)
+            gcp(A("ek0", L * i + P * par, L * i + P * par + P), A("exi", L * i + par, L * i + L, 2))
+    act(A("ek0", 0, 256), A("ek0", 0, 256), bias=-8192.0)
     for k in range(0, A0, 512):
         (gcp if k < 512 * CFG["gconv"] else cp)(A("R0", k, k + 512), A("rti", k, k + 512))
 
@@ -254,7 +266,9 @@ def build():
     def tables(k):
         send("tw%d" % k, -AT[k], [(A("w%d" % k), A("w0")), (A("ek%d" % k), A("ek0"))])
         send("tz%d" % k, -AT[k], [(A("Z%d" % k, 0, A0), A("Z0"))])
-        send("tr%d" % k, -AT[k], [(A("R%d" % k, 0, A0), A("R0"))])
+        if k > 1:
+            send("tr%d" % k, -AT[k], [(A("R%d" % k, 0, A0), A("R0"))])
+    send("tr1", -AT[1], [(A("R1", 0, A0), A("R0"))])
     columns(1)
     tables(1)
 
@@ -266,36 +280,37 @@ def build():
         for i, s in enumerate("ab"):
             tag[0] = "%s%d" % (s, t)
             a, b, c, d = ("B%d" % (4 * i + k) for k in range(4))
-            four = (c, d, "B%d" % (6 - 4 * i), "B%d" % (7 - 4 * i))
+            four = (c, d, b)
             nv1, nv2, zv = CFG["nv1"][i], CFG["nv2"][i], CFG["z"][i]
 
             def N(name, lo=0, hi=None, k=1, s=s):
                 return A(name + s, lo, hi, k)
             wh, wl = A("w%d" % t, 0, 128), A("w%d" % t, 128, 256)
-            j0, j1 = (0, H) if CFG["hm"] else (P * i, P * i + P)
-            hb = "B1" if CFG["hm"] else b
-            U, KU = A(hb, 4 * j0 + 1, 4 * j1, 4), A(hb, 4 * j0 + 3, 4 * j1, 4)
-            if not (CFG["hm"] and i):
-                for j in range(j0, j1, P):
-                    o, pe = A(a, j - j0, j - j0 + P), A("pm" + "ab"[j // P], 0, P)
-                    mm([(o, wh, pe, True, False), (o, wh, A("k2048", 0, P), False, False),
-                        (o, wl, A("k2048", 0, P), False, False), (o, wl, pe, False, True)])
-                ui, u, uu, su, hs, hh = (A(x, j0, j1) for x in ("ui", "u", "uu", "su", "hs", "hh"))
-                cp(ui, A(a, 0, j1 - j0))
-                ts(u, ui, 4095, ALU.bitwise_and)
-                ts(U, u, 2048.0, ALU.subtract)
-                ts(KU, u, A("ek%d" % t, 256, 257), ALU.mult)
-                tt(uu, u, u if CFG["uu2"] else U, ALU.mult)
-                ts(su, uu, 5, ALU.arith_shift_right)
-                tt(hs, su, KU, ALU.add)
-                ts(hh, hs, 4095, ALU.bitwise_and)
-                ts(A("cq", j0, j1), hh, (8 + t) / 16.0, ALU.mult, -15.0 / 32, ALU.add)
-                ts(A("ch", j0, j1), A("cq", j0, j1), 2048.0, ALU.subtract)
-            U, ch = A(hb, 4 * P * i + 1, 4 * P * i + 4 * P, 4), A("ch", P * i, P * i + P)
+            tri = CFG["tri"][i]
+            U, KU = A(a, 64, 128), A(a, 128, 192)
+            o, pe = A(a, 0, P), N("pm", 0, P)
+            mm([(o, wh, pe, True, False), (o, wh, A("k2048", 0, P), False, False),
+                (o, wl, A("k2048", 0, P), False, False), (o, wl, pe, False, True)])
+            ui, u, uu, su, hs, hh, cq, ch = (A(x, P * i, P * i + P) for x in ("ui", "u", "uu", "su", "hs", "hh", "cq", "ch"))
+            cp(ui, o)
+            ts(u, ui, 4095, ALU.bitwise_and)
+            ts(N("uh") if CFG["p1"] else U, u, 2048.0, ALU.subtract)
+            ts(KU, u, A("ek%d" % t, 256, 257), ALU.mult)
+            tt(uu, u, u if CFG["uu2"] else U, ALU.mult)
+            ts(su, uu, 5, ALU.arith_shift_right)
+            tt(hs, su, KU, ALU.add)
+            if CFG["p1"]:
+                mm([(x, A("idb"), N("uh"), True, True) for x in (U, KU)])
+            ts(hh, hs, 4095, ALU.bitwise_and)
+            ts(cq, hh, (8 + t) / 16.0, ALU.mult, -15.0 / 32, ALU.add)
+            if CFG["gch"][i]:
+                gcp(A("cf", P * i, P * i + P), cq)
+            else:
+                ts(ch, cq, 2048.0, ALU.subtract)
             mm([(A(c, 0, L), A("nih"), N("pm"), True, True)])
             for l0, l1 in steps(0, wide[i], P):
                 act(N("pz", 16 * l0, 16 * l1, 16), A(c, l0, l1), bias=-1024.0)
-                if t and (i, l0 // P) in CFG["gprep"]:
+                if (t or CFG["g0"]) and (i, l0 // P) in CFG["gprep"]:
                     for k in range(16):
                         gcp(N("prep", 16 * l0 + k, 16 * l1, 16), N("pz", 16 * l0, 16 * l1, 16))
                 else:
@@ -304,11 +319,14 @@ def build():
             if t < ROUNDS - 1:
                 mm([(A(d, par, L, 2), A("nih"), N("pm", P * par, P * par + P), True, True) for par in range(2)])
                 act(A(Zn[0], n + L * i, n + L * i + L), A(d, 0, L), bias=-1024.0)
-            (gcp if CFG["gd1"] else act)(N("d1", 3, 4 * L, 4), A("ek%d" % t, L * i, L * i + L))
-            ops[-1]["ins"].append(ch)
+            (gcp if CFG["gd1"] else act)(N("d1", W - 1, W * L, W), A("ek%d" % t, L * i, L * i + L))
+            ops[-1]["ins"].append(cq)
             key = A(a, 192, 320)
             ke, ko = A(a, 192, 256), A(a, 256, 320)
             opening = [(key, A("idb"), A("k2048"), True, False), (ke, A("idb"), ch, False, False), (ko, A("idb"), ch, False, False)]
+            if CFG["gch"][i]:
+                cf = A("cf", P * i, P * i + P)
+                opening = [(key, A("idb"), A("zero"), True, False), (ke, A("idf"), cf, False, False), (ko, A("idf"), cf, False, False)]
             if zv > 1:
                 for l0, l1 in steps(0, P, step):
                     tt(N("zg", 16 * l0, 16 * l1), Ind(A(Z), A("cq", P * i + l0, P * i + l1)), N("prep", 16 * l0, 16 * l1), ALU.subtract)
@@ -327,27 +345,34 @@ def build():
                         items += [(o, A("idb"), N("zg", m, 16 * P, 16), False, True)]
                     mm(items)
                     act(N("ad", 512 * k, 512 * k + 512), A(bk), ACT.Abs)
-                mm(opening)
+                mm(opening[:1], "key")
+                mm(opening[1:], "key")
                 if zv == 2:
-                    mm([(ke, route("gzn", m), N("zg", m, 16 * P, 16), False, False) for m in range(16)])
-                mm([(ke, route("gz2" if zv == 2 else "gz", m), N("re", m, 16 * P, 16), False, False) for m in range(16)])
+                    mm([(ke, route("gzn", m), N("zg", m, 16 * P, 16), False, False) for m in range(16)], "key")
+                mm([(ke, route("gz2" if zv == 2 else "gz", m), N("re", m, 16 * P, 16), False, False) for m in range(16)], "key")
                 for k in range(2):
-                    mm([(ko, route("gz", m), N("ad", P * m, P * m + P), False, m == 15) for m in range(8 * k, 8 * k + 8)])
+                    mm([(ko, route("gz", m), N("ad", P * m, P * m + P), False, False) for m in range(8 * k, 8 * k + 8)], "key")
             elif zv == 0:
                 for l0, l1 in steps(0, P, 32):
                     act(N("zg", 16 * l0, 16 * l1), Ind(A(Z), A("cq", P * i + l0, P * i + l1)))
                 for k in range(4):
-                    bk, x0 = four[k % CFG["zb"]], 512 * (k // 2) + 1024 * (k % 2)
+                    bk, x0 = four[k % (2 + tri)], 512 * (k // 2) + 1024 * (k % 2)
+                    if (i, k % 2) in CFG["gprep"]:
+                        mm([(A(bk), A("idb"), N("zg", x0 % 1024, x0 % 1024 + 512), True, False)]
+                           + [(A(bk, m, 512, 16), A("ih"), N("pm", x0 // 16, x0 // 16 + 32), False, m == 15) for m in range(16)])
+                        act(N("ad", x0, x0 + 512), A(bk), ACT.Abs, bias=1024.0)
+                        continue
                     mm([(A(bk), A("nidb"), N("prep", x0, x0 + 512), True, False), (A(bk), A("idb"), N("zg", x0 % 1024, x0 % 1024 + 512), False, True)])
                     act(N("ad", x0, x0 + 512), A(bk), ACT.Abs)
-                mm(opening)
+                mm(opening[:1], "key")
+                mm(opening[1:], "key")
                 for par in range(2):
-                    mm([((ke, ko)[par], route("gz", m), N("ad", 1024 * par + m, 1024 * par + 1024, 16), False, par == 1 and m == 15) for m in range(16)])
+                    mm([((ke, ko)[par], route("gz", m), N("ad", 1024 * par + m, 1024 * par + 1024, 16), False, False) for m in range(16)], "key")
             else:
                 for l0, l1 in steps(0, P, sstep):
                     act(N("zg", 16 * l0, 16 * l1), Ind(A(Z), A("cq", P * i + l0, P * i + l1)))
                 for k in range(4):
-                    bk, items = four[k % CFG["zb"]], []
+                    bk, items = four[k % (2 + tri)], []
                     for m in range(4 * k, 4 * k + 4):
                         o0 = L * (m % 4)
                         items += [(A(bk, o0, o0 + L), A("ih"), N("pm"), True, False),
@@ -365,16 +390,19 @@ def build():
             mm([(A(a, 320 + qh, 328, 2), A("prm", 128 * (2 * qh + gp), 128 * (2 * qh + gp) + 128), N("ah", gp, 8, 2), gp == 0, gp == 1)
                 for qh in range(2) for gp in range(2)])
             ts(N("au"), A(a, 320, 328), 2048.0, ALU.add)
-            e = N("d1", 2, 4 * L, 4)
+            e = N("e")
             (cp if CFG["e_v"][i] == 1 else act)(e, Ind(A(R), N("au")))
-            cp(N("eu"), e if CFG["e_v"][i] else Ind(A(R), N("au")))
+            (gcp if CFG["e_v"][i] == 3 else cp)(N("eu"), e if CFG["e_v"][i] else Ind(A(R), N("au")))
             act(N("lin"), Ind(A(R), N("au")) if CFG["lin_g"] else e, bias=2464.0 * t - 131072.0, scale=2080.0)
-            for par in range(2):
-                tt(A(b, 2 + 4 * P * par, 4 * P * (par + 1), 4), N("d1", 2 + 4 * P * par, 4 * P * (par + 1), 4), U, ALU.mult)
-            tt(N("nn"), N("lin"), A(b, 2, 512, 4), ALU.add)
+            if CFG["p1"]:
+                tt(key, e, A(a, 64, 192), ALU.mult)
+            for par in range(2 * (1 - CFG["p1"])):
+                tt((ke, ko)[par], N("e", P * par, P * par + P), U, ALU.mult)
+            tt(N("nn"), N("lin"), key, ALU.add)
             ts(N("e2"), N("nn"), 5, ALU.arith_shift_right, 4095, ALU.bitwise_and)
-            cp(N("e2u"), N("e2"))
-            ts(N("d1", 0, 4 * L, 4), N("e2"), 4096.0, ALU.add)
+            (gcp if CFG["ge2u"][i] else cp)(N("e2u"), N("e2"))
+            gcp(N("d1", 0, W * L, W), N("e2"))
+            act(N("d1", W - 2, W * L, W), e, bias=-4096.0)
 
             def votes(off, cmp, raw, nv):
                 ns = L - nv
@@ -382,7 +410,7 @@ def build():
                     for l0, l1 in steps(0, ns, sstep):
                         act(N(raw, 16 * l0, 16 * l1), Ind(A(X, 0, NV), N(off, nv + l0, nv + l1)))
                     for j, (k0, k1) in enumerate(steps(0, 16, 512 // ns)):
-                        bk, items = (c, d)[j % 2], []
+                        bk, items = ((d, b) if tri and raw == "x1" else (c, d))[j % 2], []
                         for k in range(k0, k1):
                             o = A(bk, ns * (k - k0), ns * (k - k0 + 1))
                             items += [(o, A("ih"), N("pm", nv, L), True, False), (o, A("idb"), N(raw, k, 16 * ns, 16), False, True)]
@@ -391,41 +419,44 @@ def build():
                 for l0, l1 in steps(0, nv, step):
                     tt(N(cmp, 16 * l0, 16 * l1), Ind(A(X, 0, NV), N(off, l0, l1)), N("prep", 16 * l0, 16 * l1), ALU.is_ge)
 
-            def sums(out, cmp, nv, whole, half, first):
+            def sums(out, cmp, nv, whole, half):
                 ns = L - nv
-                for who in CFG["first"][cmp + s]:
-                    for lo, hi in steps(0, nv, P) * (who == "V"):
-                        o = out(lo, hi)
-                        f = first(o, lo, hi, False)
-                        mm(f + [(o, route(whole, k), N(cmp, 16 * lo + k, 16 * hi, 16), k == 0 and not f, k == 15) for k in range(16)])
-                    if ns and who == "S":
-                        o = out(nv, L)
-                        for j, (k0, k1) in enumerate(steps(0, 16, 512 // ns)):
-                            mm(first(o, nv, L, True) * (j == 0)
-                               + [(o, route(half, k), N(cmp, 16 * nv + ns * k, 16 * nv + ns * k + ns), False, k == 15) for k in range(k0, k1)])
+                for lo, hi in steps(0, nv, P):
+                    mm([(out(lo, hi), route(whole, k), N(cmp, 16 * lo + k, 16 * hi, 16), False, False) for k in range(16)], cmp)
+                for k0, k1 in steps(0, 16, 512 // ns) if ns else ():
+                    mm([(out(nv, L), route(half, k), N(cmp, 16 * nv + ns * k, 16 * nv + ns * k + ns), False, False) for k in range(k0, k1)], cmp)
             votes("eu", "c1", "x1", nv1)
             votes("e2u", "c2", "x2", nv2)
-            sums(lambda lo, hi: A(a, 328 + lo, 328 + hi), "c1", nv1, "gsp", "ghalf",
-                 lambda o, lo, hi, sc: [(o, A("idb"), A("k8", lo, hi), True, False)] if sc else [])
             g1 = A(a, 328, 456)
+            mm([(g1, A("idb"), A("k8", L - nv1, 2 * L - nv1), True, False)], "c1")
+            sums(lambda lo, hi: A(a, 328 + lo, 328 + hi), "c1", nv1, "gsp", "ghalf")
             act(N("gq"), g1, bias=-8.5)
+            if W == 3:
+                act(N("r9"), N("gq"), ACT.Relu, scale=64.0)
             act(N("sb"), g1, ACT.Sign, bias=A("bar%d" % t), accum=A("cnt", i, i + 1))
             if i and t < ROUNDS - 1:
-                o = A(a, 464, 465)
-                mm([(o, A("half"), A("cnt", 0, 1), True, False), (o, A("half"), A("cnt", 1, 2), False, True)], 4)
-                cp(A("cnti"), o)
-                ts(A("par"), A("cnti"), 1, ALU.bitwise_and)
-                ts(A("bo%d" % t), A("par"), -1.0, ALU.mult, -3.5, ALU.add)
+                o = A(a, 464, 466)
+                mm([(o, A("half"), A("cnt"), True, True)])
+                if CFG["sbar"]:
+                    act(A("cj"), o, scale=-1.0, accum=A("c0"))
+                    act(A("c1"), A("c0"), bias=12582912.0, scale=-0.5)
+                    act(A("c2"), A("c1"), bias=-12582912.0)
+                    act(A("c3"), A("c2"), ACT.Abs, bias=A("c0"), scale=2.0)
+                    act(A("bo%d" % t), A("c3"), bias=-3.5, scale=-1.0)
+                else:
+                    cp(A("cnti"), o)
+                    ts(A("par"), A("cnti"), 1, ALU.bitwise_and)
+                    ts(A("bo%d" % t), A("par"), -1.0, ALU.mult, -3.5, ALU.add)
                 send("ab%d" % t, AT[t] - AT[t + 1], [(A("bar%d" % (t + 1)), A("bo%d" % t))])
                 if t + 2 < ROUNDS:
                     columns(t + 2)
-            mm([(A(b, 2, 512, 4), A("nib"), N("gq"), True, True)])
-            mm([(A(b, 3, 512, 4), A("ib"), N("sb"), True, True)])
-            sums(lambda lo, hi: A(b, 4 * lo + 1, 4 * hi, 4), "c2", nv2, "gb", "gbh",
-                 lambda o, lo, hi, sc: [(o, A("nib"), N("gq", lo, hi), True, False)] + ([] if sc else [(o, A("nib"), A("k8", lo, hi), False, False)]))
+            mm([(A(b, 0, W * L), A("nib"), N("y0"), True, False)], "c2")
+            mm([(A(b, 2, W * L, W), A("ib"), N("sb"), False, False)], "c2")
+            mm([(A(b, 1, W * L, W), A("nib"), N(x), False, False) for x in ("gq", "r9")], "c2")
+            sums(lambda lo, hi: A(b, W * lo + 1, W * hi, W), "c2", nv2, "gb", "gbh")
             for l0, l1 in steps(0, L, P if CFG["csplit"][i] else L):
-                scan(N("sc", 4 * l0, 4 * l1), A(b, 4 * l0, 4 * l1), N("d1", 4 * l0, 4 * l1), ALU.min, ALU.max)
-                ts(N("fi", l0, l1), N("sc", 4 * l0 + 3, 4 * l1, 4), 4095, ALU.bitwise_and)
+                scan(N("sc", W * l0, W * l1), A(b, W * l0, W * l1), N("d1", W * l0, W * l1), ALU.min, ALU.max)
+                ts(N("fi", l0, l1), N("sc", W * l0 + W - 1, W * l1, W), 4095, ALU.bitwise_and)
                 ts(N("f", l0, l1), N("fi", l0, l1), 2048.0, ALU.subtract)
             fe, fo = N("f", 0, P), N("f", P, L)
             w = 16 // len(CFG["eq"][i])
@@ -442,9 +473,9 @@ def build():
                     act(N("x1", w * P * h, w * P * h + w * P), A(bk, 0, w * P), ACT.Abs)
                     act(x, N("x1", w * P * h, w * P * h + w * P), ACT.Relu, bias=1.0, scale=-1.0)
             ye, co = A(a, 0, P), A(b, 1, 4 * P, 4)
+            mm([(ye, A("idb"), A("k2048", 0, P), True, False)], "ye")
             for k0, k1 in steps(0, 16, w):
-                mm([(ye, A("idb"), A("k2048", 0, P), True, False)] * (k0 == 0)
-                   + [(ye, A("ni8"), N("eq", k * P, k * P + P), False, k == 15) for k in range(k0, k1)])
+                mm([(ye, A("ni8"), N("eq", k * P, k * P + P), False, False) for k in range(k0, k1)], "ye")
             for k0, k1 in steps(0, 16, 8):
                 mm([(co, route("gsp", k), N("eq", k * P, k * P + P), k == 0, k == 15) for k in range(k0, k1)])
             act(N("cm", 0, P), ye, ACT.Sign, bias=2048.0, scale=-1.0)
@@ -463,7 +494,7 @@ def build():
                 cp(N("xr", 16 * l0, 16 * l1), Ind(A(X), N("ro", l0, l1)))
             for l0, l1 in steps(0, ps, CFG["rstep"]) + steps(ps, P, CFG["rstep"]):
                 scan(N("qs", 16 * l0, 16 * l1), A("rmask", 0, 16 * (l1 - l0)), N("xr", 16 * l0, 16 * l1), ALU.mult, ALU.max)
-            cp(A(Xn, Qn[1] + P * i, Qn[1] + P * i + P), N("qs", 15, 16 * P, 16))
+            (gcp if CFG["gq"] and not i else cp)(A(Xn, Qn[1] + P * i, Qn[1] + P * i + P), N("qs", 15, 16 * P, 16))
             ops[-1]["mark"] = True
             for l0, l1 in steps(0, L, P if CFG["fsplit"][i] and t < ROUNDS - 1 else L):
                 o, o2, o3 = A(d, l0, l1), A(a, 192 + l0, 192 + l1), A(a, 456 + l0 // 16, 456 + l1 // 16)
@@ -471,8 +502,17 @@ def build():
                 act(N("bs", l0, l1), o, bias=REC - 2048.0 - 8192.0 + H * t + P * i)
                 mm([(o2, A("idb"), N("f", l0, l1), True, False), (o2, A("ni8"), N("cm", l0, l1), False, True)])
                 tt(N("F", l0, l1), N("bs", l0, l1), o2, ALU.max)
-                mm([(o3, route("g0", x), N("F", l0 + x, l1, 16), x == 0, x == 15) for x in range(16)])
-                ts(N("lu", l0 // 16, l1 // 16), o3, 2048.0, ALU.add)
+                if CFG["lv"][i]:
+                    vtr(N("Ft"), N("F"))
+                    mm([(A(a, 456 + qh, 464, 2), A("prm", 128 * (2 * qh + gp), 128 * (2 * qh + gp) + 128), N("Ft", 16 * gp, L, 32), gp == 0, gp == 1)
+                        for qh in range(2) for gp in range(2)])
+                else:
+                    mm([(o3, route("g0", x), N("F", l0 + x, l1, 16), x == 0, x == 15) for x in range(16)])
+                if CFG["glu"] and not i:
+                    act(A("lf", l0 // 16, l1 // 16), o3, bias=2048.0)
+                    gcp(N("lu", l0 // 16, l1 // 16), A("lf", l0 // 16, l1 // 16))
+                else:
+                    ts(N("lu", l0 // 16, l1 // 16), o3, 2048.0, ALU.add)
             mm([(A(d, par, L, 2), A("idb"), N("F", P * par, P * par + P), True, True) for par in range(2)])
             mine = A(Rn[0], Rn[1] + L * i, Rn[1] + L * i + L)
             act(mine, A(d, 0, L), bias=2048.0)
@@ -508,17 +548,18 @@ def build():
 
 def cost(op):
     kind, n = op["work"]
+    f = CFG["f"]
     if kind == "gather":
-        return 0.06 + n * GATHER * CYC, 0.0
+        return 0.06 + n * GATHER * CYC * f, 0.0
     if kind == "plain":
-        return 0.06 + n * CYC, 0.0
+        return 0.06 + n * CYC * f, 0.0
     if kind == "pe":
-        return 0.02 + n * PECYC, 0.0
+        return 0.02 + n * PECYC * f, 0.0
     if kind == "aff":
-        return 0.17 + 2 * n * CYC, 0.0
+        return (0.17 + 2 * n * CYC) * f, 0.0
     if kind == "dma":
         return 0.1 * n, 1.5
-    return (0.3 * n, 0.0) if kind == "send" else (0.0, 1.6)
+    return (CFG["send"] * n, 0.0) if kind == "send" else (0.0, 1.6)
 
 
 def overlap(a, b):
@@ -536,34 +577,45 @@ def dependencies(ops):
     for i, op in enumerate(ops):
         op["i"] = i
         deps = {}
+
+        def mates(j):
+            return op.get("group") and ops[j].get("group") == op["group"] and not ops[j]["opens"]
         acc = [(a, False) for a in op["ins"]] + [(a, True) for a in op["outs"]]
         for a, wr in acc:
             for j, b, bw in hist.setdefault(a[0], []):
-                if (wr or bw) and overlap(a, b):
+                if (wr or bw) and overlap(a, b) and not mates(j):
                     deps[j] = deps.get(j, False) or ops[j]["q"] != "P" or op["q"] != "P"
             if a[0] in PSUM and op["q"] == "P":
-                if last.get(a[0], i) != i:
-                    deps[last[a[0]]] = deps.get(last[a[0]], False)
-                last[a[0]] = i
+                before = last.setdefault(a[0], [])
+                for j in before:
+                    if j != i and not mates(j):
+                        deps[j] = deps.get(j, False)
+                before[:] = [j for j in before if op["group"] and ops[j]["group"] == op["group"]] + [i]
         for a, wr in acc:
             h = hist[a[0]]
             if wr:
-                h[:] = [e for e in h if e[0] == i or not covers(a, e[1])]
+                h[:] = [e for e in h if e[0] == i or mates(e[0]) or not covers(a, e[1])]
             h.append((i, a, wr))
         op["deps"] = deps
         op["banks"] = {a[0] for a, _ in acc if a[0] in PSUM}
 
 
-def improve(ops, pred, seq, rounds, nxt):
+def improve(ops, pred, seq, rounds, nxt, x=1):
     n = len(ops)
     wake, width = CFG["wake"], CFG["width"] * (2 if nxt else 1)
-    q = [op["q"] for op in ops]
+    q = ["RVSPGY".index(op["q"]) for op in ops] + [0]
     cost = [op["cost"] for op in ops]
-    lat = [op["lat"] if not nxt else 0.0 if op.get("mark") else -1e9 for op in ops]
-    banks = [tuple(op["banks"]) for op in ops]
+    banks = [tuple(int(b[1]) for b in op["banks"]) for op in ops]
     back = {k: i for i, k in nxt.items()}
     inside = set(seq) | set(back)
-    pr = [tuple((j, d) for j, d in p.items() if j in inside) for p in pred]
+    goals = [(i, 0.0) for i in back if ops[i].get("mark")] or [(i, op["lat"]) for i, op in enumerate(ops) if op["lat"]]
+    pr, above = [], []
+    for i, p in enumerate(pred):
+        over = 0
+        for j in p:
+            over |= above[j] if j in inside else 0
+        pr.append(tuple((j, d) for j, d in p.items() if j in inside and (d > wake or not over >> j & 1)))
+        above.append(over | sum(1 << j for j in p if j in inside))
     pred = [[j for j, d in p] for p in pr]
     succ = [[] for _ in range(n)]
     for i in inside:
@@ -571,34 +623,29 @@ def improve(ops, pred, seq, rounds, nxt):
             succ[j].append(i)
 
     def run(seq):
-        end, by = [None] * n, [None] * n
-        last, users = {}, {}
-        top, at = 0.0, 0
-        for i in seq + [nxt[k] for k in seq if nxt]:
-            s, w = 0.0, None
-            for j, d in pr[i]:
-                if end[j] is None:
-                    return None
-                x = end[j] + d
-                if x > s:
-                    s, w = x, (j, 0)
+        end, by = [1e9] * n + [-1.0], [None] * n
+        last, user = [n] * 6, [n] * 8
+        for i in seq + [nxt[k] for k in seq] if nxt else seq:
             qi = q[i]
-            if qi != "R":
-                j = last.get(qi)
-                if j is not None and end[j] > s:
-                    s, w = end[j], (j, 1)
+            w = last[qi]
+            s = end[w]
+            if qi:
                 last[qi] = i
             for b in banks[i]:
-                u = users.setdefault(b, {})
-                for q2, j in u.items():
-                    if q2 != qi and end[j] + wake > s:
-                        s, w = end[j] + wake, (j, 1)
-                u[qi] = i
-            end[i] = s = s + cost[i]
+                j = user[b]
+                if q[j] != qi and end[j] + wake > s:
+                    s, w = end[j] + wake, j
+                user[b] = i
+            w = -1 - w
+            for j, d in pr[i]:
+                if end[j] + d >= s:
+                    s, w = end[j] + d, j
+            if s <= 0.0:
+                s, w = 0.0, None
+            end[i] = s + cost[i]
             by[i] = w
-            if s + lat[i] > top:
-                top, at = s + lat[i], i
-        return top, end, by, at
+        top, at = max((end[i] + d, i) for i, d in goals)
+        return (top, end, by, at) if top < 1e9 else None
 
     def moved(seq, pos, j, i, early):
         part = seq[pos[j]:pos[i] + 1]
@@ -613,16 +660,14 @@ def improve(ops, pred, seq, rounds, nxt):
 
     def arcs(now, seq):
         top, end, by, i = now
-        timed = sorted(seq, key=lambda k: end[nxt.get(k, k)] - cost[k])
-        if not nxt or run(timed):
-            seq = timed
+        seq = sorted(seq, key=lambda k: end[nxt.get(k, k)] - cost[k])
         pos = [-1] * n
         for p, k in enumerate(seq):
             pos[k] = p
         pairs, block = [], []
         while by[i] is not None:
-            j, res = by[i]
-            block = block[-3:] + [i] if res else []
+            j = max(by[i], -1 - by[i])
+            block = block[-3:] + [i] if by[i] < 0 else []
             pairs += [(back.get(j, j), back.get(k, k)) for k in block if (j in back) == (k in back) and pos[back.get(j, j)] < pos[back.get(k, k)]]
             i = j
         return seq, pos, pairs
@@ -630,7 +675,6 @@ def improve(ops, pred, seq, rounds, nxt):
     now = run(seq)
     best = (now[0], seq)
     seq, pos, pairs = arcs(now, seq)
-    x = CFG["seed"]
     for it in range(rounds):
         x = (x * 1103515245 + 12345) % 2147483648
         j, i = pairs[(x >> 8) % len(pairs)]
@@ -643,9 +687,9 @@ def improve(ops, pred, seq, rounds, nxt):
             now = r
             seq, pos, pairs = arcs(now, s2)
             if now[0] < best[0]:
-                best = (now[0], seq)
+                best = (now[0], s2)
     top, end, by, i = run(best[1])
-    return top, [None if end[k] is None else end[k] - cost[k] for k in range(n)]
+    return top, [end[k] - cost[k] for k in range(n)]
 
 
 def steady(ops, pred, succ, start):
@@ -664,7 +708,7 @@ def steady(ops, pred, succ, start):
         if start[i] > edge and ops[i]["round"] >= 0:
             first.setdefault(ops[i]["kind"], i)
     nxt = {i: where[k, ops[i]["round"] + 1] for k, i in first.items() if (k, ops[i]["round"] + 1) in where}
-    top, at = improve(ops, pred, list(nxt), CFG["steady"], nxt)
+    top, at = min(improve(ops, pred, list(nxt), CFG["steady"], nxt, CFG["seed"] + k) for k in range(CFG["starts"]))
     span = top - max(at[i] + ops[i]["cost"] for i in nxt if ops[i].get("mark"))
     PLAN["span"] = span
     key = [0.0] * n
@@ -768,6 +812,8 @@ def plan():
         dependencies(ops)
         schedule(ops)
         PLAN["ops"], PLAN["seq"] = ops, sorted(range(len(ops)), key=lambda i: ops[i]["pos"])
+        for i in {ops[i]["group"]: i for i in PLAN["seq"] if ops[i].get("group")}.values():
+            ops[i]["stop"] = True
     return PLAN["ops"], PLAN["seq"]
 
 

import math
from concourse.mybir import AluOpType, ActivationFunctionType

ALU = AluOpType
ACT = ActivationFunctionType
ROUNDS, RANKS, H, A0, NV, REC = 4, 4, 128, 2048, 4096, 3584
L, P = 128, 64
CFG = dict(p1=1, g0=0, w=3, ge2u=(0, 0), gq=1, gprep=((1, 1),), gd1=1, gconv=2, gch=(0, 0), sbar=1, glu=1, lv=(0, 1),
           z=(0, 3), nv1=(64, 128), nv2=(64, 64), step=32, sstep=32, rec_s=(64, 32), rstep=32, eq=("VV", "VVVV"), e_v=(0, 3), delta=1,
           ro1=(1, 0), ddw=(0, 1), lin_g=0, csplit=(0, 0), uu2=1, fsplit=(0, 0), tri=(1, 1), eb=(2, 3),
           first=dict(c1a="VS", c2a="SV", c1b="SV", c2b="SV"),
           lead=2.0, wake=0.25, same=0.1, send=1.2, f=1.2, bw=250e3, rbw=150e3, passes=6, al=0.5, boost={"ek0": 30.0, "w0": 30.0, "Z0": 30.0, "R0": 30.0, "X0": 30.0}, rounds=25000, steady=25000, starts=2, width=0.1, seed=13)
B = 32768.0
AT = [0]
for _t in range(ROUNDS):
    AT.append((AT[-1] + 1 + _t % 3) % RANKS)
SLOT = [AT.index(x) for x in AT]
F32, BF, I32, U16, F16 = "float32", "bfloat16", "int32", "uint16", "float16"
LOGICAL = {}


def declare(dtype, **bufs):
    for n, w in bufs.items():
        LOGICAL[n] = ("sbuf", [128, w], dtype)


declare(BF, pin=256, ones=512, blk=128, gsp=144, gz=144, gz2=144, gzn=144, ghalf=144, gb=144, gbh=144, g0=144, idb=128, nidb=128, ih=128, nih=128,
        ib=128, nib=128, i8=128, ni8=128, prm=512, bc=2048, rmask=1024, k8=256, y0a=3 * L, y0b=3 * L, nrb=128, k2048=128, QL=H, Z4=256)
declare(BF, zero=128)
declare(F32, idf=128, cf=H, lf=8, cj=2, c0=1, c1=1, c2=1, c3=1, seg=128, half=128, cnt=2, whf=1, wlf=1, yv=256, yl=256, R4=256)
declare(I32, rti=2048, exi=256, wti=1, kmi=1, whi=1, wli=1, cnti=1, par=1, ui=H, u=H, uu=H, su=H, hs=H, hh=H)
declare(F16, ch=H)
declare(U16, cq=H)
OWN = {"rti", "exi", "pin", "wti", "kmi", "yv", "yl", "QL", "R4"}
for _t in range(ROUNDS):
    declare(BF, **{"X%d" % _t: NV + 16, "Z%d" % _t: A0 + 256 * _t, "w%d" % _t: 256})
    declare(F32, **{"R%d" % _t: A0 + 256 * _t, "ek%d" % _t: 264, "bar%d" % _t: 1, "bo%d" % _t: 1, "FL%d" % _t: 256})
    OWN |= {n + str(_t) for n in ("X", "Z", "w", "R", "ek", "bar", "bo", "FL")}
for _s in "ab":
    for _d, _names in ((BF, dict(pz=16 * L, prep=16 * L, zg=16 * P, re=16 * P, ad=16 * L, c1=16 * L, c2=16 * L, x1=16 * L, x2=16 * L,
                                 dl=P, r9=L, gq=L, sb=L, eq=16 * P, cm=L, xr=16 * P, qs=16 * P)),
                       (F32, dict(e=L, tr=L, lin=L, d1=4 * L, rt1=P, bs=L, pq=L)),
                       (I32, dict(mk=L, ai=8, nn=L, e2=L, sc=4 * L, fi=L)),
                       (F16, dict(uh=P, pm=L, ah=8, f=L, F=L, Ft=L)),
                       (U16, dict(au=8, eu=L, e2u=L, ro=P, lu=8))):
        declare(_d, **{n + _s: w for n, w in _names.items()})
SCRATCH, PLACE = {}, {}
for _n, (_w, _s, _d) in LOGICAL.items():
    if _n in OWN:
        SCRATCH[_n], PLACE[_n] = (_w, _s, _d), (_n, 0)
    else:
        _k = "pool_" + _d
        _o = SCRATCH.get(_k, (0, [128, 0]))[1][1]
        PLACE[_n] = (_k, _o)
        SCRATCH[_k] = ("sbuf", [128, _o + (_s[1] + 31) // 32 * 32], _d)
for _b in range(8):
    LOGICAL["B%d" % _b] = SCRATCH["B%d" % _b] = ("psum", [128, 512], F32)
    PLACE["B%d" % _b] = ("B%d" % _b, 0)
LOADS = ("p0", "wt", "km", "zp", "rt", "ax", "ex")
SEMAPHORES = (["v", "s", "t", "gp", "out", "sent", "aq", "aya", "ayb", "afa", "afb"] + ["ld_" + n for n in LOADS]
              + ["%s%d" % (k, t) for k in ("tz", "tr", "tx", "tw", "ab", "af") for t in range(ROUNDS)]
              + ["u%d%d" % (t, k) for t in range(ROUNDS) for k in range(t + 2, ROUNDS)])
WIDTH = {n: s[1][1] for n, s in LOGICAL.items()}
PSUM = {n for n, s in LOGICAL.items() if s[0] == "psum"}
TWO = {n for n, s in LOGICAL.items() if s[2] in (BF, F16, U16)}
CYC, PECYC, GATHER = 0.83e-3, 0.42e-3, 1.75


def A(name, lo=0, hi=None, st=1):
    return (name, lo, WIDTH[name] if hi is None else hi, st)


def Ind(win, off):
    return ("@", win, off)


def size(a):
    return 16 * size(a[2]) if a[0] == "@" else (a[2] - a[1] + a[3] - 1) // a[3]


def nbytes(a):
    return 128 * size(a) * (2 if a[0] in TWO else 4)


def ap(T, a):
    if a[0] == "@":
        return ap(T, a[1]).indirect(ap(T, a[2]))
    name, o = PLACE[a[0]]
    if a[3] == 1:
        return T[name][:, o + a[1]:o + a[2]]
    return T[name][:, o + a[1]:o + a[2]:a[3]]


def flat(aps):
    out = []
    for a in aps:
        if isinstance(a, tuple):
            out += [a[1], a[2]] if a[0] == "@" else [a]
    return out


def build():
    ops = []
    tag = [""]

    def add(q, work, outs, ins, fn, **kw):
        op = dict(q=q, work=work, outs=flat(outs), ins=flat(ins), fn=fn, tag=tag[0], **kw)
        ops.append(op)
        return op

    def vwork(aps, mode):
        n = max(size(a) for a in aps)
        if any(a[0] == "@" for a in aps):
            return ("gather", n)
        per = 1.0
        if mode == "tt":
            per = 1.0 if any(a[0] in PSUM for a in aps[1:]) else 2.0
        elif all(a[0] in TWO for a in aps):
            per = 0.5
        return ("plain", max(64, n * per))

    def tt(out, a, b, op):
        add("V", vwork((out, a, b), "tt"), [out], [a, b], lambda c: c["V"].tensor_tensor(ap(c["T"], out), ap(c["T"], a), ap(c["T"], b), op))

    def ts(out, a, s1, op0, s2=None, op1=None):
        def fn(c):
            x1 = ap(c["T"], s1) if isinstance(s1, tuple) else s1
            if op1 is None:
                return c["V"].tensor_scalar(ap(c["T"], out), ap(c["T"], a), x1, None, op0)
            return c["V"].tensor_scalar(ap(c["T"], out), ap(c["T"], a), x1, s2, op0, op1)
        add("V", vwork((out, a), "ts"), [out], [a, s1], fn)

    def cp(out, a):
        add("V", vwork((out, a), "ts"), [out], [a], lambda c: c["V"].tensor_copy(ap(c["T"], out), ap(c["T"], a)))

    def fill(out, val):
        add("V", vwork((out,), "ts"), [out], [], lambda c: c["V"].memset(ap(c["T"], out), val))

    def scan(out, d0, d1, op0, op1):
        add("V", vwork((out, d0, d1), "ts"), [out], [d0, d1],
            lambda c: c["V"].tensor_tensor_scan(ap(c["T"], out), ap(c["T"], d0), ap(c["T"], d1), 0.0, op0, op1))

    def vtr(out, a):
        add("V", vwork((out, a), "ts"), [out], [a], lambda c: c["V"].transpose(ap(c["T"], out), ap(c["T"], a)))

    def act(out, a, func=None, bias=0.0, scale=1.0, accum=None):
        func = ACT.Identity if func is None else func

        def fn(c):
            x = ap(c["T"], accum) if accum is not None else None
            b = ap(c["T"], bias) if isinstance(bias, tuple) else bias
            return c["S"].activation(ap(c["T"], out), ap(c["T"], a), func, bias=b, scale=scale, accum_out=x)
        add("S", ("gather" if a[0] == "@" else "plain", size(out)), [out] + ([accum] if accum is not None else []), [a, bias], fn)

    def mm(items, group=None):
        def fn(c):
            m = None
            for k, (o, l, r, s, e) in enumerate(items):
                m = c["P"].matmul(ap(c["T"], o), ap(c["T"], l), ap(c["T"], r), s, e or (k == len(items) - 1 and "stop" in op))
            return m
        outs, ins = [], []
        for o, l, r, s, e in items:
            for x, d in ((o, outs), (l, ins), (r, ins)):
                if x not in d:
                    d.append(x)
        op = add("P", ("pe", sum(max(64, size(i[2])) * (1 if i[2][0] in TWO else 4) for i in items)), outs, ins, fn,
                 group=group and (group, tag[0]), opens=items[0][3])

    def aff(out, a, pattern, cmp, base, cm):
        add("G", ("aff", size(out)), [out], [a], lambda c: c["g"].affine_select(ap(c["T"], out), ap(c["T"], a), pattern, cmp, 0.0, base, cm), sem="gp")

    def gcp(out, a):
        aff(out, a, [[0, size(out)]], ALU.is_ge, 0, 0)

    def iota(out, pattern, base):
        add("G", ("aff", size(out)), [out], [], lambda c: c["g"].iota(ap(c["T"], out), pattern, base, 0, allow_small_or_imprecise_dtypes=True), sem="gp")

    def load(q, out, name):
        add(q, ("dma", 1), [out], [], lambda c: c[q].dma_start(ap(c["T"], out), c["T"][name][:]), sem="ld_" + name, inc=16, nbytes=nbytes(out), bulk="load")

    def store(name, lo, a):
        add("Y", ("dma", 1), [], [a], lambda c: c["Y"].dma_start(c["T"][name][:, lo:lo + size(a)], ap(c["T"], a)), sem="out", inc=16, nbytes=nbytes(a))

    def send(name, by, pairs, behind=(), bulk="table"):
        def fn(c):
            to = c["T"].cores[(c["rank"] + by) % RANKS]
            topo = c["topo"]
            rid, pid, _ = topo.addr(to)
            for dst, src in pairs:
                c["g"].remote_dma(ap(c["T"], dst), ap(c["T"], src), c["T"].sem[name], c["T"].sem["sent"], pid, rid, topo.mask(c["core"], to))
        k = len(pairs)
        o = add("G", ("send", k), [], [x for _, x in pairs] + list(behind), fn, sem="sent", inc=16 * k, own=True, bulk=bulk and "call")
        add("R", ("land", 0), [x for x, _ in pairs], [], None, sem=name, inc=16 * k, after=o, bulk=bulk, nbytes=sum(nbytes(x) for x, _ in pairs))

    def route(tab, x):
        return A(tab, 15 - x, 143 - x)

    def steps(lo, hi, step):
        return [(x, min(hi, x + step)) for x in range(lo, hi, step)]

    step, sstep, W = CFG["step"], CFG["sstep"], CFG["w"]
    load("Y", A("pin"), "p0"); load("S", A("wti"), "wt"); load("S", A("kmi"), "km")
    load("Y", A("Z0"), "zp"); load("Y", A("rti"), "rt"); load("Y", A("X0", 0, NV), "ax"); load("Y", A("exi"), "ex")
    fill(A("ones"), 1.0)
    aff(A("blk"), A("ones", 0, 128), [[-16, 8], [0, 16]], ALU.is_ge, 0, 1)
    aff(A("blk"), A("blk"), [[16, 8], [0, 16]], ALU.is_ge, 15, -1)
    aff(A("idb"), A("ones", 0, 128), [[-1, 128]], ALU.is_equal, 0, 1)
    fill(A("gsp"), 0.0)
    aff(A("gsp", 15, 143, 16), A("ones", 0, 8), [[-16, 8]], ALU.is_ge, 0, 1)
    aff(A("gsp", 15, 143, 16), A("gsp", 15, 143, 16), [[16, 8]], ALU.is_ge, 15, -1)
    for name, src, scale in (("nidb", "idb", -1.0), ("ih", "idb", 0.5), ("nih", "idb", -0.5), ("gz", "gsp", 4096.0), ("ghalf", "gsp", 0.5),
                             ("gb", "gsp", B), ("gbh", "gsp", B / 2), ("ib", "idb", B), ("nib", "idb", -B), ("i8", "idb", 8192.0), ("ni8", "idb", -8192.0)):
        act(A(name), A(src), scale=scale)
    if 2 in CFG["z"]:
        act(A("gz2"), A("gsp"), scale=8192.0)
        act(A("gzn"), A("gsp"), scale=-4096.0)
    if any(CFG["gch"]):
        act(A("idf"), A("idb"))
        act(A("zero"), A("idb"), scale=0.0)
    fill(A("k2048"), 2048.0)
    act(A("seg"), A("ones", 0, 128), scale=0.0)
    act(A("seg", 0, 128, 16), A("ones", 0, 8), scale=1e9)
    for qh in range(2):
        for gp in range(2):
            k = 128 * (2 * qh + gp)
            aff(A("prm", k, k + 128), A("ones", 0, 128), [[-32, 4], [-1000, 2], [-1, 16]], ALU.is_equal, 1000 * gp - 16 * qh, 1)
    act(A("k8", 0, L), A("ones", 0, L), scale=0.0)
    act(A("k8", L), A("ones", 0, L), scale=8.0)
    act(A("bar0"), A("ones", 0, 1), scale=-3.5)
    act(A("half"), A("ones", 0, 128), scale=0.5)
    for k in range(0, 16, 4):
        aff(A("bc", 128 * k, 128 * k + 512), A("ones"), [[-1, 4], [-16, 8], [0, 16]], ALU.is_equal, -k, 1)
    for k in range(0, 1024, 512):
        act(A("rmask", k, k + 512), A("ones"))
    act(A("rmask", 0, 1024, 16), A("ones", 0, 64), scale=0.0)
    act(A("g0"), A("ones", 0, 144), scale=0.0)
    aff(A("g0", 15, 143, 16), A("ones", 0, 8), [[-16, 8]], ALU.is_equal, 0, 1)
    iota(A("nrb"), [[0, 2], [1, P]], 0)
    ts(A("whi"), A("wti"), 6, ALU.logical_shift_right)
    ts(A("wli"), A("wti"), 63, ALU.bitwise_and)
    ts(A("whf"), A("whi"), -32.0, ALU.mult)
    ts(A("wlf"), A("wli"), -0.5, ALU.mult)
    ts(A("w0", 0, 128), A("blk"), A("whf"), ALU.mult)
    ts(A("w0", 128, 256), A("blk"), A("wlf"), ALU.mult)
    fill(A("ek0", 256, 264), 0.0)
    ts(A("ek0", 256, 257), A("kmi"), 4096.0 - (0 if CFG["uu2"] else 64), ALU.subtract)
    fill(A("X0", NV, NV + 16), 0.0)
    wide = [max(CFG["nv1"][i], CFG["nv2"][i], (L, 0, P, P)[CFG["z"][i]]) for i in range(2)]
    for i, s in enumerate("ab"):
        for l0, l1 in steps(0, wide[i], P):
            if not (CFG["g0"] and (i, l0 // P) in CFG["gprep"]):
                fill(A("pz" + s, 16 * l0, 16 * l1), 0.0)
        act(A("y0" + s), A("ones", 0, W * L), scale=0.0)
        act(A("y0" + s, 0, W * L, W), A("ones", 0, L))
        act(A("y0" + s, 1, W * CFG["nv2"][i], W), A("ones", 0, CFG["nv2"][i]), scale=8.0)
        for par in range(2):
            ts(A("pm" + s, P * par, P * par + P), A("pin", L * i + par, L * i + L, 2), -2.0, ALU.mult, -2048.0, ALU.add)
            gcp(A("ek0", L * i + P * par, L * i + P * par + P), A("exi", L * i + par, L * i + L, 2))
    act(A("ek0", 0, 256), A("ek0", 0, 256), bias=-8192.0)
    for k in range(0, A0, 512):
        (gcp if k < 512 * CFG["gconv"] else cp)(A("R0", k, k + 512), A("rti", k, k + 512))

    def columns(k):
        send("tx%d" % k, -AT[k], [(A("X%d" % k, 0, REC), A("X0", 0, REC)), (A("X%d" % k, REC + H * k), A("X0", REC + H * k))])

    def tables(k):
        send("tw%d" % k, -AT[k], [(A("w%d" % k), A("w0")), (A("ek%d" % k), A("ek0"))])
        send("tz%d" % k, -AT[k], [(A("Z%d" % k, 0, A0), A("Z0"))])
        if k > 1:
            send("tr%d" % k, -AT[k], [(A("R%d" % k, 0, A0), A("R0"))])
    send("tr1", -AT[1], [(A("R1", 0, A0), A("R0"))])
    columns(1)
    tables(1)

    for t in range(ROUNDS):
        n = A0 + 256 * t
        X, Z, R, Xn = "X%d" % t, "Z%d" % t, "R%d" % t, "X%d" % SLOT[t + 1]
        Zn, Rn = (A("%s%d" % (x, t + 1), n, n + 256) if t < ROUNDS - 1 else A(x + "4") for x in "ZR")
        Qn = A(Xn, REC + H * t, REC + H * t + H)
        for i, s in enumerate("ab"):
            tag[0] = "%s%d" % (s, t)
            a, b, c, d = ("B%d" % (4 * i + k) for k in range(4))
            four = (c, d, b)
            nv1, nv2, zv = CFG["nv1"][i], CFG["nv2"][i], CFG["z"][i]

            def N(name, lo=0, hi=None, k=1, s=s):
                return A(name + s, lo, hi, k)
            wh, wl = A("w%d" % t, 0, 128), A("w%d" % t, 128, 256)
            tri = CFG["tri"][i]
            U, KU = A(a, 64, 128), A(a, 128, 192)
            o, pe = A(a, 0, P), N("pm", 0, P)
            mm([(o, wh, pe, True, False), (o, wh, A("k2048", 0, P), False, False),
                (o, wl, A("k2048", 0, P), False, False), (o, wl, pe, False, True)])
            ui, u, uu, su, hs, hh, cq, ch = (A(x, P * i, P * i + P) for x in ("ui", "u", "uu", "su", "hs", "hh", "cq", "ch"))
            cp(ui, o)
            ts(u, ui, 4095, ALU.bitwise_and)
            ts(N("uh") if CFG["p1"] else U, u, 2048.0, ALU.subtract)
            ts(KU, u, A("ek%d" % t, 256, 257), ALU.mult)
            tt(uu, u, u if CFG["uu2"] else U, ALU.mult)
            ts(su, uu, 5, ALU.arith_shift_right)
            tt(hs, su, KU, ALU.add)
            if CFG["p1"]:
                mm([(x, A("idb"), N("uh"), True, True) for x in (U, KU)])
            ts(hh, hs, 4095, ALU.bitwise_and)
            ts(cq, hh, (8 + t) / 16.0, ALU.mult, -15.0 / 32, ALU.add)
            if CFG["gch"][i]:
                gcp(A("cf", P * i, P * i + P), cq)
            else:
                ts(ch, cq, 2048.0, ALU.subtract)
            mm([(A(c, 0, L), A("nih"), N("pm"), True, True)])
            for l0, l1 in steps(0, wide[i], P):
                act(N("pz", 16 * l0, 16 * l1, 16), A(c, l0, l1), bias=-1024.0)
                if (t or CFG["g0"]) and (i, l0 // P) in CFG["gprep"]:
                    for k in range(16):
                        gcp(N("prep", 16 * l0 + k, 16 * l1, 16), N("pz", 16 * l0, 16 * l1, 16))
                else:
                    scan(N("prep", 16 * l0, 16 * l1), A("rmask", 0, 16 * (l1 - l0)), N("pz", 16 * l0, 16 * l1), ALU.mult, ALU.add)
            act(N("pq"), A(c, 0, L), bias=255 + 2047.5 - 1024)
            if t < ROUNDS - 1:
                mm([(A(d, par, L, 2), A("nih"), N("pm", P * par, P * par + P), True, True) for par in range(2)])
                act(A(Zn[0], n + L * i, n + L * i + L), A(d, 0, L), bias=-1024.0)
            (gcp if CFG["gd1"] else act)(N("d1", W - 1, W * L, W), A("ek%d" % t, L * i, L * i + L))
            ops[-1]["ins"].append(cq)
            key = A(a, 192, 320)
            ke, ko = A(a, 192, 256), A(a, 256, 320)
            opening = [(key, A("idb"), A("k2048"), True, False), (ke, A("idb"), ch, False, False), (ko, A("idb"), ch, False, False)]
            if CFG["gch"][i]:
                cf = A("cf", P * i, P * i + P)
                opening = [(key, A("idb"), A("zero"), True, False), (ke, A("idf"), cf, False, False), (ko, A("idf"), cf, False, False)]
            if zv > 1:
                for l0, l1 in steps(0, P, step):
                    tt(N("zg", 16 * l0, 16 * l1), Ind(A(Z), A("cq", P * i + l0, P * i + l1)), N("prep", 16 * l0, 16 * l1), ALU.subtract)
                    if zv == 3:
                        act(N("re", 16 * l0, 16 * l1), N("zg", 16 * l0, 16 * l1), ACT.Abs)
                if zv == 2:
                    ts(N("re"), N("zg"), 0.0, ALU.max)
                if CFG["delta"]:
                    tt(N("dl"), N("pm", P, L), N("pm", 0, P), ALU.subtract)
                for k in range(2):
                    bk, items = (c, d)[k], []
                    for m in range(8 * k, 8 * k + 8):
                        o = A(bk, P * (m % 8), P * (m % 8) + P)
                        items += ([(o, A("ih"), N("dl"), True, False)] if CFG["delta"] else
                                  [(o, A("nih"), N("pm", 0, P), True, False), (o, A("ih"), N("pm", P, L), False, False)])
                        items += [(o, A("idb"), N("zg", m, 16 * P, 16), False, True)]
                    mm(items)
                    act(N("ad", 512 * k, 512 * k + 512), A(bk), ACT.Abs)
                mm(opening[:1], "key")
                mm(opening[1:], "key")
                if zv == 2:
                    mm([(ke, route("gzn", m), N("zg", m, 16 * P, 16), False, False) for m in range(16)], "key")
                mm([(ke, route("gz2" if zv == 2 else "gz", m), N("re", m, 16 * P, 16), False, False) for m in range(16)], "key")
                for k in range(2):
                    mm([(ko, route("gz", m), N("ad", P * m, P * m + P), False, False) for m in range(8 * k, 8 * k + 8)], "key")
            elif zv == 0:
                for l0, l1 in steps(0, P, 32):
                    act(N("zg", 16 * l0, 16 * l1), Ind(A(Z), A("cq", P * i + l0, P * i + l1)))
                for k in range(4):
                    bk, x0 = four[k % (2 + tri)], 512 * (k // 2) + 1024 * (k % 2)
                    if (i, k % 2) in CFG["gprep"]:
                        mm([(A(bk), A("idb"), N("zg", x0 % 1024, x0 % 1024 + 512), True, False)]
                           + [(A(bk, m, 512, 16), A("ih"), N("pm", x0 // 16, x0 // 16 + 32), False, m == 15) for m in range(16)])
                        act(N("ad", x0, x0 + 512), A(bk), ACT.Abs, bias=1024.0)
                        continue
                    mm([(A(bk), A("nidb"), N("prep", x0, x0 + 512), True, False), (A(bk), A("idb"), N("zg", x0 % 1024, x0 % 1024 + 512), False, True)])
                    act(N("ad", x0, x0 + 512), A(bk), ACT.Abs)
                mm(opening[:1], "key")
                mm(opening[1:], "key")
                for par in range(2):
                    mm([((ke, ko)[par], route("gz", m), N("ad", 1024 * par + m, 1024 * par + 1024, 16), False, False) for m in range(16)], "key")
            else:
                for l0, l1 in steps(0, P, sstep):
                    act(N("zg", 16 * l0, 16 * l1), Ind(A(Z), A("cq", P * i + l0, P * i + l1)))
                for k in range(4):
                    bk, items = four[k % (2 + tri)], []
                    for m in range(4 * k, 4 * k + 4):
                        o0 = L * (m % 4)
                        items += [(A(bk, o0, o0 + L), A("ih"), N("pm"), True, False),
                                  (A(bk, o0, o0 + P), A("idb"), N("zg", m, 16 * P, 16), False, False),
                                  (A(bk, o0 + P, o0 + L), A("idb"), N("zg", m, 16 * P, 16), False, True)]
                    mm(items)
                    act(N("ad", 512 * k, 512 * k + 512), A(bk), ACT.Abs, bias=1024.0)
                mm(opening)
                for k in range(4):
                    mm([(key, route("gz", m), N("ad", L * m, L * m + L), False, m == 15) for m in range(4 * k, 4 * k + 4)])
            vtr(N("tr"), key)
            scan(N("mk"), A("seg"), N("tr"), ALU.add, ALU.min)
            ts(N("ai"), N("mk", 15, L, 16), 4095, ALU.bitwise_and)
            ts(N("ah"), N("ai"), 2048.0, ALU.subtract)
            mm([(A(a, 320 + qh, 328, 2), A("prm", 128 * (2 * qh + gp), 128 * (2 * qh + gp) + 128), N("ah", gp, 8, 2), gp == 0, gp == 1)
                for qh in range(2) for gp in range(2)])
            ts(N("au"), A(a, 320, 328), 2048.0, ALU.add)
            e = N("e")
            (cp if CFG["e_v"][i] == 1 else act)(e, Ind(A(R), N("au")))
            (gcp if CFG["e_v"][i] == 3 else cp)(N("eu"), e if CFG["e_v"][i] else Ind(A(R), N("au")))
            act(N("lin"), Ind(A(R), N("au")) if CFG["lin_g"] else e, bias=2464.0 * t - 131072.0, scale=2080.0)
            if CFG["p1"]:
                tt(key, e, A(a, 64, 192), ALU.mult)
            for par in range(2 * (1 - CFG["p1"])):
                tt((ke, ko)[par], N("e", P * par, P * par + P), U, ALU.mult)
            tt(N("nn"), N("lin"), key, ALU.add)
            ts(N("e2"), N("nn"), 5, ALU.arith_shift_right, 4095, ALU.bitwise_and)
            (gcp if CFG["ge2u"][i] else cp)(N("e2u"), N("e2"))
            gcp(N("d1", 0, W * L, W), N("e2"))
            act(N("d1", W - 2, W * L, W), e, bias=-4096.0)

            def votes(off, cmp, raw, nv):
                ns = L - nv
                if ns:
                    for l0, l1 in steps(0, ns, sstep):
                        act(N(raw, 16 * l0, 16 * l1), Ind(A(X, 0, NV), N(off, nv + l0, nv + l1)))
                    for j, (k0, k1) in enumerate(steps(0, 16, 512 // ns)):
                        bk, items = ((d, b) if tri and raw == "x1" else (c, d))[j % 2], []
                        for k in range(k0, k1):
                            o = A(bk, ns * (k - k0), ns * (k - k0 + 1))
                            items += [(o, A("ih"), N("pm", nv, L), True, False), (o, A("idb"), N(raw, k, 16 * ns, 16), False, True)]
                        mm(items)
                        act(N(cmp, 16 * nv + ns * k0, 16 * nv + ns * k1), A(bk, 0, ns * (k1 - k0)), ACT.Sign, bias=1024.5)
                for l0, l1 in steps(0, nv, step):
                    tt(N(cmp, 16 * l0, 16 * l1), Ind(A(X, 0, NV), N(off, l0, l1)), N("prep", 16 * l0, 16 * l1), ALU.is_ge)

            def sums(out, cmp, nv, whole, half):
                ns = L - nv
                for lo, hi in steps(0, nv, P):
                    mm([(out(lo, hi), route(whole, k), N(cmp, 16 * lo + k, 16 * hi, 16), False, False) for k in range(16)], cmp)
                for k0, k1 in steps(0, 16, 512 // ns) if ns else ():
                    mm([(out(nv, L), route(half, k), N(cmp, 16 * nv + ns * k, 16 * nv + ns * k + ns), False, False) for k in range(k0, k1)], cmp)
            votes("eu", "c1", "x1", nv1)
            votes("e2u", "c2", "x2", nv2)
            g1 = A(a, 328, 456)
            mm([(g1, A("idb"), A("k8", L - nv1, 2 * L - nv1), True, False)], "c1")
            sums(lambda lo, hi: A(a, 328 + lo, 328 + hi), "c1", nv1, "gsp", "ghalf")
            act(N("gq"), g1, bias=-8.5)
            if W == 3:
                act(N("r9"), N("gq"), ACT.Relu, scale=64.0)
            act(N("sb"), g1, ACT.Sign, bias=A("bar%d" % t), accum=A("cnt", i, i + 1))
            if i and t < ROUNDS - 1:
                o = A(a, 464, 466)
                mm([(o, A("half"), A("cnt"), True, True)])
                if CFG["sbar"]:
                    act(A("cj"), o, scale=-1.0, accum=A("c0"))
                    act(A("c1"), A("c0"), bias=12582912.0, scale=-0.5)
                    act(A("c2"), A("c1"), bias=-12582912.0)
                    act(A("c3"), A("c2"), ACT.Abs, bias=A("c0"), scale=2.0)
                    act(A("bo%d" % t), A("c3"), bias=-3.5, scale=-1.0)
                else:
                    cp(A("cnti"), o)
                    ts(A("par"), A("cnti"), 1, ALU.bitwise_and)
                    ts(A("bo%d" % t), A("par"), -1.0, ALU.mult, -3.5, ALU.add)
                send("ab%d" % t, AT[t] - AT[t + 1], [(A("bar%d" % (t + 1)), A("bo%d" % t))])
                if t + 2 < ROUNDS:
                    columns(t + 2)
            mm([(A(b, 0, W * L), A("nib"), N("y0"), True, False)], "c2")
            mm([(A(b, 2, W * L, W), A("ib"), N("sb"), False, False)], "c2")
            mm([(A(b, 1, W * L, W), A("nib"), N(x), False, False) for x in ("gq", "r9")], "c2")
            sums(lambda lo, hi: A(b, W * lo + 1, W * hi, W), "c2", nv2, "gb", "gbh")
            for l0, l1 in steps(0, L, P if CFG["csplit"][i] else L):
                scan(N("sc", W * l0, W * l1), A(b, W * l0, W * l1), N("d1", W * l0, W * l1), ALU.min, ALU.max)
                ts(N("fi", l0, l1), N("sc", W * l0 + W - 1, W * l1, W), 4095, ALU.bitwise_and)
                ts(N("f", l0, l1), N("fi", l0, l1), 2048.0, ALU.subtract)
            fe, fo = N("f", 0, P), N("f", P, L)
            w = 16 // len(CFG["eq"][i])
            for h, who in enumerate(CFG["eq"][i]):
                bk, items = four[h % CFG["eb"][i]], []
                for k in range(w):
                    o = A(bk, k * P, k * P + P)
                    items += [(o, A("nidb"), fe, True, False), (o, A("bc", 128 * (w * h + k), 128 * (w * h + k) + 128), fo, False, True)]
                mm(items)
                x = N("eq", w * P * h, w * P * h + w * P)
                if who == "V":
                    ts(x, A(bk, 0, w * P), 0.0, ALU.is_equal)
                else:
                    act(N("x1", w * P * h, w * P * h + w * P), A(bk, 0, w * P), ACT.Abs)
                    act(x, N("x1", w * P * h, w * P * h + w * P), ACT.Relu, bias=1.0, scale=-1.0)
            ye, co = A(a, 0, P), A(b, 1, 4 * P, 4)
            mm([(ye, A("idb"), A("k2048", 0, P), True, False)], "ye")
            for k0, k1 in steps(0, 16, w):
                mm([(ye, A("ni8"), N("eq", k * P, k * P + P), False, False) for k in range(k0, k1)], "ye")
            for k0, k1 in steps(0, 16, 8):
                mm([(co, route("gsp", k), N("eq", k * P, k * P + P), k == 0, k == 15) for k in range(k0, k1)])
            act(N("cm", 0, P), ye, ACT.Sign, bias=2048.0, scale=-1.0)
            if CFG["ro1"][i]:
                o = A(c, 0, P)
                mm([(o, A("idb"), fe, True, False), (o, A("ni8"), N("cm", 0, P), False, True)])
                ts(N("ro"), o, 2048.0 + 8192.0, ALU.add, 4096.0, ALU.min)
            else:
                tt(N("rt1"), fe, ye, ALU.max)
                ts(N("ro"), N("rt1"), 2048.0, ALU.add)
            act(N("cm", P, L), co, ACT.Sign)
            ps = CFG["rec_s"][i]
            for l0, l1 in steps(0, ps, CFG["rstep"]):
                act(N("xr", 16 * l0, 16 * l1), Ind(A(X), N("ro", l0, l1)))
            for l0, l1 in steps(ps, P, CFG["rstep"]):
                cp(N("xr", 16 * l0, 16 * l1), Ind(A(X), N("ro", l0, l1)))
            for l0, l1 in steps(0, ps, CFG["rstep"]) + steps(ps, P, CFG["rstep"]):
                scan(N("qs", 16 * l0, 16 * l1), A("rmask", 0, 16 * (l1 - l0)), N("xr", 16 * l0, 16 * l1), ALU.mult, ALU.max)
            (gcp if CFG["gq"] and not i else cp)(A(Xn, Qn[1] + P * i, Qn[1] + P * i + P), N("qs", 15, 16 * P, 16))
            ops[-1]["mark"] = True
            for l0, l1 in steps(0, L, P if CFG["fsplit"][i] and t < ROUNDS - 1 else L):
                o, o2, o3 = A(d, l0, l1), A(a, 192 + l0, 192 + l1), A(a, 456 + l0 // 16, 456 + l1 // 16)
                mm([(o, A("idb"), A("nrb", l0, l1), True, False), (o, A("i8"), N("cm", l0, l1), False, True)])
                act(N("bs", l0, l1), o, bias=REC - 2048.0 - 8192.0 + H * t + P * i)
                mm([(o2, A("idb"), N("f", l0, l1), True, False), (o2, A("ni8"), N("cm", l0, l1), False, True)])
                tt(N("F", l0, l1), N("bs", l0, l1), o2, ALU.max)
                if CFG["lv"][i]:
                    vtr(N("Ft"), N("F"))
                    mm([(A(a, 456 + qh, 464, 2), A("prm", 128 * (2 * qh + gp), 128 * (2 * qh + gp) + 128), N("Ft", 16 * gp, L, 32), gp == 0, gp == 1)
                        for qh in range(2) for gp in range(2)])
                else:
                    mm([(o3, route("g0", x), N("F", l0 + x, l1, 16), x == 0, x == 15) for x in range(16)])
                if CFG["glu"] and not i:
                    act(A("lf", l0 // 16, l1 // 16), o3, bias=2048.0)
                    gcp(N("lu", l0 // 16, l1 // 16), A("lf", l0 // 16, l1 // 16))
                else:
                    ts(N("lu", l0 // 16, l1 // 16), o3, 2048.0, ALU.add)
            mm([(A(d, par, L, 2), A("idb"), N("F", P * par, P * par + P), True, True) for par in range(2)])
            mine = A(Rn[0], Rn[1] + L * i, Rn[1] + L * i + L)
            act(mine, A(d, 0, L), bias=2048.0)
            if t == ROUNDS - 1:
                send("af" + s, AT[t + 1], [(A("FL%d" % t, L * i, L * i + L), mine)])
                store("yr", 256 * t + L * i, A("FL%d" % t, L * i, L * i + L))
        tag[0] = "u%d" % t
        for k in range(t + 2, ROUNDS):
            send("u%d%d" % (t, k), AT[t + 1] - AT[k], [(A("%s%d" % (x[0][0], k), x[1], x[2]), x) for x in (Zn, Rn, Qn)])
        if t + 2 < ROUNDS:
            tables(t + 2)
        if SLOT[ROUNDS] == t:
            send("aq", AT[t + 1] - AT[ROUNDS], [(A("QL"), Qn)])
        if t == ROUNDS - 1:
            k = REC + H * SLOT[ROUNDS]
            gcp(A(Xn, k, k + H), A("QL"))
            ops[-1]["ins"].append(A("fa"))
        if t < ROUNDS - 1:
            send("af%d" % t, AT[t + 1], [(A("FL%d" % t), Rn)])
            store("yr", 256 * t, A("FL%d" % t))
        for l0, l1, i in sorted((l0, l1, i) for i in range(2) for l0, l1 in steps(0, L, L if CFG["ddw"][i] or t == ROUNDS - 1 else P)):
            s = "ab"[i]
            tag[0] = "%s%d" % (s, t)
            tt(A("pm" + s, l0, l1), Ind(A(Xn, 0, NV), A("lu" + s, l0 // 16, l1 // 16)), A("pq" + s, l0, l1), ALU.subtract)
    for i, s in enumerate("ab"):
        tag[0] = s + "4"
        for par in range(2):
            ts(A("yv", L * i + par, L * i + L, 2), A("pm" + s, P * par, P * par + P), -0.5, ALU.mult, -1024.0, ALU.add)
    send("aya", AT[ROUNDS], [(A("yl"), A("yv"))])
    store("yp", 0, A("yl"))
    return ops


def cost(op):
    kind, n = op["work"]
    f = CFG["f"]
    if kind == "gather":
        return 0.06 + n * GATHER * CYC * f, 0.0
    if kind == "plain":
        return 0.06 + n * CYC * f, 0.0
    if kind == "pe":
        return 0.02 + n * PECYC * f, 0.0
    if kind == "aff":
        return (0.17 + 2 * n * CYC) * f, 0.0
    if kind == "dma":
        return 0.1 * n, 1.5
    return (CFG["send"] * n, 0.0) if kind == "send" else (0.0, 1.6)


def overlap(a, b):
    if a[1] >= b[2] or b[1] >= a[2]:
        return False
    return (a[1] - b[1]) % math.gcd(a[3], b[3]) == 0


def covers(a, b):
    return a[1] <= b[1] and b[2] <= a[2] and b[3] % a[3] == 0 and (b[1] - a[1]) % a[3] == 0


def dependencies(ops):
    hist, last = {}, {}
    for i, op in enumerate(ops):
        op["i"] = i
        deps = {}

        def mates(j):
            return op.get("group") and ops[j].get("group") == op["group"] and not ops[j]["opens"]
        acc = [(a, False) for a in op["ins"]] + [(a, True) for a in op["outs"]]
        for a, wr in acc:
            for j, b, bw in hist.setdefault(a[0], []):
                if (wr or bw) and overlap(a, b) and not mates(j):
                    deps[j] = deps.get(j, False) or ops[j]["q"] != "P" or op["q"] != "P"
            if a[0] in PSUM and op["q"] == "P":
                before = last.setdefault(a[0], [])
                for j in before:
                    if j != i and not mates(j):
                        deps[j] = deps.get(j, False)
                before[:] = [j for j in before if op["group"] and ops[j]["group"] == op["group"]] + [i]
        for a, wr in acc:
            h = hist[a[0]]
            if wr:
                h[:] = [e for e in h if e[0] == i or mates(e[0]) or not covers(a, e[1])]
            h.append((i, a, wr))
        op["deps"] = deps
        op["banks"] = {a[0] for a, _ in acc if a[0] in PSUM}


def improve(ops, pred, seq, rounds, nxt, x=1):
    n = len(ops)
    wake, width = CFG["wake"], CFG["width"] * (2 if nxt else 1)
    q = ["RVSPGY".index(op["q"]) for op in ops] + [0]
    cost = [op["cost"] for op in ops]
    banks = [tuple(int(b[1]) for b in op["banks"]) for op in ops]
    back = {k: i for i, k in nxt.items()}
    inside = set(seq) | set(back)
    goals = [(i, 0.0) for i in back if ops[i].get("mark")] or [(i, op["lat"]) for i, op in enumerate(ops) if op["lat"]]
    pr, above = [], []
    for i, p in enumerate(pred):
        over = 0
        for j in p:
            over |= above[j] if j in inside else 0
        pr.append(tuple((j, d) for j, d in p.items() if j in inside and (d > wake or not over >> j & 1)))
        above.append(over | sum(1 << j for j in p if j in inside))
    pred = [[j for j, d in p] for p in pr]
    succ = [[] for _ in range(n)]
    for i in inside:
        for j in pred[i]:
            succ[j].append(i)

    def run(seq):
        end, by = [1e9] * n + [-1.0], [None] * n
        last, user = [n] * 6, [n] * 8
        for i in seq + [nxt[k] for k in seq] if nxt else seq:
            qi = q[i]
            w = last[qi]
            s = end[w]
            if qi:
                last[qi] = i
            for b in banks[i]:
                j = user[b]
                if q[j] != qi and end[j] + wake > s:
                    s, w = end[j] + wake, j
                user[b] = i
            w = -1 - w
            for j, d in pr[i]:
                if end[j] + d >= s:
                    s, w = end[j] + d, j
            if s <= 0.0:
                s, w = 0.0, None
            end[i] = s + cost[i]
            by[i] = w
        top, at = max((end[i] + d, i) for i, d in goals)
        return (top, end, by, at) if top < 1e9 else None

    def moved(seq, pos, j, i, early):
        part = seq[pos[j]:pos[i] + 1]
        take = {i if early else j}
        for k in (reversed(part) if early else part):
            if k in take:
                take.update(x for x in (pred[k] if early else succ[k]) if pos[j] <= pos[x] <= pos[i])
        if (j if early else i) in take:
            return None
        a, b = [k for k in part if k in take], [k for k in part if k not in take]
        return seq[:pos[j]] + (a + b if early else b + a) + seq[pos[i] + 1:]

    def arcs(now, seq):
        top, end, by, i = now
        seq = sorted(seq, key=lambda k: end[nxt.get(k, k)] - cost[k])
        pos = [-1] * n
        for p, k in enumerate(seq):
            pos[k] = p
        pairs, block = [], []
        while by[i] is not None:
            j = max(by[i], -1 - by[i])
            block = block[-3:] + [i] if by[i] < 0 else []
            pairs += [(back.get(j, j), back.get(k, k)) for k in block if (j in back) == (k in back) and pos[back.get(j, j)] < pos[back.get(k, k)]]
            i = j
        return seq, pos, pairs

    now = run(seq)
    best = (now[0], seq)
    seq, pos, pairs = arcs(now, seq)
    for it in range(rounds):
        x = (x * 1103515245 + 12345) % 2147483648
        j, i = pairs[(x >> 8) % len(pairs)]
        s2 = moved(seq, pos, j, i, (x >> 7) & 1)
        r = s2 and run(s2)
        if not r:
            continue
        x = (x * 1103515245 + 12345) % 2147483648
        if r[0] <= now[0] - width * (1 - it / rounds) * math.log((x + 1) / 2147483649.0):
            now = r
            seq, pos, pairs = arcs(now, s2)
            if now[0] < best[0]:
                best = (now[0], s2)
    top, end, by, i = run(best[1])
    return top, [end[k] - cost[k] for k in range(n)]


def steady(ops, pred, succ, start):
    n, seen, where = len(ops), {}, {}
    for i, op in enumerate(ops):
        a = (op["outs"] or op["ins"])[0]
        t = int(op["tag"][-1]) if op["tag"] else -1
        name = a[0] if a[0] in PSUM else a[0].rstrip("0123456789")
        kind = (op["tag"][:1], op["q"], name, a[1] - {"X": H, "Z": 256, "R": 256}.get(name, 0) * t, len(op["outs"]))
        seen[kind, t] = seen.get((kind, t), 0) + 1
        op["kind"], op["round"] = kind + (seen[kind, t],), t
        where[op["kind"], t] = i
    edge = max(start[i] for i, op in enumerate(ops) if op.get("mark") and op["round"] == 0)
    first = {}
    for i in sorted(range(n), key=lambda i: (start[i], i)):
        if start[i] > edge and ops[i]["round"] >= 0:
            first.setdefault(ops[i]["kind"], i)
    nxt = {i: where[k, ops[i]["round"] + 1] for k, i in first.items() if (k, ops[i]["round"] + 1) in where}
    top, at = min(improve(ops, pred, list(nxt), CFG["steady"], nxt, CFG["seed"] + k) for k in range(CFG["starts"]))
    span = top - max(at[i] + ops[i]["cost"] for i in nxt if ops[i].get("mark"))
    PLAN["span"] = span
    key = [0.0] * n
    for i in range(n - 1, -1, -1):
        j = first.get(ops[i]["kind"])
        if j in nxt:
            key[i] = at[nxt[j]] + span * (ops[i]["round"] - ops[j]["round"])
        else:
            key[i] = min([key[k] - w for k, w in succ[i].items()] + [span * (ROUNDS + 1)]) - ops[i]["cost"]
        key[i] -= CFG["boost"].get((ops[i]["outs"] or ops[i]["ins"])[0][0], 0.0) * (ops[i]["round"] < 0)
    return key


def schedule(ops):
    wake, same, al = CFG["wake"], CFG["same"], CFG["al"]
    n = len(ops)
    pred, succ = [{} for _ in range(n)], [{} for _ in range(n)]
    wire, lastload = 0.0, {}
    for i, op in enumerate(ops):
        op["cost"], op["lat"] = cost(op)
        if op.get("bulk"):
            if op["bulk"] == "load":
                wire += op["nbytes"] / CFG["bw"]
                op["lat"] += wire
            j = lastload.get(op["q"])
            if j is not None:
                pred[i][j] = ops[j]["nbytes"] / CFG["rbw"] if op["q"] == "R" else 0.0
            if op["q"] == "R":
                op["lat"] += op["nbytes"] / CFG["rbw"]
            lastload[op["q"]] = i
        for j in op["deps"]:
            pred[i][j] = ops[j]["lat"] + (wake if ops[j]["q"] != op["q"] else same if op["q"] != "P" else 0.0)
        if "after" in op:
            pred[i][op["after"]["i"]] = 0.0
        for j, w in pred[i].items():
            succ[j][i] = w

    def place(before, after, key, back):
        start, taken = [0.0] * n, {}
        left = [len(before[i]) for i in range(n)]
        ready = [i for i in range(n) if not left[i]]
        while ready:
            i = min(ready, key=lambda k: (key[k], k))
            ready.remove(i)
            op = ops[i]
            s = max([start[j] + ops[j]["cost"] + w for j, w in before[i].items()] + [op["lat"] if back else 0.0])
            busy = [(x, y) for x, y in taken.get(op["q"], []) if y > s]
            for b in op["banks"]:
                busy += [(x - wake, y + wake) for x, y, q in taken.get(b, []) if q != op["q"] and y + wake > s]
            for x, y in sorted(busy):
                if x >= s + op["cost"]:
                    break
                s = max(s, y)
            start[i] = s
            if op["q"] != "R":
                taken.setdefault(op["q"], []).append((s, s + op["cost"]))
            for b in op["banks"]:
                taken.setdefault(b, []).append((s, s + op["cost"], op["q"]))
            for k in after[i]:
                left[k] -= 1
                if not left[k]:
                    ready.append(k)
        return start

    key = [0.0] * n
    for i in range(n - 1, -1, -1):
        key[i] = min([key[k] - w for k, w in succ[i].items()] + [-ops[i]["lat"]]) - ops[i]["cost"]
    PLAN["way"] = -min(key)
    bias = [(1 - al) * op["cost"] - CFG["boost"].get((op["outs"] or op["ins"])[0][0], 0.0) for op in ops]
    key = [key[i] + bias[i] - (CFG["lead"] if ops[i]["tag"][:1] == "a" else 0.0) for i in range(n)]
    best = None
    for _ in range(CFG["passes"]):
        start = place(pred, succ, key, False)
        end = max(start[i] + ops[i]["cost"] + ops[i]["lat"] for i in range(n))
        if best is None or end < best[0]:
            best = (end, start)
        back = place(succ, pred, [-start[i] - al * ops[i]["cost"] for i in range(n)], True)
        key = [-back[i] - ops[i]["cost"] + bias[i] for i in range(n)]
    start = best[1]
    if CFG["steady"]:
        start = place(pred, succ, steady(ops, pred, succ, start), False)
    best = improve(ops, pred, sorted(range(n), key=lambda i: (start[i], i)), CFG["rounds"], {})
    last = {}
    for i in sorted(range(n), key=lambda i: (best[1][i], i)):
        ops[i]["pos"] = (best[1][i], i)
        for b in ops[i]["banks"]:
            users = last.setdefault(b, {})
            for q2, j in users.items():
                if q2 != ops[i]["q"]:
                    ops[i]["deps"][j] = True
            users[ops[i]["q"]] = i
    PLAN["end"] = best[0]


PLAN = {}


def plan():
    if "ops" not in PLAN:
        ops = build()
        dependencies(ops)
        schedule(ops)
        PLAN["ops"], PLAN["seq"] = ops, sorted(range(len(ops)), key=lambda i: ops[i]["pos"])
        for i in {ops[i]["group"]: i for i in PLAN["seq"] if ops[i].get("group")}.values():
            ops[i]["stop"] = True
    return PLAN["ops"], PLAN["seq"]


def rank_program(g, core, T, topo):
    rank = T.rank_of(core)
    if rank is None:
        return
    ops, seq = plan()
    ctx = dict(g=g, V=g.vector, S=g.scalar, P=g.tensor, Y=g.sync, T=T, topo=topo, core=core, rank=rank)
    queue = {"V": g.vector, "S": g.scalar, "P": g.tensor, "G": g, "Y": g.sync}
    default = {"V": "v", "S": "s", "P": "t"}
    total, val, known, clock = {}, {}, {q: {} for q in queue}, {}
    for i in seq:
        op = ops[i]
        q = op["q"]
        name = op.get("sem") or default[q]
        inc = op.get("inc", 1)
        if q == "R":
            total[name] = total.get(name, 0) + inc
            val[i], clock[i] = (name, total[name]), {name: total[name]}
            continue
        kn = known[q]
        hard = [j for j, h in op["deps"].items() if h]
        need = {}
        for j in hard:
            s, v = val[j]
            if kn.get(s, 0) < v:
                need[s] = max(need.get(s, 0), v)
        for j in sorted(hard, key=lambda j: -ops[j]["pos"][0]):
            s0, v0 = val[j]
            if need.get(s0) == v0:
                for s, v in clock[j].items():
                    if s != s0 and need.get(s, v + 1) <= v:
                        del need[s]
        for s in sorted(need):
            queue[q].wait_ge(T.sem[s], need[s])
        for j in hard:
            for s, v in clock[j].items():
                kn[s] = max(kn.get(s, 0), v)
        ins = op["fn"](ctx)
        total[name] = total.get(name, 0) + inc
        val[i] = (name, total[name])
        clock[i] = dict(kn)
        clock[i][name] = total[name]
        if not op.get("own"):
            ins.then_inc(T.sem[name], inc)
    for s in sorted(total):
        if known["G"].get(s, 0) < total[s]:
            g.wait_ge(T.sem[s], total[s])
